import numpy as np, ml_dtypes
CORES = [36,164,52,180,100,228,116,244]
N = 8
BF = ml_dtypes.bfloat16
def gentries(a):
    return np.ascontiguousarray(a.reshape(8, 16, -1).transpose(0, 2, 1)).reshape(8, -1)
def gtable(e):
    e = np.asarray(e); return np.ascontiguousarray(e.reshape(8, -1, 16).transpose(0, 2, 1)).reshape(128, -1).astype(np.int32)
W, I, J, A, B, P, RO = 2048, 1024, 768, 4, 16, 128, 4
def column(i, j):
    return ((((2 * i + 1) * (2 * j + 1)) >> 5) + 37 * i + j) & (W - 1)
def sized(rng, n, lo, hi, noise):
    b = np.exp2(lo + (hi - lo) * rng.random((N, 8, 1, n), dtype=np.float32))
    return (b * np.exp2(noise * (2 * rng.random((N, 8, 16, n), dtype=np.float32) - 1))).astype(np.int64)
def parts(rng):
    v = np.minimum(np.maximum(sized(rng, W, 2.6, 6.8, 0.5), 1), 127)
    rl = rng.integers(0, J, (N, 8, 16, I)); cl = rng.integers(0, I, (N, 8, 16, J))
    i = rng.integers(0, I, (N, 8, P)); j = rng.integers(0, J, (N, 8, P))
    return v, rl, cl, i, j, np.minimum(sized(rng, P, 1.0, 6.0, 0.5), 127)
def pack(v, rl, cl, i, j, z):
    return {"fig": np.ascontiguousarray(v.reshape(N, 128, W)).astype(np.float32).astype(BF), "rmate": np.ascontiguousarray(rl.reshape(N, 128, I)).astype(np.int32), "cmate": np.ascontiguousarray(cl.reshape(N, 128, J)).astype(np.int32),
            "prow": np.stack([gtable(a) for a in i]), "pcol": np.stack([gtable(a) for a in j]), "need": np.ascontiguousarray(z.reshape(N, 128, P)).astype(np.float32).astype(BF)}
def some(rng, good, free):
    n = np.flatnonzero(good & free)
    if len(n) == 0: n = np.flatnonzero(free)
    return n[rng.integers(0, len(n), 128)]
def fill(rng, v, rl, cl, i, j, z, g):
    v[:, g] = 40 + np.argsort(rng.random((N, 16, W)), axis=1); z[:, g] = 0
    seen = np.zeros((N, W), bool); rows = np.zeros((N, I), bool); cols = np.zeros((N, J), bool); ai = np.arange(I); aj = np.arange(J)
    for q in range(N):
        i[q, g] = rng.permutation(I)[:P]; j[q, g] = rng.permutation(J)[:P]; rows[q, i[q, g]] = True; cols[q, j[q, g]] = True
    x = np.array(i[:, g]); y = np.array(j[:, g])
    for t in range(RO):
        if t == RO - 1: rows[:] = False; cols[:] = False
        nx = np.zeros_like(x); ny = np.zeros_like(y)
        for q in range(N):
            to = (q + 1 + t % 3) % N
            for k in range(P):
                a, b = int(x[q, k]), int(y[q, k])
                u = some(rng, ~seen[q][column(a, aj)], ~cols[to]); w = some(rng, ~seen[q][column(ai, b)], ~rows[to])
                c = np.stack([column(a, u), column(w, b), column(w, u)])
                n = int(np.argmax(~seen[q][c[2]] & (c[0] != c[1]) & (c[0] != c[2]) & (c[1] != c[2])))
                seen[q, c[:, n]] = True; cols[to, u[n]] = True; rows[to, w[n]] = True
                rl[q, g, :, a] = u[n]; cl[q, g, :, b] = w[n]; nx[to, k] = w[n]; ny[to, k] = u[n]
        x, y = nx, ny
def setup_inputs(rng):
    return pack(*parts(rng))
def setup_inputs_ties(rng):
    v, rl, cl, i, j, z = parts(rng)
    v = rng.choice(np.array([8, 16, 32, 64]), (N, 8, 1, W)) + np.zeros((1, 1, 16, 1), np.int64)
    low = (rng.random((N, 8, 1, W)) < 0.3) & (np.arange(16)[:, None] == rng.integers(0, 16, (N, 8, 1, W)))
    z = rng.choice(np.array([0, 1, 8, 9, 16, 32, 33, 64, 65]), (N, 8, 1, P)) + np.zeros((1, 1, 16, 1), np.int64)
    v = v - low; fill(rng, v, rl, cl, i, j, z, 3)
    return pack(v, rl, cl, i, j, z)
def setup_inputs_none(rng):
    v, rl, cl, i, j, z = parts(rng)
    h = int(rng.integers(0, 8)); z[int(rng.integers(0, N))] = 0; z[:, h] = 127; v[:, h] = np.minimum(v[:, h], 126)
    for g, a, b in (((h + 1) % 8, A - 1, B - 1), ((h + 2) % 8, 0, 0)):
        v[:, g] = np.minimum(v[:, g], 10); z[:, g] = rng.integers(20, 30, (N, 16, P))
        for q in range(N):
            for k in range(8):
                x, y = int(i[q, g, k]), int(j[q, g, k]); u, w = int(rl[q, g, a, x]), int(cl[q, g, b, y])
                for c in (column(x, u), column(w, y), column(w, u)): v[q, g, :, c] = 127
    return pack(v, rl, cl, i, j, z)
def setup_inputs_alike(rng):
    v, rl, cl, i, j, z = parts(rng); z = z // 4
    i[:, [0, 4]] = i[:, [0, 4], :1]; j[:, [0, 4]] = j[:, [0, 4], :1]; z[:, [0, 4]] = z[:, [0, 4], :, :1]
    rl[:, [1, 5]] = rng.choice(np.array([0, 5, J - 1]), (N, 2, 16, I)); cl[:, [1, 5]] = rng.choice(np.array([0, 7, I - 1]), (N, 2, 16, J))
    i[:, 2] = rng.choice(np.array([0, 1, I // 2, I - 1]), (N, P)); j[:, 2] = rng.choice(np.array([0, 1, J // 2, J - 1]), (N, P))
    rl[:, 6] = rl[:, 6, :1]; cl[:, 6] = cl[:, 6, :1]
    for q in range(N):
        rl[q, 7, 0, i[q, 7]] = j[q, 7]; cl[q, 7, 0, j[q, 7]] = i[q, 7]
        cl[q, 4, :, int(j[q, 4, 0])] = int(i[q, 4, 0])
    z[:, 4] = 0
    rl[:, 3] = np.where(rng.random((N, 16, I)) < 0.5, rng.choice(np.array([0, J - 1]), (N, 16, I)), rl[:, 3])
    cl[:, 3] = np.where(rng.random((N, 16, J)) < 0.5, rng.choice(np.array([0, I - 1]), (N, 16, J)), cl[:, 3])
    i[:, 3] = np.where(rng.random((N, P)) < 0.5, rng.choice(np.array([0, I - 1]), (N, P)), i[:, 3])
    j[:, 3] = np.where(rng.random((N, P)) < 0.5, rng.choice(np.array([0, J - 1]), (N, P)), j[:, 3])
    return pack(v, rl, cl, i, j, z)
def setup_inputs_late(rng):
    v, rl, cl, i, j, z = parts(rng); z = z // 4
    for g in range(8):
        s = rng.permutation(16)
        for q in range(N):
            a, b = int(s[q % 2]), int(s[1 - q % 2])
            v[q, g, a] = np.minimum(v[q, g, a], 12); z[q, g, a] = rng.integers(13, 30, P); z[q, g, b] = np.minimum(z[q, g, b], 6)
    return pack(v, rl, cl, i, j, z)
def setup_inputs_spread(rng):
    v, rl, cl, i, j, z = parts(rng)
    v = np.minimum(np.maximum(sized(rng, W, 0.0, 7.3, 0.3), 1), 127)
    z = np.minimum(sized(rng, P, -1.0, 7.2, 0.2), 127)
    v[:, 2] = rng.integers(123, 128, (N, 16, W)); z[:, 2] = np.minimum(z[:, 2], 60)
    v[:, 5] = np.where(rng.random((N, 1, W)) < 0.5, 127, 1); z[:, 5] = 127
    return pack(v, rl, cl, i, j, z)
def check_inputs(d):
    bad = []
    for k, lo, hi in (("fig", 1, 127), ("rmate", 0, J - 1), ("cmate", 0, I - 1), ("prow", 0, I - 1), ("pcol", 0, J - 1), ("need", 0, 127)):
        v = np.asarray(d[k]).astype(np.float64)
        if not (np.all(v >= lo) and np.all(v <= hi) and np.all(v == np.floor(v))): bad.append("range of " + k)
    return bad
def look(h, c, z):
    m = c.shape[1]; v = np.take_along_axis(h, c.reshape(8, 1, m * P), 2).reshape(8, 16, m, P)
    return np.all(np.abs(v) >= z[:, :, None, :], axis=1), np.sum(np.maximum(v, 0), axis=1)
def reference(fig, rmate, cmate, prow, pcol, need):
    h = fig.astype(np.float32).astype(np.int32).reshape(N, 8, 16, W); z = need.astype(np.float32).astype(np.int32).reshape(N, 8, 16, P)
    rm = rmate.astype(np.int64).reshape(N, 8, 16, I); cm = cmate.astype(np.int64).reshape(N, 8, 16, J)
    i = np.stack([gentries(a) for a in prow]).astype(np.int64); j = np.stack([gentries(a) for a in pcol]).astype(np.int64)
    cost = np.zeros((N, 8, RO, P), np.float32); gi = np.arange(8)[:, None] + np.zeros((1, P), np.int64)
    for t in range(RO):
        ra = A * (t % (16 // A)); rb = B * (t % (16 // B)); sh = 1 + t % 3
        ni, nj, nz = [None] * N, [None] * N, [None] * N
        for q in range(N):
            x, y = i[q], j[q]
            jm = np.take_along_axis(rm[q][:, ra:ra + A], x[:, None, :], 2)
            im = np.take_along_axis(cm[q][:, rb:rb + B], y[:, None, :], 2)
            ok1, c1 = look(h[q], column(x[:, None, :], jm), z[q]); ok2, c2 = look(h[q], column(im, y[:, None, :]), z[q])
            ok3, c3 = look(h[q], column(im[:, None, :, :], jm[:, :, None, :]).reshape(8, A * B, P), z[q])
            ok = (ok1[:, :, None, :] & ok2[:, None, :, :]).reshape(8, A * B, P) & ok3
            total = (c1[:, :, None, :] + c2[:, None, :, :]).reshape(8, A * B, P) + c3
            total = np.where(ok, total, 2 ** 20)
            best = np.argmin(total, axis=1); good = np.any(ok, axis=1)
            cost[q, :, t] = np.where(good, np.take_along_axis(total, best[:, None, :], 1)[:, 0], -1)
            u = np.take_along_axis(jm, (best // B)[:, None, :], 1)[:, 0]; w = np.take_along_axis(im, (best % B)[:, None, :], 1)[:, 0]
            far = column(w, u); hit = np.zeros((8, W), bool)
            for c in (column(x, u), column(w, y), far): hit[gi[good], c[good]] = True
            size = np.abs(h[q]); fresh = np.take_along_axis(size, far[:, None, :], 2) >> 1
            h[q] = np.where(hit[:, None, :], -size, h[q])
            to = (q + sh) % N
            ni[to] = np.where(good, w, x); nj[to] = np.where(good, u, y); nz[to] = np.where(good[:, None, :], fresh, z[q])
        i = np.stack(ni); j = np.stack(nj); z = np.stack(nz)
    yp = np.stack([gtable(np.concatenate([i[q], j[q]], axis=1)) for q in range(N)])
    return {"yf": h.reshape(N, 128, W).astype(np.float32).astype(BF), "yp": yp.astype(np.float32), "yz": z.reshape(N, 128, P).astype(np.float32).astype(BF), "yc": cost.reshape(N, 8, RO * P)}

@@ -1,0 +1,499 @@
+from concourse.mybir import AluOpType as A, ActivationFunctionType as F
+
+N, W, ROUNDS = 8, 2048, 4
+SHIFT = 315
+BIG = float(2 ** 19)
+FLAG = float(2 ** 21)
+
+SPEC = {
+    "bfloat16": "WIN 2048 CW 2048 HZ 2688 HT 2048 ZR 2048 FD 10752 CD 10752 OL 3072 OHH 384 KA 128 ZB 2048 YF 2048 IOT 160 MOD16 128 MOD20 160 "
+                "DIV16 128 DIV8 128 DIV4 128 IDb 128 BLK 128 W1F 128 W1A 128 B8 8 W8F 8 W8A 8 ONE 128 BA 512 BB 128 CB 512 CIT 640 CFL 160 "
+                "ZS0 128 ZS1 128 ZS2 128 ZS3 128",
+    "float32": "UC 768 VJ 768 VO 128 U2 128 U1 32 UP 128 SU3 512 R 512 TT 128 MSC 128 MC 32 OH 160 PW 160 SC2 160 PP 16 EE 128 ZF 64 NG 16 LHF 48 SQ 384 "
+               "YP 16 YC 128 CK 128 pF 4 cc 16 IDf 128 WIT 160 MK 16 MS 8 DRM 128 DRS 160 KC 32 KM0 24 KM1 24 KM2 24 KM3 24 KR0 24 KR1 24 KR2 24 KRX 24",
+    "int32": "CM 768 PR 16 XI 672 XJ 672 MI32 16 LI 8 ZI 16 KI 32 XC 24 LHI 48 CKI 64 CI 384 pI 4 RW0 1024 RW1 1024 RW2 1024 RW3 1024 "
+             "MSG0 16 MSG1 16 MSG2 16 MSG3 16 MR0 16 MR1 16 MR2 16 MR3 16",
+    "float16": "G16 128 SEL 512 SV1 512 SU1 512 SV3 256 WJT 160",
+    "uint16": "NL 16 LST 672 OFF 8",
+}
+PSUM = ("A0", "A1", "A2", "A3", "S2", "VB", "MI", "HH")
+SCRATCH = {n: ("psum", [128, 512], "float32") for n in PSUM}
+for _ty, _l in SPEC.items():
+    _l = _l.split()
+    for _n, _c in zip(_l[::2], _l[1::2]):
+        SCRATCH[_n] = ("sbuf", [128, int(_c)], _ty)
+SEMAPHORES = ["qv", "qs", "qt", "qg", "dl", "dc", "dd", "df", "dn", "dr0", "dr1", "dr2", "dr3", "oy0", "oy1", "oy2", "oy3", "oc", "op", "oz"] + \
+    [p + str(t) for p in ("rn", "rz", "rk", "ln", "lz", "lk") for t in range(ROUNDS)]
+CHUNKS = [("f2", 384, 128, 0), ("a0", 0, 128, 2560), ("a1", 128, 128, 4608), ("a2", 256, 128, 6656), ("f1", 512, 32, 2048), ("a3", 544, 64, 8704), ("a3", 608, 64, 9728)]
+
+
+def rank_program(g, core, T, topo):
+    rank = T.rank_of(core)
+    if rank is None:
+        return
+    queues = {"v": g.vector, "s": g.scalar, "t": g.tensor, "g": g, "y": g.sync}
+    acc, cnt, final = {}, {}, {}
+    known = {q: {} for q in "vstgyx"}
+
+    def overlap(a, b):
+        if max(a[1], b[1]) >= min(a[2], b[2]):
+            return False
+        if a[3] == b[3]:
+            return a[3] == 1 or (a[1] - b[1]) % a[3] == 0
+        if a[3] < b[3]:
+            a, b = b, a
+        return any(x in range(b[1], b[2], b[3]) for x in range(a[1], a[2], a[3]))
+
+    def before(q, reads, writes):
+        deps = {}
+        for kind, regs in (("r", reads), ("w", writes)):
+            for r in regs:
+                for k2, r2, q2, ev, clk in acc.get(r[0], ()):
+                    both = kind == "r" and k2 == "r"
+                    if r[0] in PSUM:
+                        if q == q2 and (q == "t" or both or not overlap(r, r2)):
+                            continue
+                    elif both or not overlap(r, r2):
+                        continue
+                    if known[q].get(ev[0], 0) < ev[1] and (ev[0] not in deps or deps[ev[0]][0] < ev[1]):
+                        deps[ev[0]] = (ev[1], clk)
+        for s in sorted(deps):
+            if not any(s2 != s and deps[s2][1].get(s, 0) >= deps[s][0] for s2 in deps):
+                queues[q].wait_ge(T.sem[s], deps[s][0])
+        for s in deps:
+            for s2, v in list(deps[s][1].items()) + [(s, deps[s][0])]:
+                known[q][s2] = max(known[q].get(s2, 0), v)
+
+    def after(q, reads, writes, ev):
+        clk = dict(known[q])
+        clk[ev[0]] = max(clk.get(ev[0], 0), ev[1])
+        for kind, regs in (("r", reads), ("w", writes)):
+            for r in regs:
+                keep = []
+                for e in acc.get(r[0], ()):
+                    inside = r[1] <= e[1][1] and e[1][2] <= r[2] and (r[3] == 1 or (r[3] == e[1][3] and (r[1] - e[1][1]) % r[3] == 0))
+                    if not (inside and (kind == "w" or (e[0] == "r" and e[2] == q))):
+                        keep.append(e)
+                acc[r[0]] = keep + [(kind, r, q, ev, clk)]
+
+    def emit(q, call, reads, writes):
+        before(q, reads, writes)
+        s = "q" + q
+        cnt[s] = cnt.get(s, 0) + 1
+        call().then_inc(T.sem[s], 1)
+        final[s] = cnt[s]
+        after(q, reads, writes, (s, cnt[s]))
+
+    def dmas(q, sem, moves):
+        total = 16 * len(moves)
+        for out, in_ in moves:
+            before(q, in_[1], out[1])
+            queues[q].dma_start(out[0], in_[0]).then_inc(T.sem[sem], 16)
+        for out, in_ in moves:
+            after(q, in_[1], out[1], (sem, total))
+        final[sem] = total
+
+    def S(name, a, b, step=1, p0=0, p1=128):
+        t = T[name]
+        return (t[p0:p1, a:b] if step == 1 else t[p0:p1, a:b:step], [(name, a, b, step)])
+
+    def B(name, i, n=128):
+        return S(name, n * i, n * i + n)
+
+    def X(ap):
+        return (ap, [])
+
+    def G(win, off):
+        return (win[0].indirect(off[0]), win[1] + off[1])
+
+    def sc(x):
+        return x[0] if isinstance(x, tuple) else x
+
+    def rg(*xs):
+        r = []
+        for x in xs:
+            r = r + (x[1] if isinstance(x, tuple) else [])
+        return r
+
+    def cp(out, in_):
+        emit("v", lambda: g.vector.tensor_copy(out[0], in_[0]), in_[1], out[1])
+
+    def tt(out, a, b, op):
+        emit("v", lambda: g.vector.tensor_tensor(out[0], a[0], b[0], op), a[1] + b[1], out[1])
+
+    def ts(out, a, s1, op0, s2=None, op1=None):
+        if op1 is None:
+            emit("v", lambda: g.vector.tensor_scalar(out[0], a[0], sc(s1), None, op0), rg(a, s1), out[1])
+        else:
+            emit("v", lambda: g.vector.tensor_scalar(out[0], a[0], sc(s1), sc(s2), op0, op1), rg(a, s1, s2), out[1])
+
+    def ms(out, c):
+        emit("v", lambda: g.vector.memset(out[0], c), [], out[1])
+
+    def scan(out, a, b, init, op0, op1):
+        emit("v", lambda: g.vector.tensor_tensor_scan(out[0], a[0], b[0], init, op0, op1), rg(a, b), out[1])
+
+    def act(out, in_, func=F.Copy, bias=0.0, scale=1.0):
+        emit("s", lambda: g.scalar.activation(out[0], in_[0], func, bias=sc(bias), scale=sc(scale)), rg(in_, bias, scale), out[1])
+
+    def mm(out, lhsT, rhs, start, stop):
+        emit("t", lambda: g.tensor.matmul(out[0], lhsT[0], rhs[0], start, stop), lhsT[1] + rhs[1], out[1])
+
+    def iota(out, pattern, base=0, cm=0):
+        if SCRATCH[out[1][0][0]][2] == "int32":
+            emit("g", lambda: g.iota(out[0], pattern, base, cm), [], out[1])
+        else:
+            emit("g", lambda: g.iota(out[0], pattern, base, cm, allow_small_or_imprecise_dtypes=True), [], out[1])
+
+    def send(out, src, dst, rsem, lsem):
+        before("g", src[1], [])
+        rid, pid = topo.addr(dst, core)
+        g.remote_dma(out[0], src[0], T.sem[rsem], T.sem[lsem], pid, rid, topo.mask(core, dst))
+        final[lsem] = len(topo.engines(core, dst))
+
+    def recv(out, src, rsem):
+        final[rsem] = len(topo.engines(src, core))
+        after("x", [], out[1], (rsem, final[rsem]))
+
+    def load_mates(t):
+        n = "RW%d" % t
+        iota(B(n, 0, 1024), [[1, 1024]])
+        dmas("y", "dr%d" % t, [((T[n][16 * q:16 * q + 4, :], [(n, 0, 1024, 1)]), X(T.rmate[16 * q + 4 * t:16 * q + 4 * t + 4, :])) for q in range(8)])
+
+    dmas("y", "dl", [(S("PR", 0, 8), X(T.prow[:])), (S("PR", 8, 16), X(T.pcol[:]))])
+    dmas("y", "dc", [(B("CM", 0, 384), X(T.cmate[:, 0:384]))])
+    dmas("y", "dd", [(B("CM", 1, 384), X(T.cmate[:, 384:768]))])
+    dmas("s", "dn", [(S("HZ", W, W + 128), X(T.need[:]))])
+    iota(S("pI", 0, 1), [[0, 1]], 0, 1)
+    iota(B("IOT", 0, 160), [[1, 160]])
+    iota(B("DIV16", 0), [[1, 8], [0, 16]])
+    iota(B("DIV8", 0), [[1, 16], [0, 8]])
+    load_mates(0)
+    iota(B("DIV4", 0), [[1, 32], [0, 4]])
+    iota(S("VJ", 0, 768), [[2, 768]], 593)
+    iota(B("MOD16", 0), [[0, 8], [1, 16]])
+    iota(B("MOD20", 0, 160), [[0, 8], [1, 20]])
+    iota(S("ZB", 0, W), [[0, W]])
+    for t in range(1, ROUNDS):
+        load_mates(t)
+    PF, PG, PS = S("pF", 0, 1), S("pF", 1, 2), S("pF", 2, 3)
+
+    def cc(i):
+        return S("cc", i, i + 1)
+
+    ms(B("ONE", 0), 1.0)
+    ms(S("CB", 0, 512, 1, 0, 64), 4.0)
+    ms(S("CB", 0, 512, 1, 64, 128), 81.0 / 128)
+    ms(S("cc", 10, 14, 1, 64, 128), -120.0)
+    for t in range(ROUNDS):
+        ms(S("cc", 10 + t, 11 + t, 1, 0, 64), 32768.0 * (t + 1))
+    ts(S("pI", 1, 2), S("pI", 0, 1), 4, A.logical_shift_right)
+    ts(S("pI", 2, 3), S("pI", 0, 1), 15, A.bitwise_and)
+    cp(S("pF", 0, 3), S("pI", 0, 3))
+    ts(B("BLK", 0), B("DIV16", 0), PG, A.is_equal)
+    ts(S("B8", 0, 8), S("IOT", 0, 8), PG, A.is_equal)
+    for a in range(4):
+        ts(cc(a), PS, float(a), A.is_equal)
+    ts(cc(4), PS, 4.0, A.is_ge, 200.0, A.mult)
+    ts(cc(5), PS, 15.0, A.is_lt, 200.0, A.mult)
+    ts(cc(6), PG, 4.0, A.mult, PF, A.add)
+    tt(cc(7), cc(4), PF, A.add)
+    ts(cc(8), PG, 4.0, A.mult, cc(5), A.add)
+    ts(cc(9), cc(4), 2.0, A.mult, cc(6), A.add)
+    for a in range(4):
+        ts(B("SEL", a), B("BLK", 0), cc(a), A.mult)
+    for c in range(4):
+        ts(B("SV1", c), B("IOT", 0), 4.0 * c, A.subtract, cc(7), A.is_equal)
+    ts(B("IDb", 0), B("IOT", 0), PF, A.is_equal)
+    ts(B("WIT", 0, 160), B("IOT", 0, 160), cc(6), A.is_equal, 256.0, A.mult)
+    ts(B("WJT", 0, 160), B("IOT", 0, 160), 16.0, A.subtract, cc(9), A.is_equal)
+    ts(S("MK", 0, 16), S("IOT", 0, 16), PS, A.is_equal)
+    ts(S("MS", 0, 8), S("IOT", 0, 8), PG, A.is_equal)
+    for t in range(ROUNDS):
+        ts(S("ZF", 32 + 8 * t, 40 + 8 * t), S("IOT", 0, 8), 16.0, A.mult, W + 128.0 * t, A.add)
+    for c in range(4):
+        ts(B("SU1", c), B("DIV4", 0), float(c), A.subtract, cc(8), A.is_equal)
+    ts(S("KC", 0, 32), S("ZF", 32, 64), PS, A.add)
+    ts(cc(4), PS, 8.0, A.is_ge)
+    ts(cc(5), PS, 3.0, A.not_equal, 400.0, A.mult)
+    ts(cc(7), cc(4), -8.0, A.mult, PF, A.add)
+    ts(cc(14), PG, 2.0, A.mult, cc(5), A.add)
+    ts(cc(8), cc(4), 400.0, A.mult, cc(7), A.add)
+    ts(cc(15), cc(4), -400.0, A.mult, 400.0, A.add)
+    for c in range(2):
+        ts(B("SV3", c), B("DIV8", 0), float(c), A.subtract, cc(14), A.is_equal)
+    tt(cc(15), cc(15), cc(7), A.add)
+    cp(S("NL", 0, 16), S("PR", 0, 16))
+    for h in range(2):
+        for c in range(2):
+            ts(B("SU3", 2 * h + c), B("IOT", 0), 8.0 * c, A.subtract, cc(8 + 7 * h), A.is_equal)
+    act(S("W8F", 0, 8), S("B8", 0, 8), F.Copy, 0.0, BIG)
+    act(S("W8A", 0, 8), S("B8", 0, 8), F.Copy, 0.0, 64.0)
+    act(B("W1F", 0), B("BLK", 0), F.Copy, 0.0, BIG)
+    act(B("W1A", 0), B("BLK", 0), F.Copy, 0.0, 64.0)
+    for a in range(4):
+        act(B("BA", a), B("BLK", 0), F.Copy, a / 8.0, 0.0)
+    dmas("s", "df", [(S("WIN", SHIFT, W), X(T.fig[:, 0:W - SHIFT])), (S("WIN", 0, SHIFT), X(T.fig[:, W - SHIFT:W]))])
+    act(B("BB", 0), B("MOD16", 0), F.Copy, 0.0, 1.0 / 128)
+
+    def late_constants():
+        ts(S("PP", 0, 8), S("PR", 0, 8), 1024.0, A.mult, 1024.0, A.add)
+        ts(B("CFL", 0, 160), B("MOD20", 0, 160), 16.0, A.is_lt)
+        ts(B("DRM", 0), B("MOD16", 0), 0.0, A.is_equal, float(2 ** 26), A.mult)
+        tt(S("PP", 8, 16), S("PP", 0, 8), S("PR", 8, 16), A.add)
+        ts(B("DRS", 0, 160), B("MOD20", 0, 160), 0.5, A.is_gt)
+        for t in range(ROUNDS):
+            act(B("CIT", t, 160), B("CFL", 0, 160), F.Copy, 0.0, cc(10 + t))
+        for m in range(8):
+            act(B("EE", m, 16), S("MK", 0, 16), F.Copy, 0.0, S("PP", 8 + m, 9 + m))
+        mm(S("HH", 448, 456), B("EE", 0), S("MS", 0, 8), True, True)
+        for h in range(16):
+            mm(B("HH", h, 8), B("WIN", h), S("B8", 0, 8), True, True)
+        act(S("HT", 0, W), S("WIN", 0, W), F.Copy, -0.25, 0.5)
+        act(B("IDf", 0), B("IDb", 0))
+
+    def late_places():
+        cp(S("KRX", 16, 24), S("HH", 448, 456))
+        cp(S("CI", 0, 128), B("HH", 0))
+        ts(S("KI", 0, 8), S("KRX", 16, 24), 1024.0, A.subtract)
+        ts(S("CI", 128, 256), S("CI", 0, 128), 2032, A.bitwise_and)
+        ts(S("KI", 8, 16), S("KI", 0, 8), 10, A.logical_shift_right, 1023, A.bitwise_and)
+        ts(S("KI", 16, 24), S("KI", 0, 8), 1023, A.bitwise_and)
+        ts(S("CI", 256, 384), S("CI", 0, 128), 15, A.bitwise_and)
+        ts(S("KRX", 0, 8), S("KI", 8, 16), 2.0, A.mult, 17.0, A.add)
+        ts(S("KRX", 8, 16), S("KI", 16, 24), 2.0, A.mult, 593.0, A.add)
+        cp(S("ZB", 0, W, 16), S("CI", 128, 256))
+        cp(S("ZB", 1, W, 16), S("CI", 256, 384))
+        ts(S("HZ", 0, W), S("HT", 0, W), 8388608.0, A.add, 8388608.0, A.subtract)
+
+    def vb_bias():
+        mm(S("VB", 0, 512), B("ONE", 0), S("CB", 0, 512), True, False)
+
+    def lists_a(t):
+        if t > 0:
+            cp(S("NL", 0, 16), S("MR%d" % (t - 1), 0, 16))
+        act(B("VO", 0), G(S("VJ", 0, 768), S("NL", 8, 16)), F.Copy, 0.0, 0.5)
+        cp(B("G16", 0), G(B("RW%d" % t, 0, 1024), S("NL", 0, 8)))
+        if t > 0:
+            act(B("U2", 0), G(S("UC", 0, 768), S("NL", 8, 16)))
+        else:
+            ts(B("U2", 0), G(S("CM", 0, 768), S("NL", 8, 16)), 4.0, A.mult, 34.0, A.add)
+        for a in range(3):
+            mm(B("VB", a), B("SEL", a), B("G16", 0), False, False)
+        for c in range(2):
+            mm(S("VB", 384, 448), B("SV3", c), S("G16", c, 128, 2), False, c == 1)
+
+    def lists_b(t):
+        def needs(b0, b1):
+            for b in range(b0, b1):
+                o, i = S("ZR", b, W, 16), S("HZ", W + 128 * t, W + 128 * t + 128)
+                if t == 0 and b % 2 == 0:
+                    act(o, i)
+                else:
+                    cp(o, i)
+
+        tt(B("XI", 3), B("U2", 0), B("VO", 0), A.mult)
+        for a in range(3):
+            tt(B("XI", a), B("U2", 0), B("VB", a), A.mult)
+        needs(0, 8)
+        ts(S("XJ", 0, 512), S("XI", 0, 512), 5, A.logical_shift_right, 2047, A.bitwise_and)
+        needs(8, 16)
+        cp(S("LST", 0, 512), S("XJ", 0, 512))
+        if t == 0:
+            ts(S("UC", 0, 768), S("CM", 0, 768), 4.0, A.mult, 34.0, A.add)
+
+    def lists_c():
+        for c in range(4):
+            mm(S("MI", 0, 32), B("SU1", c), S("G16", c, 128, 4), c == 0, c == 3)
+        mm(S("MI", 32, 64), B("ONE", 0), S("CB", 0, 32), True, False)
+        for c in range(4):
+            mm(S("MI", 32, 64), B("SV1", c), S("G16", c, 128, 4), False, c == 3)
+        for h in range(2):
+            for c in range(2):
+                mm(S("MI", 224 + 64 * h, 288 + 64 * h), B("SU3", 2 * h + c), S("U2", c, 128, 2), c == 0, c == 1)
+
+    def names(t):
+        mm(S("MI", 64, 224), B("ONE", 0), B("CIT", t, 160), True, False)
+        mm(S("MI", 64, 224), B("U2", 0), B("WIT", 0, 160), False, False)
+        mm(S("MI", 64, 224), B("G16", 0), B("WJT", 0, 160), False, True)
+
+    vb_bias()
+    lists_a(0)
+    lists_b(0)
+    lists_c()
+    for t in range(ROUNDS):
+        dst = T.cores[(rank + 1 + t % 3) % N]
+        src = T.cores[(rank - 1 - t % 3) % N]
+        last = t == ROUNDS - 1
+        kr = "KRX" if t == 0 else "KR%d" % (t - 1)
+        win = "WIN" if t == 0 else "CW"
+        zs = W + 128 * t
+
+        mm(B("S2", 0), B("ONE", 0), B("BB", 0), True, False)
+        for a in range(4):
+            mm(B("A%d" % a, 0), B("ONE", 0), B("BA", a), True, False)
+        if t > 0:
+            names(t)
+        for name, off, cols, pos in CHUNKS:
+            o, n = S("LST", off, off + cols), 16 * cols
+            if name == "a0":
+                act(B("UP", 0), S("MI", 224, 352))
+                act(S("U1", 0, 32), S("MI", 0, 32), F.Copy, 34.0, 4.0)
+            act(S("CD", pos, pos + n), G(S(win, 0, W), o))
+            tt(S("FD", pos, pos + n), G(S("WIN", 0, W), o), S("ZR", 0, W, W // n), A.is_lt)
+            if name == "a0":
+                tt(S("XI", 512, 544), S("U1", 0, 32), S("MI", 32, 64), A.mult)
+                for h in range(2):
+                    tt(S("XI", 544 + 64 * h, 608 + 64 * h), B("UP", h, 64), S("VB", 384, 448), A.mult)
+            if name == "a1":
+                ts(S("XJ", 512, 672), S("XI", 512, 672), 5, A.logical_shift_right, 2047, A.bitwise_and)
+            if name == "a2":
+                cp(S("LST", 512, 672), S("XJ", 512, 672))
+            if name == "f1":
+                for a in range(4):
+                    mm(B("A%d" % a, 0), S("CD", pos + a, pos + n, 4), B("W1A", 0), False, False)
+                    mm(B("A%d" % a, 0), S("FD", pos + a, pos + n, 4), B("W1F", 0), False, a < 3)
+                continue
+            bank = "S2" if name == "f2" else "A" + name[1]
+            nb, b0 = n // 128, 8 if off == 608 else 0
+            for b in range(nb):
+                mm(S(bank, b0 + b, 128, 16), S("FD", pos + b, pos + n, nb), S("W8F", 0, 8), False, False)
+            for b in range(nb):
+                mm(S(bank, b0 + b, 128, 16), S("CD", pos + b, pos + n, nb), S("W8A", 0, 8), False, b0 + b == 15 and name in ("f2", "a3"))
+            if t == 0 and name == "a0":
+                late_constants()
+                names(t)
+            if t == 0 and name == "a2":
+                late_places()
+        act(B("R", 0), B("A0", 0))
+        tt(B("R", 1), B("R", 0), B("A1", 0), A.min)
+        tt(B("R", 2), B("R", 1), B("A2", 0), A.min)
+
+        tt(B("R", 3), B("R", 2), B("A3", 0), A.min)
+        tt(B("TT", 0), B("R", 3), B("S2", 0), A.add)
+        scan(B("MSC", 0), B("DRM", 0), B("TT", 0), float(2 ** 26), A.add, A.min)
+        m8 = S("MSC", 15, 128, 16)
+        ts(B("MC", t, 8), m8, BIG - 1, A.min, 1.0, A.add)
+        cp(S("MI32", 0, 8), m8)
+        for q in range(8):
+            o, i, col = S("OH", 20 * q, 20 * q + 16), B("TT", q, 16), S("MC", 8 * t + q, 8 * t + q + 1)
+            if q >= 3:
+                act(o, i, F.Relu, col, -1.0)
+                continue
+            ts(o, i, 1.0, A.add, col, A.is_equal)
+            if q == 0:
+                ts(S("MI32", 8, 16), S("MI32", 0, 8), 4, A.logical_shift_right, 3, A.bitwise_and)
+        for a in range(4):
+            ts(S("OH", 16 + a, 160, 20), S("MI32", 8, 16), float(a), A.is_equal)
+        tt(B("PW", 0, 160), B("OH", 0, 160), S("MI", 64, 224), A.mult)
+        scan(B("SC2", 0, 160), B("DRS", 0, 160), B("PW", 0, 160), 0.0, A.mult, A.add)
+        msg, km, flag = "MSG%d" % t, "KM%d" % t, FLAG * (t + 1)
+        tt(S(km, 16, 24), S("SC2", 19, 160, 20), S(kr, 16, 24), A.max)
+        for q in range(8):
+            o, col = B("EE", q, 16), S(km, 16 + q, 17 + q)
+            if q < 3:
+                ts(o, S("MK", 0, 16), col, A.mult)
+            else:
+                act(o, S("MK", 0, 16), F.Copy, 0.0, col)
+        LQ = S("HH", 448, 456)
+        mm(LQ, B("EE", 0), S("MS", 0, 8), True, True)
+        if not last:
+            vb_bias()
+        ts(S("KI", 0, 8), S(km, 16, 24), 1024.0, A.subtract)
+        ts(S("NG", 0, 8), S(km, 16, 24), flag, A.is_ge)
+        ts(S("KI", 8, 16), S("KI", 0, 8), 10, A.logical_shift_right, 1023, A.bitwise_and)
+        ts(S("KI", 16, 24), S("KI", 0, 8), 1023, A.bitwise_and)
+        ts(S(km, 0, 8), S("KI", 8, 16), 2.0, A.mult, 17.0, A.add)
+        ts(S(km, 8, 16), S("KI", 16, 24), 2.0, A.mult, 593.0, A.add)
+        tt(S("XC", 8, 16), S(km, 0, 8), S(kr, 8, 16), A.mult)
+        tt(S("XC", 0, 8), S(kr, 0, 8), S(km, 8, 16), A.mult)
+        tt(S("XC", 16, 24), S(km, 0, 8), S(km, 8, 16), A.mult)
+        ts(S("LHI", 24, 48), S("XC", 0, 24), 12, A.logical_shift_right, 15, A.bitwise_and)
+        ts(S("LI", 0, 8), LQ, 1024.0, A.subtract)
+        ts(S("LHI", 0, 24), S("XC", 0, 24), 5, A.logical_shift_right, 127, A.bitwise_and)
+        ts(S(msg, 0, 8), S("LI", 0, 8), 10, A.logical_shift_right, 1023, A.bitwise_and)
+        ts(S(msg, 8, 16), S("LI", 0, 8), 1023, A.bitwise_and)
+        send(S("MR%d" % t, 0, 16), S(msg, 0, 16), dst, "rn%d" % t, "ln%d" % t)
+        recv(S("MR%d" % t, 0, 16), src, "rn%d" % t)
+        cp(S("LHF", 0, 48), S("LHI", 0, 48))
+
+        chain = [
+            lambda: ts(S("ZF", 8, 16), LQ, flag, A.is_lt),
+            lambda: ts(S("ZF", 16, 24), S(msg, 0, 8), 2.0, A.mult, 17.0, A.add),
+            lambda: ts(S("ZF", 24, 32), S(msg, 8, 16), 2.0, A.mult, 593.0, A.add),
+            lambda: tt(S("ZF", 32, 40), S("ZF", 8, 16), B("KC", t, 8), A.mult),
+            lambda: tt(S("ZI", 0, 8), S("ZF", 16, 24), S("ZF", 24, 32), A.mult),
+            lambda: ts(S("ZI", 8, 16), S("ZI", 0, 8), 5, A.logical_shift_right, 2047, A.bitwise_and),
+            lambda: tt(S("ZF", 40, 48), S("ZI", 8, 16), S("ZF", 32, 40), A.max),
+            lambda: cp(S("OFF", 0, 8), S("ZF", 40, 48)),
+            lambda: cp(B("ZS%d" % t, 0), G(S("HZ", 0, zs + 128), S("OFF", 0, 8))),
+            lambda: send(S("HZ", zs + 128, zs + 256), B("ZS%d" % t, 0), dst, "rz%d" % t, "lz%d" % t)]
+        step = 0
+        if not last:
+            for step in range(4):
+                chain[step]()
+            step = 4
+        for h in range(2):
+            for q in range(4 * h, 4 * h + 4):
+                for c in range(3):
+                    n, m = 3 * q + c, 8 * c + q
+                    act(B("SQ", n, 16), S("IOT", 0, 16), F.Square, S("LHF", 24 + m, 25 + m), -1.0)
+                    ts(B("OL", n), B("IOT", 0), S("LHF", m, m + 1), A.is_equal, S("NG", q, q + 1), A.mult)
+                    if not last and step < len(chain):
+                        chain[step]()
+                        step += 1
+            act(B("OHH", h, 192), B("SQ", h, 192), F.Relu, 4096.0, -4096.0)
+            for q in range(4 * h, 4 * h + 4):
+                for c in range(3):
+                    n = 3 * q + c
+                    mm(S("HH", q, 128, 8), B("OL", n), B("OHH", n, 16), c == 0, c == 2)
+        recv(S("HZ", zs + 128, zs + 256), src, "rz%d" % t)
+        if not last:
+            send(S("KR%d" % t, 0, 24), S(km, 0, 24), dst, "rk%d" % t, "lk%d" % t)
+            recv(S("KR%d" % t, 0, 24), src, "rk%d" % t)
+            lists_a(t + 1)
+        else:
+            other = [
+                lambda: ts(S("CK", 0, 32), S("MC", 0, 32), 1.0, A.subtract),
+                lambda: ts(S("CK", 32, 64), S("MC", 0, 32), BIG, A.is_lt),
+                lambda: cp(S("CKI", 0, 32), S("CK", 0, 32)),
+                lambda: ts(S("CKI", 32, 64), S("CKI", 0, 32), 6, A.logical_shift_right),
+                lambda: ts(S("CK", 64, 96), S("CKI", 32, 64), 1.0, A.add),
+                lambda: tt(S("CK", 96, 128), S("CK", 64, 96), S("CK", 32, 64), A.mult),
+                lambda: ts(S("CK", 0, 32), S("CK", 96, 128), 1.0, A.subtract)]
+            for i in range(len(chain)):
+                chain[i]()
+                if i >= 2 and i - 2 < len(other):
+                    other[i - 2]()
+        for d in range(1 if last else 2):
+            tt(S("ZB", d, W, 16), S("ZB", d, W, 16), B("HH", 0), A.subtract)
+        if last:
+            ts(B("KA", 0), S("ZB", 0, W, 16), 0.0, A.is_gt)
+            for s in range(16):
+                if s % 3 == 2:
+                    act(S("ZB", s, W, 16), B("KA", 0), F.Copy, -1.0, 2.0)
+                else:
+                    ts(S("ZB", s, W, 16), B("KA", 0), 2.0, A.mult, -1.0, A.add)
+        for h in range(16):
+            mm(B("A%d" % (h // 4), h % 4), B("ZB", h), B("IDb", 0), True, True)
+        if last:
+            mm(S("S2", 0, 128, 1, 0, 32), S("CK", 0, 32), B("IDf", 0), True, True)
+            act(S("YC", 0, 128, 1, 0, 32), S("S2", 0, 128, 1, 0, 32))
+            cp(S("YP", 0, 16), S("MR3", 0, 16))
+            dmas("s", "op", [(X(T.yp[:]), S("YP", 0, 16))])
+            dmas("s", "oz", [(X(T.yz[:]), S("HZ", W + 512, W + 640))])
+            dmas("s", "oc", [(X(T.yc[:, 128 * q:128 * q + 128]), S("YC", 0, 128, 1, 8 * q, 8 * q + 8)) for q in range(ROUNDS)])
+            for h in range(4):
+                tt(B("YF", h, 512), B("WIN", h, 512), S("A%d" % h, 0, 512), A.mult)
+                if h == 0:
+                    dmas("y", "oy0", [(X(T.yf[:, W - SHIFT:W]), S("YF", 0, SHIFT)), (X(T.yf[:, 0:512 - SHIFT]), S("YF", SHIFT, 512))])
+                else:
+                    dmas("y", "oy%d" % h, [(X(T.yf[:, 512 * h - SHIFT:512 * h + 512 - SHIFT]), B("YF", h, 512))])
+        else:
+            for h in range(4):
+                act(B("CW", h, 512), S("A%d" % h, 0, 512), F.Relu)
+            lists_b(t + 1)
+            lists_c()
+
+    for s in sorted(final):
+        g.wait_ge(T.sem[s], final[s])

@@ -2,29 +2,45 @@ from concourse.mybir import AluOpType as A, ActivationFunctionType as F
 
 N, W, ROUNDS = 8, 2048, 4
 SHIFT = 315
-BIG = float(2 ** 19)
-FLAG = float(2 ** 21)
+BIG = float(2 ** 20)
+NONE = float(2 ** 19)
+M2, M16 = 1.5 * 2 ** 24, 1.5 * 2 ** 27
+OWN_ON_SCALAR = True
+MATES_ON_SCALAR = True
+COSTS_LATE = True
+NEEDS, FIRST_NEEDS = "ggggggss", "ssssvvvv"
+FILL = {"start": (512, 1920), "min": (256, 0), "index": (128, 512), "seed": (128, 0), "count": (128, 0), "hot": (0, 0), "product": (128, 0), "sum": (128, 0), "names": (128, 0),
+        "spread": (384, 512), "squares": (0, 128), "sent": (1920, 512), "mates": (384, 512), "copied": (256, 256), "places": (128, 256), "cast": (128, 0), "init": (768, 1024), "costs": (1024, 2304), "parts": (4096, 4096)}
+FIRST = {(0, 0): {"start": (768, 1536), "min": (0, 0), "index": (128, 256), "seed": (0, 0), "count": (0, 0), "product": (0, 0), "sum": (0, 0), "spread": (128, 256),
+                  "sent": (3072, 2176), "mates": (512, 256), "places": (0, 512)},
+         (1, -1): {"mates": (1024, 512)}}
+FREE = ("min", "count", "sent", "mates", "places", "cast", "costs", "parts")
+
+
+def fills(H, t):
+    return {k: v + (k in FREE,) for k, v in dict(FILL, **FIRST.get((H, t), {})).items()}
+
 
 SPEC = {
-    "bfloat16": "WIN 2048 CW 2048 HZ 2688 HT 2048 ZR 2048 FD 10752 CD 10752 OL 3072 OHH 384 KA 128 ZB 2048 YF 2048 IOT 160 MOD16 128 MOD20 160 "
-                "DIV16 128 DIV8 128 DIV4 128 IDb 128 BLK 128 W1F 128 W1A 128 B8 8 W8F 8 W8A 8 ONE 128 BA 512 BB 128 CB 512 CIT 640 CFL 160 "
-                "ZS0 128 ZS1 128 ZS2 128 ZS3 128",
-    "float32": "UC 768 VJ 768 VO 128 U2 128 U1 32 UP 128 SU3 512 R 512 TT 128 MSC 128 MC 32 OH 160 PW 160 SC2 160 PP 16 EE 128 ZF 64 NG 16 LHF 48 SQ 384 "
-               "YP 16 YC 128 CK 128 pF 4 cc 16 IDf 128 WIT 160 MK 16 MS 8 DRM 128 DRS 160 KC 32 KM0 24 KM1 24 KM2 24 KM3 24 KR0 24 KR1 24 KR2 24 KRX 24",
-    "int32": "CM 768 PR 16 XI 672 XJ 672 MI32 16 LI 8 ZI 16 KI 32 XC 24 LHI 48 CKI 64 CI 384 pI 4 RW0 1024 RW1 1024 RW2 1024 RW3 1024 "
-             "MSG0 16 MSG1 16 MSG2 16 MSG3 16 MR0 16 MR1 16 MR2 16 MR3 16",
-    "float16": "G16 128 SEL 512 SV1 512 SU1 512 SV3 256 WJT 160",
-    "uint16": "NL 16 LST 672 OFF 8",
+    "bfloat16": "WIN0 2560 WIN1 2560 CW0 2048 CW1 2048 FIN 2048 YF 2048 ZR 2048 FD 5376 CD 5376 OL 1536 SQ 384 SD 384 SR 384 OHH 384 ZB 256 SG 128 "
+                "SEED 128 KEEP 128 CNT 128 OH 128 ZS 1024 ZI 1280 "
+                "IOT 128 I16 32 U8 8 N32 32 D16 128 ONE 128 IDb 128 E0 128 CA 128 CB 128 CC 128 CD1 128 CE 256 SEL 3584 NMW 128 OWW 140 W32 96 W1 1536 BI 256 LW 144 SGW 1024",
+    "float32": "MSC 256 PW 128 SC 128 CK 32 KF 8 NT 4 OFF 4 LHF 24 EE 128 EE2 64 UUS 80 T1 128 T2 256 T3 256 MK 16 MS 16 pF 8 cc 44 DRM 256 "
+               "IDf 128 ONf 128 YC 256 CF 64 MFo 16 MFi 16 OWNW 1024",
+    "int32": "NW0 1024 NW1 1024 PR 16 XI 336 XJ 336 MI 12 XC 12 LHI 28 CI 64 pI 8",
+    "float16": "GG 256 OWN 256",
+    "uint16": "NL 16 MSG 48 MR 48 OFFL 8 LST 672",
 }
-PSUM = ("A0", "A1", "A2", "A3", "S2", "VB", "MI", "HH")
+PSUM = ("S0", "S1", "NM", "VV", "UB", "LQ", "HH", "YB")
 SCRATCH = {n: ("psum", [128, 512], "float32") for n in PSUM}
 for _ty, _l in SPEC.items():
     _l = _l.split()
     for _n, _c in zip(_l[::2], _l[1::2]):
         SCRATCH[_n] = ("sbuf", [128, int(_c)], _ty)
-SEMAPHORES = ["qv", "qs", "qt", "qg", "dl", "dc", "dd", "df", "dn", "dr0", "dr1", "dr2", "dr3", "oy0", "oy1", "oy2", "oy3", "oc", "op", "oz"] + \
-    [p + str(t) for p in ("rn", "rz", "rk", "ln", "lz", "lk") for t in range(ROUNDS)]
-CHUNKS = [("f2", 384, 128, 0), ("a0", 0, 128, 2560), ("a1", 128, 128, 4608), ("a2", 256, 128, 6656), ("f1", 512, 32, 2048), ("a3", 544, 64, 8704), ("a3", 608, 64, 9728)]
+SEMAPHORES = ["qv", "qs", "qt", "qg", "df", "ls"] + [p + str(h) for p in ("dl", "dn", "dm", "dw", "dc", "oa", "ob", "oc", "op", "oz") for h in range(2)] + \
+    [p + str(h) + str(t) for p in ("rn", "rz", "cw") for h in range(2) for t in range(ROUNDS)]
+F1 = 192
+LISTS = [("a0", 0, 64), ("a1", 64, 64), ("a2", 128, 64), ("f1", F1, 16), ("c4", 208, 64), ("a3", 272, 64)]
 
 
 def rank_program(g, core, T, topo):
@@ -71,7 +87,7 @@ def rank_program(g, core, T, topo):
             for r in regs:
                 keep = []
                 for e in acc.get(r[0], ()):
-                    inside = r[1] <= e[1][1] and e[1][2] <= r[2] and (r[3] == 1 or (r[3] == e[1][3] and (r[1] - e[1][1]) % r[3] == 0))
+                    inside = r[4] and r[1] <= e[1][1] and e[1][2] <= r[2] and (r[3] == 1 or (r[3] == e[1][3] and (r[1] - e[1][1]) % r[3] == 0))
                     if not (inside and (kind == "w" or (e[0] == "r" and e[2] == q))):
                         keep.append(e)
                 acc[r[0]] = keep + [(kind, r, q, ev, clk)]
@@ -88,6 +104,7 @@ def rank_program(g, core, T, topo):
         total = 16 * len(moves)
         for out, in_ in moves:
             before(q, in_[1], out[1])
+        for out, in_ in moves:
             queues[q].dma_start(out[0], in_[0]).then_inc(T.sem[sem], 16)
         for out, in_ in moves:
             after(q, in_[1], out[1], (sem, total))
@@ -95,7 +112,7 @@ def rank_program(g, core, T, topo):
 
     def S(name, a, b, step=1, p0=0, p1=128):
         t = T[name]
-        return (t[p0:p1, a:b] if step == 1 else t[p0:p1, a:b:step], [(name, a, b, step)])
+        return (t[p0:p1, a:b] if step == 1 else t[p0:p1, a:b:step], [(name, a, b, step, p1 - p0 == 128)])
 
     def B(name, i, n=128):
         return S(name, n * i, n * i + n)
@@ -145,355 +162,404 @@ def rank_program(g, core, T, topo):
         else:
             emit("g", lambda: g.iota(out[0], pattern, base, cm, allow_small_or_imprecise_dtypes=True), [], out[1])
 
-    def send(out, src, dst, rsem, lsem):
+    def pick(out, in_, pattern, base=0, cm=0):
+        emit("g", lambda: g.affine_select(out[0], in_[0], pattern, A.is_equal, 0.0, base, cm), in_[1], out[1])
+
+    def send(out, src, dst, frm, rsem):
         before("g", src[1], [])
         rid, pid = topo.addr(dst, core)
-        g.remote_dma(out[0], src[0], T.sem[rsem], T.sem[lsem], pid, rid, topo.mask(core, dst))
-        final[lsem] = len(topo.engines(core, dst))
-
-    def recv(out, src, rsem):
-        final[rsem] = len(topo.engines(src, core))
+        g.remote_dma(out[0], src[0], T.sem[rsem], T.sem["ls"], pid, rid, topo.mask(core, dst))
+        final["ls"] = final.get("ls", 0) + len(topo.engines(core, dst))
+        final[rsem] = len(topo.engines(frm, core))
         after("x", [], out[1], (rsem, final[rsem]))
 
-    def load_mates(t):
-        n = "RW%d" % t
-        iota(B(n, 0, 1024), [[1, 1024]])
-        dmas("y", "dr%d" % t, [((T[n][16 * q:16 * q + 4, :], [(n, 0, 1024, 1)]), X(T.rmate[16 * q + 4 * t:16 * q + 4 * t + 4, :])) for q in range(8)])
+    def rows(t, H):
+        return t[64 * H:64 * H + 64, :]
 
-    dmas("y", "dl", [(S("PR", 0, 8), X(T.prow[:])), (S("PR", 8, 16), X(T.pcol[:]))])
-    dmas("y", "dc", [(B("CM", 0, 384), X(T.cmate[:, 0:384]))])
-    dmas("y", "dd", [(B("CM", 1, 384), X(T.cmate[:, 384:768]))])
-    dmas("s", "dn", [(S("HZ", W, W + 128), X(T.need[:]))])
+    def part(name, h, a, b):
+        return S(name, a, b, 1, 64 * h, 64 * h + 64)
+
+    def load_mates(q, H):
+        dmas(q, "dm%d" % H, [(part("NW%d" % H, 0, 0, 768), X(rows(T.cmate, H))), (part("NW%d" % H, 1, 0, 1024), X(rows(T.rmate, H)))])
+
+    def load_figures(q, H):
+        r = slice(64 * H, 64 * H + 64)
+        dmas(q, "dw%d" % H, [m for h in range(2) for m in ((part("WIN%d" % H, h, SHIFT, W), X(T.fig[r, 0:W - SHIFT])), (part("WIN%d" % H, h, 0, SHIFT), X(T.fig[r, W - SHIFT:W])))])
+
+    def pieces(H, x0, x1):
+        cuts = [(0, x0, min(x1, SHIFT)), (0, max(x0, SHIFT), x1), (1, x0, x1)]
+        return [(h, a, b, (1024 * h + a - SHIFT) % W) for h, a, b in cuts if a < b]
+
+    for H in range(2):
+        dmas("s", "dl%d" % H, [(part("PR", h, 8 * H, 8 * H + 8), X(rows((T.pcol, T.prow)[h], H))) for h in range(2)])
+        dmas("s", "dn%d" % H, [(part("ZI", h, 640 * H, 640 * H + 128), X(rows(T.need, H))) for h in range(2)])
+    load_mates("y", 0)
+    load_figures("y", 0)
+    before("y", S("NW0", 0, 1024)[1], [])
+    load_mates("y", 1)
+    load_figures("y", 1)
+    before("y", S("NW1", 0, 1024)[1], [])
+    for H in range(2):
+        dmas("y", "dc%d" % H, [(S("CW%d" % H, 0, W), X(T.fig[:]))])
+    dmas("y", "df", [(part("FIN", h, 1024 * H + a, 1024 * H + b), X(T.fig[64 * H:64 * H + 64, c:c + b - a])) for H in range(2) for h, a, b, c in pieces(H, 0, 1024)])
+
     iota(S("pI", 0, 1), [[0, 1]], 0, 1)
-    iota(B("IOT", 0, 160), [[1, 160]])
-    iota(B("DIV16", 0), [[1, 8], [0, 16]])
-    iota(B("DIV8", 0), [[1, 16], [0, 8]])
-    load_mates(0)
-    iota(B("DIV4", 0), [[1, 32], [0, 4]])
-    iota(S("VJ", 0, 768), [[2, 768]], 593)
-    iota(B("MOD16", 0), [[0, 8], [1, 16]])
-    iota(B("MOD20", 0, 160), [[0, 8], [1, 20]])
-    iota(S("ZB", 0, W), [[0, W]])
-    for t in range(1, ROUNDS):
-        load_mates(t)
-    PF, PG, PS = S("pF", 0, 1), S("pF", 1, 2), S("pF", 2, 3)
-
-    def cc(i):
-        return S("cc", i, i + 1)
-
-    ms(B("ONE", 0), 1.0)
-    ms(S("CB", 0, 512, 1, 0, 64), 4.0)
-    ms(S("CB", 0, 512, 1, 64, 128), 81.0 / 128)
-    ms(S("cc", 10, 14, 1, 64, 128), -120.0)
-    for t in range(ROUNDS):
-        ms(S("cc", 10 + t, 11 + t, 1, 0, 64), 32768.0 * (t + 1))
-    ts(S("pI", 1, 2), S("pI", 0, 1), 4, A.logical_shift_right)
-    ts(S("pI", 2, 3), S("pI", 0, 1), 15, A.bitwise_and)
-    cp(S("pF", 0, 3), S("pI", 0, 3))
-    ts(B("BLK", 0), B("DIV16", 0), PG, A.is_equal)
-    ts(S("B8", 0, 8), S("IOT", 0, 8), PG, A.is_equal)
-    for a in range(4):
-        ts(cc(a), PS, float(a), A.is_equal)
-    ts(cc(4), PS, 4.0, A.is_ge, 200.0, A.mult)
-    ts(cc(5), PS, 15.0, A.is_lt, 200.0, A.mult)
-    ts(cc(6), PG, 4.0, A.mult, PF, A.add)
-    tt(cc(7), cc(4), PF, A.add)
-    ts(cc(8), PG, 4.0, A.mult, cc(5), A.add)
-    ts(cc(9), cc(4), 2.0, A.mult, cc(6), A.add)
-    for a in range(4):
-        ts(B("SEL", a), B("BLK", 0), cc(a), A.mult)
-    for c in range(4):
-        ts(B("SV1", c), B("IOT", 0), 4.0 * c, A.subtract, cc(7), A.is_equal)
-    ts(B("IDb", 0), B("IOT", 0), PF, A.is_equal)
-    ts(B("WIT", 0, 160), B("IOT", 0, 160), cc(6), A.is_equal, 256.0, A.mult)
-    ts(B("WJT", 0, 160), B("IOT", 0, 160), 16.0, A.subtract, cc(9), A.is_equal)
-    ts(S("MK", 0, 16), S("IOT", 0, 16), PS, A.is_equal)
-    ts(S("MS", 0, 8), S("IOT", 0, 8), PG, A.is_equal)
-    for t in range(ROUNDS):
-        ts(S("ZF", 32 + 8 * t, 40 + 8 * t), S("IOT", 0, 8), 16.0, A.mult, W + 128.0 * t, A.add)
-    for c in range(4):
-        ts(B("SU1", c), B("DIV4", 0), float(c), A.subtract, cc(8), A.is_equal)
-    ts(S("KC", 0, 32), S("ZF", 32, 64), PS, A.add)
-    ts(cc(4), PS, 8.0, A.is_ge)
-    ts(cc(5), PS, 3.0, A.not_equal, 400.0, A.mult)
-    ts(cc(7), cc(4), -8.0, A.mult, PF, A.add)
-    ts(cc(14), PG, 2.0, A.mult, cc(5), A.add)
-    ts(cc(8), cc(4), 400.0, A.mult, cc(7), A.add)
-    ts(cc(15), cc(4), -400.0, A.mult, 400.0, A.add)
-    for c in range(2):
-        ts(B("SV3", c), B("DIV8", 0), float(c), A.subtract, cc(14), A.is_equal)
-    tt(cc(15), cc(15), cc(7), A.add)
-    cp(S("NL", 0, 16), S("PR", 0, 16))
+    iota(B("IOT", 0), [[1, 128]])
     for h in range(2):
-        for c in range(2):
-            ts(B("SU3", 2 * h + c), B("IOT", 0), 8.0 * c, A.subtract, cc(8 + 7 * h), A.is_equal)
-    act(S("W8F", 0, 8), S("B8", 0, 8), F.Copy, 0.0, BIG)
-    act(S("W8A", 0, 8), S("B8", 0, 8), F.Copy, 0.0, 64.0)
-    act(B("W1F", 0), B("BLK", 0), F.Copy, 0.0, BIG)
-    act(B("W1A", 0), B("BLK", 0), F.Copy, 0.0, 64.0)
+        iota(B("CA", h, 64), [[16, 4], [64, 2], [1, 8]], 8 * h)
+        iota(B("CB", h, 64), [[1, 4], [4, 2], [0, 8]])
+    iota(S("OWNW", 0, 256), [[1, 256]])
+    for h in range(2):
+        iota(B("CC", h, 64), [[1, 4], [4, 8], [0, 2]])
+        iota(B("CD1", h, 64), [[1, 4], [4, 8], [32, 2]], 64 * h)
+    iota(S("N32", 0, 32), [[1, 8], [0, 4]])
+    for q in range(4):
+        iota(B("BI", q, 64), [[8, 2], [16, 4], [1, 8]])
+    for q in range(4):
+        iota(B("CE", q, 64), [[0, 2], [1, 4], [0, 8]], 4 * q)
+    iota(B("D16", 0), [[1, 8], [0, 16]])
+    iota(S("U8", 0, 8), [[1, 4], [0, 2]])
+    iota(S("I16", 0, 32), [[0, 2], [1, 16]])
+
+    def cc(i, n=1):
+        return S("cc", i, i + n)
+
+    pP, pH, pG, pS, pA, pM, pQ, pT = [S("pF", i, i + 1) for i in range(8)]
+    I4 = S("IOT", 0, 4)
+    pad = [(part("NW%d" % H, 0, 768, 1024)[0], [("pad", H, H + 1, 1, True)]) for H in range(2)]
+    ms(pad[0], 0)
+    for i, (sh, mask) in enumerate([(6, 1), (4, 3), (0, 15), (0, 3), (4, 7), (4, 1), (2, 3)]):
+        ts(S("pI", i + 1, i + 2), S("pI", 0, 1), sh, A.logical_shift_right, mask, A.bitwise_and)
+    cp(S("pF", 0, 8), S("pI", 0, 8))
+    for q in range(1, 4):
+        act(B("OWNW", q, 256), B("OWNW", 0, 256), F.Copy, 256.0 * q)
+    ts(cc(0), pH, 1000.0, A.mult, pP, A.add)
+    ts(cc(1), pH, -100.0, A.mult, 100.0, A.add)
+    ts(cc(2), pS, 2.0, A.is_ge, 100.0, A.mult)
+    ts(cc(3), pH, 100.0, A.mult, pG, A.add)
+    ts(cc(4, 4), I4, pA, A.not_equal, 100.0, A.mult)
+    ts(cc(8, 4), I4, pT, A.is_equal, 2.0, A.mult)
+    ts(cc(16), pH, -1.0, A.mult, 1.0, A.add)
+    ts(cc(17), pH, 593.0, A.mult)
+    ts(cc(18), pS, 0.0, A.is_equal)
+    ts(cc(19), pS, 1.0, A.is_equal)
+    ts(cc(20), pH, -584.5, A.mult, 593.0, A.add)
+    ts(cc(21), pH, -1.0, A.mult, 2.0, A.add)
+    tt(cc(1), cc(1), pG, A.add)
+    tt(cc(3), cc(3), cc(2), A.add)
+    ts(cc(8, 4), cc(8, 4), pH, A.mult, cc(16), A.add)
+    ts(cc(12, 4), I4, pT, A.is_equal, cc(17), A.mult)
+    tt(cc(20), cc(20), cc(19), A.mult)
+    tt(cc(28), cc(21), cc(18), A.mult)
+    ts(cc(4, 4), cc(4, 4), cc(1), A.add)
+    ts(cc(23), pS, 0.0, A.not_equal, 100.0, A.mult)
+    ts(cc(24), pA, 32.0, A.mult, cc(1), A.add)
+    ts(cc(22), pG, 2.0, A.mult, pH, A.add)
+    tt(cc(23), cc(23), cc(1), A.add)
+    ts(cc(24), cc(16), 100.0, A.mult, cc(24), A.add)
+    for kp in range(2):
+        ts(B("SEL", kp), B("CA", 0), 64.0 * kp, A.subtract, cc(0), A.is_equal)
+        ts(B("SEL", 2 + kp), B("CB", 0), 4.0 * kp, A.subtract, cc(3), A.is_equal)
     for a in range(4):
-        act(B("BA", a), B("BLK", 0), F.Copy, a / 8.0, 0.0)
-    dmas("s", "df", [(S("WIN", SHIFT, W), X(T.fig[:, 0:W - SHIFT])), (S("WIN", 0, SHIFT), X(T.fig[:, W - SHIFT:W]))])
-    act(B("BB", 0), B("MOD16", 0), F.Copy, 0.0, 1.0 / 128)
+        for kp in range(2):
+            ts(B("SEL", 4 + 2 * a + kp), B("CB", 0), 4.0 * kp, A.subtract, cc(4 + a), A.is_equal)
+    for c in range(8):
+        ts(B("SEL", 12 + c), B("CC", 0), 4.0 * c, A.subtract, cc(23), A.is_equal)
+        ts(B("SEL", 20 + c), B("CD1", 0), 4.0 * c, A.subtract, cc(24), A.is_equal)
+        if c == 3:
+            cp(B("NL", 0, 8), B("PR", 0, 8))
+
+    def weights():
+        ms(B("E0", 0), 1.0 / 128)
+        ms(S("DRM", 0, 256), 0.0)
+        ms(pad[1], 0)
+        ms(B("ONE", 0), 1.0)
+        ts(B("W32", 0, 32), S("N32", 0, 32), cc(22), A.is_equal, BIG, A.mult)
+        ts(B("W32", 1, 32), S("N32", 0, 32), cc(22), A.is_equal, 64.0, A.mult)
+        ms(S("DRM", 0, 256, 64), NONE)
+        ts(cc(25), pS, 8.0, A.is_equal, cc(18), A.add)
+        ts(cc(26), cc(22), 2.0, A.mult)
+        ts(cc(27), cc(22), 2.0, A.mult, 1.0, A.add)
+        ts(cc(29), pS, 2.0, A.is_lt)
+        ts(cc(30), pS, -1.0, A.mult, pA, A.add)
+        ts(cc(31), pH, -4.0, A.mult, 4.0, A.add)
 
     def late_constants():
-        ts(S("PP", 0, 8), S("PR", 0, 8), 1024.0, A.mult, 1024.0, A.add)
-        ts(B("CFL", 0, 160), B("MOD20", 0, 160), 16.0, A.is_lt)
-        ts(B("DRM", 0), B("MOD16", 0), 0.0, A.is_equal, float(2 ** 26), A.mult)
-        tt(S("PP", 8, 16), S("PP", 0, 8), S("PR", 8, 16), A.add)
-        ts(B("DRS", 0, 160), B("MOD20", 0, 160), 0.5, A.is_gt)
-        for t in range(ROUNDS):
-            act(B("CIT", t, 160), B("CFL", 0, 160), F.Copy, 0.0, cc(10 + t))
-        for m in range(8):
-            act(B("EE", m, 16), S("MK", 0, 16), F.Copy, 0.0, S("PP", 8 + m, 9 + m))
-        mm(S("HH", 448, 456), B("EE", 0), S("MS", 0, 8), True, True)
-        for h in range(16):
-            mm(B("HH", h, 8), B("WIN", h), S("B8", 0, 8), True, True)
-        act(S("HT", 0, W), S("WIN", 0, W), F.Copy, -0.25, 0.5)
-        act(B("IDf", 0), B("IDb", 0))
+        FILL = fills(1, -1)
+        yield FILL["init"]
+        cp(B("NL", 1, 8), B("PR", 1, 8))
+        for a in range(2):
+            ts(B("W1", a, 256), S("CE", 0, 256), cc(26 + a), A.is_equal, BIG, A.mult)
+            act(B("W1", 2 + a, 256), B("W1", a, 256), F.Copy, 0.0, 64.0 / BIG)
+        ts(cc(30), cc(30), pH, A.mult, pP, A.add)
+        tt(cc(31), cc(31), pG, A.add)
+        ts(cc(32), cc(18), pH, A.mult, -2.0, A.mult)
+        ts(cc(33), cc(16), cc(29), A.mult)
+        ts(cc(17), pH, 1.0, A.add, cc(29), A.mult)
+        ts(S("MK", 0, 16), S("IOT", 0, 16), pS, A.is_equal)
+        tt(cc(32), cc(32), cc(33), A.subtract)
+        ts(B("NMW", 0), B("IOT", 0), cc(30), A.is_equal, cc(21), A.mult)
+        ts(S("OWW", 128, 136), S("IOT", 0, 8), cc(31), A.is_equal, cc(17), A.mult)
+        ts(S("OWW", 136, 140), I4, cc(31), A.is_equal, cc(17), A.mult)
+        ts(B("OWW", 0), B("D16", 0), cc(31), A.is_equal, cc(32), A.mult)
+        yield from lists(1, 0)
+        ts(S("MS", 0, 8), S("IOT", 0, 8), pM, A.is_equal, 0.5, A.mult)
+        ts(S("MS", 8, 16), S("IOT", 0, 8), pM, A.is_equal)
+        ms(S("LW", 0, 144), 0.0)
+        ms(B("SEED", 0), -1.0)
+        ms(B("KEEP", 0), 1.0)
+        ts(cc(2), pH, 100.0, A.mult, pG, A.add)
+        ts(cc(34), pH, 288.0, A.mult, -296.5, A.add)
+        ms(S("KEEP", 0, 128, 16), 0.0)
+        ts(S("LW", 16, 144, 16), S("U8", 0, 8), cc(2), A.is_equal)
+        ts(cc(35), pQ, -2.0, A.mult, 1.0, A.add)
+        ms(B("OH", 0), -7.5)
+        act(cc(40), pQ, F.Copy, 0.0, 7.5)
+        act(cc(41), pQ, F.Copy, -M16, 2 * M16)
+        act(cc(36, 4), I4, F.Identity, pP, 128.0)
+        act(B("W32", 2, 32), B("W32", 1, 32), F.Copy, 0.0, cc(25))
+        act(cc(36, 4), cc(36, 4), F.Copy, float(W))
+        for a in range(2):
+            act(B("W1", 4 + a, 256), B("W1", 2 + a, 256), F.Copy, 0.0, cc(25))
+        act(B("ONf", 0), B("ONE", 0))
+        pick(B("IDb", 0), B("ONE", 0), [[-1, 128]], 0, 1)
+        for H in range(2):
+            mm(B("YB", H), B("E0", 0), B("OH", 0), True, False)
+            for hi in range(16):
+                mm(B("YB", H), S("LW", 16 - hi, 144 - hi), B("WIN%d" % H, hi), False, hi == 15)
+        yield FILL["costs"]
+        act(S("T2", 0, 256), S("YB", 0, 256), F.Copy, M16, 1.0)
+        act(S("T3", 0, 256), S("YB", 0, 256), F.Identity, cc(40), pQ)
+        act(S("T2", 0, 256), S("T2", 0, 256), F.Identity, cc(41), cc(35))
+        yield FILL["parts"]
+        tt(S("ZB", 0, 256), S("T2", 0, 256), S("T3", 0, 256), A.add)
+        for hi in range(8):
+            pick(B("SGW", hi), B("ONE", 0), [[-8, 2], [-32, 4], [0, 16]], -hi, 1)
+        pick(B("IDf", 0), B("ONf", 0), [[-1, 128]], 0, 1)
 
-    def late_places():
-        cp(S("KRX", 16, 24), S("HH", 448, 456))
-        cp(S("CI", 0, 128), B("HH", 0))
-        ts(S("KI", 0, 8), S("KRX", 16, 24), 1024.0, A.subtract)
-        ts(S("CI", 128, 256), S("CI", 0, 128), 2032, A.bitwise_and)
-        ts(S("KI", 8, 16), S("KI", 0, 8), 10, A.logical_shift_right, 1023, A.bitwise_and)
-        ts(S("KI", 16, 24), S("KI", 0, 8), 1023, A.bitwise_and)
-        ts(S("CI", 256, 384), S("CI", 0, 128), 15, A.bitwise_and)
-        ts(S("KRX", 0, 8), S("KI", 8, 16), 2.0, A.mult, 17.0, A.add)
-        ts(S("KRX", 8, 16), S("KI", 16, 24), 2.0, A.mult, 593.0, A.add)
-        cp(S("ZB", 0, W, 16), S("CI", 128, 256))
-        cp(S("ZB", 1, W, 16), S("CI", 256, 384))
-        ts(S("HZ", 0, W), S("HT", 0, W), 8388608.0, A.add, 8388608.0, A.subtract)
-
-    def vb_bias():
-        mm(S("VB", 0, 512), B("ONE", 0), S("CB", 0, 512), True, False)
-
-    def lists_a(t):
-        if t > 0:
-            cp(S("NL", 0, 16), S("MR%d" % (t - 1), 0, 16))
-        act(B("VO", 0), G(S("VJ", 0, 768), S("NL", 8, 16)), F.Copy, 0.0, 0.5)
-        cp(B("G16", 0), G(B("RW%d" % t, 0, 1024), S("NL", 0, 8)))
-        if t > 0:
-            act(B("U2", 0), G(S("UC", 0, 768), S("NL", 8, 16)))
+    def lists(H, t):
+        FILL = fills(H, t - 1)
+        nl = B("NL", H, 8) if t == 0 else B("MR", 3 * H + t - 1, 8)
+        gg, own, need = B("GG", H), B("OWN", H), B("ZI", 5 * H + t)
+        mates = S("NW%d" % H, 0, 1024)
+        mates = (mates[0], mates[1] + pad[H][1])
+        if MATES_ON_SCALAR:
+            act(gg, G(mates, nl), F.Identity, cc(12 + (t + 1) % 4), cc(8 + t))
         else:
-            ts(B("U2", 0), G(S("CM", 0, 768), S("NL", 8, 16)), 4.0, A.mult, 34.0, A.add)
-        for a in range(3):
-            mm(B("VB", a), B("SEL", a), B("G16", 0), False, False)
-        for c in range(2):
-            mm(S("VB", 384, 448), B("SV3", c), S("G16", c, 128, 2), False, c == 1)
+            ts(gg, G(mates, nl), cc(8 + t), A.mult, cc(12 + (t + 1) % 4), A.add)
+        if OWN_ON_SCALAR:
+            act(own, G(S("OWNW", 0, 1024), nl), F.Identity, cc(20), cc(28))
+        else:
+            ts(own, G(S("OWNW", 0, 1024), nl), cc(28), A.mult, cc(20), A.add)
 
-    def lists_b(t):
-        def needs(b0, b1):
-            for b in range(b0, b1):
-                o, i = S("ZR", b, W, 16), S("HZ", W + 128 * t, W + 128 * t + 128)
-                if t == 0 and b % 2 == 0:
-                    act(o, i)
-                else:
-                    cp(o, i)
+        def spread(out, sel, name, n):
+            for c in range(n):
+                mm(out, B("SEL", sel + c), S(name, 128 * H + c, 128 * H + 128, n), c == 0, c == n - 1)
 
-        tt(B("XI", 3), B("U2", 0), B("VO", 0), A.mult)
-        for a in range(3):
-            tt(B("XI", a), B("U2", 0), B("VB", a), A.mult)
-        needs(0, 8)
-        ts(S("XJ", 0, 512), S("XI", 0, 512), 5, A.logical_shift_right, 2047, A.bitwise_and)
-        needs(8, 16)
-        cp(S("LST", 0, 512), S("XJ", 0, 512))
-        if t == 0:
-            ts(S("UC", 0, 768), S("CM", 0, 768), 4.0, A.mult, 34.0, A.add)
+        def needs(who):
+            for b, by in enumerate(NEEDS if H + t else FIRST_NEEDS):
+                o = S("ZR", 1024 * H + b, 1024 * H + 1024, 8)
+                if by == who == "s":
+                    act(o, need)
+                elif by == who == "v":
+                    cp(o, need)
+                elif by == who:
+                    pick(o, need, [[0, 128]])
 
-    def lists_c():
-        for c in range(4):
-            mm(S("MI", 0, 32), B("SU1", c), S("G16", c, 128, 4), c == 0, c == 3)
-        mm(S("MI", 32, 64), B("ONE", 0), S("CB", 0, 32), True, False)
-        for c in range(4):
-            mm(S("MI", 32, 64), B("SV1", c), S("G16", c, 128, 4), False, c == 3)
-        for h in range(2):
-            for c in range(2):
-                mm(S("MI", 224 + 64 * h, 288 + 64 * h), B("SU3", 2 * h + c), S("U2", c, 128, 2), c == 0, c == 1)
+        needs("g")
+        spread(S("UB", 0, 64), 0, "GG", 2)
+        for a in range(4):
+            spread(B("VV", a, 64), 4 + 2 * a, "GG", 2)
+        spread(B("VV", 4, 64), 2, "OWN", 2)
+        spread(S("YB", 0, 16), 12, "OWN", 8)
+        spread(S("YB", 16, 32), 20, "GG", 8)
+        if H + t == 0:
+            needs("v")
+        yield FILL["mates"]
+        act(S("UUS", 0, 64), S("UB", 0, 64), F.Copy, 17.0, 2.0)
+        yield FILL["copied"]
+        act(S("UUS", 64, 80), S("YB", 0, 16), F.Copy, 17.0, 2.0)
+        for name, col, cols in LISTS:
+            if cols == 64:
+                tt(S("XI", col, col + 64), S("UUS", 0, 64), B("VV", int(name[1]), 64), A.mult)
+        needs("s")
+        tt(S("XI", F1, F1 + 16), S("UUS", 64, 80), S("YB", 16, 32), A.mult)
+        act(S("WIN%d" % H, W + 128 * t, W + 128 * t + 128), need, F.Copy, 0.0, 2.0)
+        yield FILL["places"]
+        ts(S("XJ", 0, 336), S("XI", 0, 336), 5, A.logical_shift_right, 2047, A.bitwise_and)
+        if H + t:
+            needs("v")
+        yield FILL["cast"]
+        cp(B("LST", H, 336), S("XJ", 0, 336))
 
-    def names(t):
-        mm(S("MI", 64, 224), B("ONE", 0), B("CIT", t, 160), True, False)
-        mm(S("MI", 64, 224), B("U2", 0), B("WIT", 0, 160), False, False)
-        mm(S("MI", 64, 224), B("G16", 0), B("WJT", 0, 160), False, True)
-
-    vb_bias()
-    lists_a(0)
-    lists_b(0)
-    lists_c()
-    for t in range(ROUNDS):
+    def tail(H, t):
         dst = T.cores[(rank + 1 + t % 3) % N]
         src = T.cores[(rank - 1 - t % 3) % N]
-        last = t == ROUNDS - 1
-        kr = "KRX" if t == 0 else "KR%d" % (t - 1)
-        win = "WIN" if t == 0 else "CW"
-        zs = W + 128 * t
-
-        mm(B("S2", 0), B("ONE", 0), B("BB", 0), True, False)
-        for a in range(4):
-            mm(B("A%d" % a, 0), B("ONE", 0), B("BA", a), True, False)
-        if t > 0:
-            names(t)
-        for name, off, cols, pos in CHUNKS:
-            o, n = S("LST", off, off + cols), 16 * cols
-            if name == "a0":
-                act(B("UP", 0), S("MI", 224, 352))
-                act(S("U1", 0, 32), S("MI", 0, 32), F.Copy, 34.0, 4.0)
-            act(S("CD", pos, pos + n), G(S(win, 0, W), o))
-            tt(S("FD", pos, pos + n), G(S("WIN", 0, W), o), S("ZR", 0, W, W // n), A.is_lt)
-            if name == "a0":
-                tt(S("XI", 512, 544), S("U1", 0, 32), S("MI", 32, 64), A.mult)
-                for h in range(2):
-                    tt(S("XI", 544 + 64 * h, 608 + 64 * h), B("UP", h, 64), S("VB", 384, 448), A.mult)
-            if name == "a1":
-                ts(S("XJ", 512, 672), S("XI", 512, 672), 5, A.logical_shift_right, 2047, A.bitwise_and)
-            if name == "a2":
-                cp(S("LST", 512, 672), S("XJ", 512, 672))
-            if name == "f1":
-                for a in range(4):
-                    mm(B("A%d" % a, 0), S("CD", pos + a, pos + n, 4), B("W1A", 0), False, False)
-                    mm(B("A%d" % a, 0), S("FD", pos + a, pos + n, 4), B("W1F", 0), False, a < 3)
-                continue
-            bank = "S2" if name == "f2" else "A" + name[1]
-            nb, b0 = n // 128, 8 if off == 608 else 0
-            for b in range(nb):
-                mm(S(bank, b0 + b, 128, 16), S("FD", pos + b, pos + n, nb), S("W8F", 0, 8), False, False)
-            for b in range(nb):
-                mm(S(bank, b0 + b, 128, 16), S("CD", pos + b, pos + n, nb), S("W8A", 0, 8), False, b0 + b == 15 and name in ("f2", "a3"))
-            if t == 0 and name == "a0":
-                late_constants()
-                names(t)
-            if t == 0 and name == "a2":
-                late_places()
-        act(B("R", 0), B("A0", 0))
-        tt(B("R", 1), B("R", 0), B("A1", 0), A.min)
-        tt(B("R", 2), B("R", 1), B("A2", 0), A.min)
-
-        tt(B("R", 3), B("R", 2), B("A3", 0), A.min)
-        tt(B("TT", 0), B("R", 3), B("S2", 0), A.add)
-        scan(B("MSC", 0), B("DRM", 0), B("TT", 0), float(2 ** 26), A.add, A.min)
-        m8 = S("MSC", 15, 128, 16)
-        ts(B("MC", t, 8), m8, BIG - 1, A.min, 1.0, A.add)
-        cp(S("MI32", 0, 8), m8)
+        last, FILL = t == ROUNDS - 1, fills(H, t)
+        bank, win, r = "S%d" % H, "WIN%d" % H, slice(64 * H, 64 * H + 64)
+        yield FILL["start"]
+        scan(S("MSC", 0, 256), S("DRM", 0, 256), S(bank, 0, 256), 0.0, A.max, A.min)
+        yield FILL["min"]
+        m, ck = S("MSC", 63, 256, 64), S("CK", 16 * H + t, 16 * H + 16, 4)
+        taken = [S("CK", 16 * H + 4 * q + t, 16 * H + 4 * q + t + 1) for q in range(4)]
+        cp(S("MI", 0, 4), m)
+        act(ck, m, F.Copy, -NONE)
+        yield FILL["index"]
+        ts(S("MI", 4, 8), S("MI", 0, 4), 2 ** 19 + 15, A.bitwise_and)
+        ts(S("MI", 8, 12), S("MI", 0, 4), 4, A.logical_shift_right, 2 ** 15 + 3, A.bitwise_and)
+        yield FILL["seed"]
+        cp(S("SEED", 0, 128, 16), S("MI", 4, 12))
+        yield FILL["count"]
+        scan(B("CNT", 0), B("KEEP", 0), B("SEED", 0), 0.0, A.mult, A.add)
+        yield FILL["hot"]
+        ts(B("OH", 0), B("CNT", 0), 0.0, A.is_equal)
+        yield FILL["product"]
+        tt(B("PW", 0), B("OH", 0), B("NM", 0), A.mult)
+        yield FILL["product"]
+        scan(B("SC", 0), B("KEEP", 0), B("PW", 0), 0.0, A.mult, A.add)
+        yield FILL["sum"]
+        act(S("NT", 0, 4), ck, F.Relu, cc(36 + t))
+        tt(S("KF", 0, 8), S("SC", 15, 128, 16), S("NM", 128, 136), A.add)
+        yield FILL["names"]
         for q in range(8):
-            o, i, col = S("OH", 20 * q, 20 * q + 16), B("TT", q, 16), S("MC", 8 * t + q, 8 * t + q + 1)
-            if q >= 3:
-                act(o, i, F.Relu, col, -1.0)
-                continue
-            ts(o, i, 1.0, A.add, col, A.is_equal)
-            if q == 0:
-                ts(S("MI32", 8, 16), S("MI32", 0, 8), 4, A.logical_shift_right, 3, A.bitwise_and)
-        for a in range(4):
-            ts(S("OH", 16 + a, 160, 20), S("MI32", 8, 16), float(a), A.is_equal)
-        tt(B("PW", 0, 160), B("OH", 0, 160), S("MI", 64, 224), A.mult)
-        scan(B("SC2", 0, 160), B("DRS", 0, 160), B("PW", 0, 160), 0.0, A.mult, A.add)
-        msg, km, flag = "MSG%d" % t, "KM%d" % t, FLAG * (t + 1)
-        tt(S(km, 16, 24), S("SC2", 19, 160, 20), S(kr, 16, 24), A.max)
-        for q in range(8):
-            o, col = B("EE", q, 16), S(km, 16 + q, 17 + q)
-            if q < 3:
-                ts(o, S("MK", 0, 16), col, A.mult)
-            else:
-                act(o, S("MK", 0, 16), F.Copy, 0.0, col)
-        LQ = S("HH", 448, 456)
-        mm(LQ, B("EE", 0), S("MS", 0, 8), True, True)
-        if not last:
-            vb_bias()
-        ts(S("KI", 0, 8), S(km, 16, 24), 1024.0, A.subtract)
-        ts(S("NG", 0, 8), S(km, 16, 24), flag, A.is_ge)
-        ts(S("KI", 8, 16), S("KI", 0, 8), 10, A.logical_shift_right, 1023, A.bitwise_and)
-        ts(S("KI", 16, 24), S("KI", 0, 8), 1023, A.bitwise_and)
-        ts(S(km, 0, 8), S("KI", 8, 16), 2.0, A.mult, 17.0, A.add)
-        ts(S(km, 8, 16), S("KI", 16, 24), 2.0, A.mult, 593.0, A.add)
-        tt(S("XC", 8, 16), S(km, 0, 8), S(kr, 8, 16), A.mult)
-        tt(S("XC", 0, 8), S(kr, 0, 8), S(km, 8, 16), A.mult)
-        tt(S("XC", 16, 24), S(km, 0, 8), S(km, 8, 16), A.mult)
-        ts(S("LHI", 24, 48), S("XC", 0, 24), 12, A.logical_shift_right, 15, A.bitwise_and)
-        ts(S("LI", 0, 8), LQ, 1024.0, A.subtract)
-        ts(S("LHI", 0, 24), S("XC", 0, 24), 5, A.logical_shift_right, 127, A.bitwise_and)
-        ts(S(msg, 0, 8), S("LI", 0, 8), 10, A.logical_shift_right, 1023, A.bitwise_and)
-        ts(S(msg, 8, 16), S("LI", 0, 8), 1023, A.bitwise_and)
-        send(S("MR%d" % t, 0, 16), S(msg, 0, 16), dst, "rn%d" % t, "ln%d" % t)
-        recv(S("MR%d" % t, 0, 16), src, "rn%d" % t)
-        cp(S("LHF", 0, 48), S("LHI", 0, 48))
-
-        chain = [
-            lambda: ts(S("ZF", 8, 16), LQ, flag, A.is_lt),
-            lambda: ts(S("ZF", 16, 24), S(msg, 0, 8), 2.0, A.mult, 17.0, A.add),
-            lambda: ts(S("ZF", 24, 32), S(msg, 8, 16), 2.0, A.mult, 593.0, A.add),
-            lambda: tt(S("ZF", 32, 40), S("ZF", 8, 16), B("KC", t, 8), A.mult),
-            lambda: tt(S("ZI", 0, 8), S("ZF", 16, 24), S("ZF", 24, 32), A.mult),
-            lambda: ts(S("ZI", 8, 16), S("ZI", 0, 8), 5, A.logical_shift_right, 2047, A.bitwise_and),
-            lambda: tt(S("ZF", 40, 48), S("ZI", 8, 16), S("ZF", 32, 40), A.max),
-            lambda: cp(S("OFF", 0, 8), S("ZF", 40, 48)),
-            lambda: cp(B("ZS%d" % t, 0), G(S("HZ", 0, zs + 128), S("OFF", 0, 8))),
-            lambda: send(S("HZ", zs + 128, zs + 256), B("ZS%d" % t, 0), dst, "rz%d" % t, "lz%d" % t)]
-        step = 0
-        if not last:
-            for step in range(4):
-                chain[step]()
-            step = 4
+            act(B("EE", q, 16), S("MK", 0, 16), F.Copy, 0.0, S("KF", (q + 4) % 8, (q + 4) % 8 + 1))
+        mm(S("LQ", 0, 8), B("EE", 0), S("MS", 0, 8), True, True)
+        tt(S("XC", 8, 12), S("KF", 0, 4), S("KF", 4, 8), A.mult)
+        tt(S("XC", 0, 8), S("KF", 0, 8), S("NM", 132, 140), A.mult)
+        ts(S("LHI", 24, 28), S("XC", 8, 12), 5, A.logical_shift_right, 2047, A.bitwise_and)
+        ts(S("LHI", 12, 24), S("XC", 0, 12), 12, A.logical_shift_right, 15, A.bitwise_and)
+        tt(S("OFF", 0, 4), S("LHI", 24, 28), S("NT", 0, 4), A.max)
+        ts(S("LHI", 0, 12), S("XC", 0, 12), 5, A.logical_shift_right, 127, A.bitwise_and)
+        for q in range(4):
+            act(B("EE2", q, 16), S("MK", 0, 16), F.Copy, 0.0, S("OFF", q, q + 1))
         for h in range(2):
-            for q in range(4 * h, 4 * h + 4):
+            mm(part("UB", h, 64, 72), S("EE2", 0, 64), S("MS", 8, 16), True, True)
+        yield FILL["spread"]
+        out, land = (B("MFo", H, 8), B("MFi", H, 8)) if last else (B("MSG", 3 * H + t, 8), B("MR", 3 * H + t, 8))
+        ts(out, S("LQ", 0, 8), cc(34), A.add)
+        send(land, out, dst, src, "rn%d%d" % (H, t))
+        cp(S("LHF", 0, 24), S("LHI", 0, 24))
+        cp(S("OFFL", 0, 8), S("UB", 64, 72))
+        act(B("T1", 0), G(S(win, 0, W + 128 * t + 128), S("OFFL", 0, 8)), F.Copy, M2, 511.0 / 512)
+
+        def hot(q):
+            for c in range(3):
+                n = 4 * c + q
+                ts(B("OL", 3 * q + c), B("IOT", 0), S("LHF", n, n + 1), A.is_equal, taken[q], A.mult)
+                act(B("SQ", 3 * q + c, 32), S("I16", 0, 32), F.Square, S("LHF", 12 + n, 13 + n), -1.0)
+
+        def hits(half):
+            act(B("OHH", half, 192), B("SQ", half, 192), F.Relu, 1.0, -1.0)
+            for q in (2 * half, 2 * half + 1):
+                costs = S("HH", 0, 128, 1, 32 * q, 32 * q + 32)
+                mm(costs, B("IDb", q, 32), B("ZB", H), True, False)
                 for c in range(3):
-                    n, m = 3 * q + c, 8 * c + q
-                    act(B("SQ", n, 16), S("IOT", 0, 16), F.Square, S("LHF", 24 + m, 25 + m), -1.0)
-                    ts(B("OL", n), B("IOT", 0), S("LHF", m, m + 1), A.is_equal, S("NG", q, q + 1), A.mult)
-                    if not last and step < len(chain):
-                        chain[step]()
-                        step += 1
-            act(B("OHH", h, 192), B("SQ", h, 192), F.Relu, 4096.0, -4096.0)
-            for q in range(4 * h, 4 * h + 4):
-                for c in range(3):
-                    n = 3 * q + c
-                    mm(S("HH", q, 128, 8), B("OL", n), B("OHH", n, 16), c == 0, c == 2)
-        recv(S("HZ", zs + 128, zs + 256), src, "rz%d" % t)
+                    mm(costs, B("OHH", 3 * q + c, 32), B("OL", 3 * q + c), False, c == 2)
+
+        hot(0)
+        act(B("ZS", 4 * H + t), B("T1", 0), F.Copy, -M2 / 2, 0.5)
+        send(B("ZI", 5 * H + t + 1), B("ZS", 4 * H + t), dst, src, "rz%d%d" % (H, t))
+        hot(1)
+        hot(2)
+        hits(0)
+        hot(3)
+        yield FILL["squares"]
+        hits(1)
+        yield FILL["sent"]
         if not last:
-            send(S("KR%d" % t, 0, 24), S(km, 0, 24), dst, "rk%d" % t, "lk%d" % t)
-            recv(S("KR%d" % t, 0, 24), src, "rk%d" % t)
-            lists_a(t + 1)
-        else:
-            other = [
-                lambda: ts(S("CK", 0, 32), S("MC", 0, 32), 1.0, A.subtract),
-                lambda: ts(S("CK", 32, 64), S("MC", 0, 32), BIG, A.is_lt),
-                lambda: cp(S("CKI", 0, 32), S("CK", 0, 32)),
-                lambda: ts(S("CKI", 32, 64), S("CKI", 0, 32), 6, A.logical_shift_right),
-                lambda: ts(S("CK", 64, 96), S("CKI", 32, 64), 1.0, A.add),
-                lambda: tt(S("CK", 96, 128), S("CK", 64, 96), S("CK", 32, 64), A.mult),
-                lambda: ts(S("CK", 0, 32), S("CK", 96, 128), 1.0, A.subtract)]
-            for i in range(len(chain)):
-                chain[i]()
-                if i >= 2 and i - 2 < len(other):
-                    other[i - 2]()
-        for d in range(1 if last else 2):
-            tt(S("ZB", d, W, 16), S("ZB", d, W, 16), B("HH", 0), A.subtract)
-        if last:
-            ts(B("KA", 0), S("ZB", 0, W, 16), 0.0, A.is_gt)
-            for s in range(16):
-                if s % 3 == 2:
-                    act(S("ZB", s, W, 16), B("KA", 0), F.Copy, -1.0, 2.0)
+            later = lists(H, t + 1)
+            if COSTS_LATE:
+                yield next(later)
+            act(B("ZB", H), B("HH", 0))
+            cw = T["CW%d" % H]
+            dmas("y", "cw%d%d" % (H, t), [((cw[64 * h:64 * h + 64:8, :], [("CW%d" % H, 0, W, 1, False)]), B("ZB", H)) for h in range(2)])
+            yield from later
+            return
+        act(B("SG", 0), B("HH", 0), F.Sign)
+        for hi in range(8):
+            mm(B(("VV", "UB")[hi // 4], hi % 4), B("SGW", hi), B("SG", 0), True, True)
+        ts(B("CI", 0, 16), B("CK", H, 16), NONE, A.add)
+        ts(B("CF", 0, 16), B("CK", H, 16), 0.0, A.is_equal, -8193.0, A.mult)
+        ts(B("CI", 1, 16), B("CI", 0, 16), 6, A.logical_shift_right)
+        yield FILL["mates"]
+        tt(B("CF", 1, 16), B("CI", 1, 16), B("CF", 0, 16), A.add)
+        mm(S("YB", 0, 128, 1, 0, 16), B("CF", 1, 16), B("IDf", 0), True, True)
+        for u in range(2):
+            x0 = 1024 * H
+            tt(S("YF", x0 + 512 * u, x0 + 512 * u + 512), S("FIN", x0 + 512 * u, x0 + 512 * u + 512), S(("VV", "UB")[u], 0, 512), A.mult)
+            dmas("y", ("oa%d", "ob%d")[u] % H, [(X(T.yf[r, c:c + b - a]), part("YF", h, x0 + a, x0 + b)) for h, a, b, c in pieces(H, 512 * u, 512 * u + 512)])
+        act(S("YC", 128 * H, 128 * H + 128, 1, 0, 16), S("YB", 0, 128, 1, 0, 16))
+        q = "s" if H else "y"
+        dmas(q, "oc%d" % H, [(X(T.yc[4 * H:4 * H + 4, :]), S("YC", 128 * H, 128 * H + 128, 1, 0, 16))])
+        dmas(q, "op%d" % H, [(X(T.yp[r, 8 - 8 * h:16 - 8 * h]), part("MFi", h, 8 * H, 8 * H + 8)) for h in range(2)])
+        dmas(q, "oz%d" % H, [(X(T.yz[r, :]), part("ZI", 0, 640 * H + 512, 640 * H + 640))])
+
+    def window(H, t, chain):
+        bank, win = "S%d" % H, "WIN%d" % H
+        cost, kind, func = (win, 1, F.Copy) if t == 0 else ("CW%d" % H, 2, F.Relu)
+        mm(S(bank, 0, 256), B("E0", 0), S("BI", 0, 256), True, False)
+        done, summed, left, waiting = {"FD": 0, "CD": 0}, {"FD": 0, "CD": 0}, [2 * len(LISTS)], []
+
+        def sums(data, k, i):
+            name, col, cols = LISTS[i]
+            pos, n = 16 * col, 16 * cols
+            left[0] -= 1
+            if name == "f1":
+                for a in range(2):
+                    mm(S(bank, 0, 256), S(data, pos + a, pos + n, 2), B("W1", 2 * k + a, 256), False, False)
+                return
+            for b in range(8):
+                if name == "c4":
+                    out, w = S(bank, b, 256, 8), B("W32", k, 32)
                 else:
-                    ts(S("ZB", s, W, 16), B("KA", 0), 2.0, A.mult, -1.0, A.add)
-        for h in range(16):
-            mm(B("A%d" % (h // 4), h % 4), B("ZB", h), B("IDb", 0), True, True)
-        if last:
-            mm(S("S2", 0, 128, 1, 0, 32), S("CK", 0, 32), B("IDf", 0), True, True)
-            act(S("YC", 0, 128, 1, 0, 32), S("S2", 0, 128, 1, 0, 32))
-            cp(S("YP", 0, 16), S("MR3", 0, 16))
-            dmas("s", "op", [(X(T.yp[:]), S("YP", 0, 16))])
-            dmas("s", "oz", [(X(T.yz[:]), S("HZ", W + 512, W + 640))])
-            dmas("s", "oc", [(X(T.yc[:, 128 * q:128 * q + 128]), S("YC", 0, 128, 1, 8 * q, 8 * q + 8)) for q in range(ROUNDS)])
-            for h in range(4):
-                tt(B("YF", h, 512), B("WIN", h, 512), S("A%d" % h, 0, 512), A.mult)
-                if h == 0:
-                    dmas("y", "oy0", [(X(T.yf[:, W - SHIFT:W]), S("YF", 0, SHIFT)), (X(T.yf[:, 0:512 - SHIFT]), S("YF", SHIFT, 512))])
+                    out, w = S(bank, 8 * int(name[1]) + b, 256, 32), S("W32", 32 * k, 32 * k + 32, 4)
+                mm(out, S(data, pos + b, pos + n, 8), w, False, left[0] == 0 and b == 7)
+            if name == "c4" and k == 0:
+                mm(S("NM", 0, 140), B("OWN", H), S("OWW", 0, 140), True, False)
+                mm(B("NM", 0), B("GG", H), B("NMW", 0), False, True)
+
+        def gather(data, n):
+            end = min(done[data] + n, 5376)
+            while done[data] < end:
+                e = done[data]
+                name, col, cols = [l for l in LISTS if 16 * l[1] <= e][-1]
+                e1 = min(end, 16 * (col + cols) if data == "FD" or col != F1 else 16 * (col + 80))
+                o = S("LST", 336 * H + e // 16, 336 * H + e1 // 16)
+                if data == "CD":
+                    act(S("CD", e, e1), G(S(cost, 0, W), o), func)
                 else:
-                    dmas("y", "oy%d" % h, [(X(T.yf[:, 512 * h - SHIFT:512 * h + 512 - SHIFT]), B("YF", h, 512))])
-        else:
-            for h in range(4):
-                act(B("CW", h, 512), S("A%d" % h, 0, 512), F.Relu)
-            lists_b(t + 1)
-            lists_c()
+                    step, z = 64 // cols, 1024 * H
+                    tt(S("FD", e, e1), G(S(win, 0, W), o), S("ZR", z + step * (e - 16 * col), z + step * (e1 - 16 * col), step), A.is_lt)
+                done[data] = e1
+                while summed[data] < len(LISTS) and 16 * (LISTS[summed[data]][1] + LISTS[summed[data]][2]) <= e1:
+                    waiting.append((data, 0 if data == "FD" else kind, summed[data]))
+                    summed[data] += 1
+
+        def flush():
+            while waiting:
+                sums(*waiting.pop(0))
+
+        for nv, ns, free in chain:
+            if free:
+                flush()
+            gather("CD", ns)
+            gather("FD", nv)
+        while min(done.values()) < 5376:
+            flush()
+            for data in sorted(done, key=done.get):
+                gather(data, min(16 * (col + cols) - done[data] for name, col, cols in LISTS if 16 * (col + cols) > done[data] or col == LISTS[-1][1]))
+        flush()
+
+    for pause, _ in enumerate(lists(0, 0)):
+        if pause == 0:
+            weights()
+    chain = late_constants()
+    for t in range(ROUNDS):
+        for H in range(2):
+            window(H, t, chain)
+            chain = tail(H, t)
+    for _ in chain:
+        pass
 
     for s in sorted(final):
         g.wait_ge(T.sem[s], final[s])

@@ -7,28 +7,32 @@ NONE = float(2 ** 19)
 M2, M16 = 1.5 * 2 ** 24, 1.5 * 2 ** 27
 OWN_ON_SCALAR = True
 MATES_ON_SCALAR = True
-COSTS_LATE = True
-NEEDS, FIRST_NEEDS = "ggggggss", "ssssvvvv"
-FILL = {"start": (512, 1920), "min": (256, 0), "index": (128, 512), "seed": (128, 0), "count": (128, 0), "hot": (0, 0), "product": (128, 0), "sum": (128, 0), "names": (128, 0),
-        "spread": (384, 512), "squares": (0, 128), "sent": (1920, 512), "mates": (384, 512), "copied": (256, 256), "places": (128, 256), "cast": (128, 0), "init": (768, 1024), "costs": (1024, 2304), "parts": (4096, 4096)}
-FIRST = {(0, 0): {"start": (768, 1536), "min": (0, 0), "index": (128, 256), "seed": (0, 0), "count": (0, 0), "product": (0, 0), "sum": (0, 0), "spread": (128, 256),
-                  "sent": (3072, 2176), "mates": (512, 256), "places": (0, 512)},
-         (1, -1): {"mates": (1024, 512)}}
+COSTS_LATE = False
+CAST = "ss"
+SQUARES, LAST_SQUARES = (0, 1), (0, 1)
+NEEDS, FIRST_NEEDS = "gggggsss", "ssssvvvv"
+FILL = {"start": (640, 1792), "min": (0, 256), "index": (0, 512), "seed": (0, 0), "count": (0, 0), "hot": (128, 0), "product": (128, 0), "sum": (128, 0), "names": (128, 0),
+        "spread": (256, 512), "far": (128, 0), "sent": (2176, 1152), "mates": (256, 640), "copied": (256, 0), "places": (128, 1024), "cast": (128, 0),
+        "init": (768, 1024), "costs": (1024, 2304)}
+FIRST = {(0, 0): {"start": (768, 1408), "min": (0, 0), "index": (128, 256), "seed": (0, 0), "count": (0, 0), "product": (0, 0), "sum": (0, 0), "spread": (0, 512),
+                  "hot": (0, 0), "sent": (3072, 2688), "mates": (512, 0), "copied": (256, 384), "places": (0, 512)},
+         (1, -1): {"mates": (1024, 512)}, (0, 3): {"count": (256, 128), "spread": (384, 512), "sent": (1792, 1024)}}
+REST = {"min": 2, "index": 1, "seed": 1, "count": 1, "init": 5}
 FREE = ("min", "count", "sent", "mates", "places", "cast", "costs", "parts")
 
 
 def fills(H, t):
-    return {k: v + (k in FREE,) for k, v in dict(FILL, **FIRST.get((H, t), {})).items()}
+    return {k: v + (k in FREE, REST.get(k, 0)) for k, v in dict(FILL, **FIRST.get((H, t), {})).items()}
 
 
 SPEC = {
-    "bfloat16": "WIN0 2560 WIN1 2560 CW0 2048 CW1 2048 FIN 2048 YF 2048 ZR 2048 FD 5376 CD 5376 OL 1536 SQ 384 SD 384 SR 384 OHH 384 ZB 256 SG 128 "
+    "bfloat16": "WIN0 2560 WIN1 2560 FIN 2048 YF 2048 ZR 2048 FD 5376 OL 768 SQ 768 SD 384 SR 384 SN 384 OHH 384 SG 64 "
                 "SEED 128 KEEP 128 CNT 128 OH 128 ZS 1024 ZI 1280 "
-                "IOT 128 I16 32 U8 8 N32 32 D16 128 ONE 128 IDb 128 E0 128 CA 128 CB 128 CC 128 CD1 128 CE 256 SEL 3584 NMW 128 OWW 140 W32 96 W1 1536 BI 256 LW 144 SGW 1024",
-    "float32": "MSC 256 PW 128 SC 128 CK 32 KF 8 NT 4 OFF 4 LHF 24 EE 128 EE2 64 UUS 80 T1 128 T2 256 T3 256 MK 16 MS 16 pF 8 cc 44 DRM 256 "
+                "IOT 128 N32 32 D16 128 ONE 128 IDb 128 E0 128 CA 128 CB 128 CC 128 CD1 128 CE 256 SEL 3584 NMW 128 OWW 140 W32 64 W1 1024 BI 256 LW 160 SGW 2048",
+    "float32": "CW0 2048 CW1 2048 ZF 128 MSC 256 PW 128 SC 128 CK 32 KF 8 NT 4 OFF 4 LHF 24 EE 128 EE2 64 UUS 80 T1 128 MK 16 MS 16 pF 8 cc 40 DRM 256 "
                "IDf 128 ONf 128 YC 256 CF 64 MFo 16 MFi 16 OWNW 1024",
     "int32": "NW0 1024 NW1 1024 PR 16 XI 336 XJ 336 MI 12 XC 12 LHI 28 CI 64 pI 8",
-    "float16": "GG 256 OWN 256",
+    "float16": "GG 256 OWN 256 CD 5376 ZH 128",
     "uint16": "NL 16 MSG 48 MR 48 OFFL 8 LST 672",
 }
 PSUM = ("S0", "S1", "NM", "VV", "UB", "LQ", "HH", "YB")
@@ -37,9 +41,10 @@ for _ty, _l in SPEC.items():
     _l = _l.split()
     for _n, _c in zip(_l[::2], _l[1::2]):
         SCRATCH[_n] = ("sbuf", [128, int(_c)], _ty)
-SEMAPHORES = ["qv", "qs", "qt", "qg", "df", "ls"] + [p + str(h) for p in ("dl", "dn", "dm", "dw", "dc", "oa", "ob", "oc", "op", "oz") for h in range(2)] + \
+SEMAPHORES = ["qv", "qs", "qt", "qg", "df", "ls"] + [p + str(h) for p in ("dl", "dn", "dm", "dw", "y0", "y1", "y2", "y3", "oc", "op", "oz") for h in range(2)] + \
     [p + str(h) + str(t) for p in ("rn", "rz", "cw") for h in range(2) for t in range(ROUNDS)]
 F1 = 192
+CUTS = (2048, 3072, 4352, 5376)
 LISTS = [("a0", 0, 64), ("a1", 64, 64), ("a2", 128, 64), ("f1", F1, 16), ("c4", 208, 64), ("a3", 272, 64)]
 
 
@@ -162,8 +167,8 @@ def rank_program(g, core, T, topo):
         else:
             emit("g", lambda: g.iota(out[0], pattern, base, cm, allow_small_or_imprecise_dtypes=True), [], out[1])
 
-    def pick(out, in_, pattern, base=0, cm=0):
-        emit("g", lambda: g.affine_select(out[0], in_[0], pattern, A.is_equal, 0.0, base, cm), in_[1], out[1])
+    def pick(out, in_, pattern, base=0, cm=0, op=A.is_equal):
+        emit("g", lambda: g.affine_select(out[0], in_[0], pattern, op, 0.0, base, cm), in_[1], out[1])
 
     def send(out, src, dst, frm, rsem):
         before("g", src[1], [])
@@ -199,8 +204,6 @@ def rank_program(g, core, T, topo):
     load_mates("y", 1)
     load_figures("y", 1)
     before("y", S("NW1", 0, 1024)[1], [])
-    for H in range(2):
-        dmas("y", "dc%d" % H, [(S("CW%d" % H, 0, W), X(T.fig[:]))])
     dmas("y", "df", [(part("FIN", h, 1024 * H + a, 1024 * H + b), X(T.fig[64 * H:64 * H + 64, c:c + b - a])) for H in range(2) for h, a, b, c in pieces(H, 0, 1024)])
 
     iota(S("pI", 0, 1), [[0, 1]], 0, 1)
@@ -218,8 +221,7 @@ def rank_program(g, core, T, topo):
     for q in range(4):
         iota(B("CE", q, 64), [[0, 2], [1, 4], [0, 8]], 4 * q)
     iota(B("D16", 0), [[1, 8], [0, 16]])
-    iota(S("U8", 0, 8), [[1, 4], [0, 2]])
-    iota(S("I16", 0, 32), [[0, 2], [1, 16]])
+    iota(S("CW0", 0, W), [[0, W]])
 
     def cc(i, n=1):
         return S("cc", i, i + n)
@@ -272,17 +274,20 @@ def rank_program(g, core, T, topo):
     def weights():
         ms(B("E0", 0), 1.0 / 128)
         ms(S("DRM", 0, 256), 0.0)
-        ms(pad[1], 0)
         ms(B("ONE", 0), 1.0)
-        ts(B("W32", 0, 32), S("N32", 0, 32), cc(22), A.is_equal, BIG, A.mult)
-        ts(B("W32", 1, 32), S("N32", 0, 32), cc(22), A.is_equal, 64.0, A.mult)
-        ms(S("DRM", 0, 256, 64), NONE)
-        ts(cc(25), pS, 8.0, A.is_equal, cc(18), A.add)
         ts(cc(26), cc(22), 2.0, A.mult)
         ts(cc(27), cc(22), 2.0, A.mult, 1.0, A.add)
         ts(cc(29), pS, 2.0, A.is_lt)
         ts(cc(30), pS, -1.0, A.mult, pA, A.add)
         ts(cc(31), pH, -4.0, A.mult, 4.0, A.add)
+        yield
+        yield
+        ms(pad[1], 0)
+        yield
+        ts(B("W32", 0, 32), S("N32", 0, 32), cc(22), A.is_equal, BIG, A.mult)
+        ts(B("W32", 1, 32), S("N32", 0, 32), cc(22), A.is_equal, 64.0, A.mult)
+        ms(S("DRM", 0, 256, 64), NONE)
+        yield
 
     def late_constants():
         FILL = fills(1, -1)
@@ -305,37 +310,29 @@ def rank_program(g, core, T, topo):
         yield from lists(1, 0)
         ts(S("MS", 0, 8), S("IOT", 0, 8), pM, A.is_equal, 0.5, A.mult)
         ts(S("MS", 8, 16), S("IOT", 0, 8), pM, A.is_equal)
-        ms(S("LW", 0, 144), 0.0)
-        ms(B("SEED", 0), -1.0)
-        ms(B("KEEP", 0), 1.0)
+        ms(S("LW", 0, 160), 0.0)
+        iota(B("SEED", 0), [[0, 128]], -1)
+        iota(S("SD", 0, 384), [[0, 384]], -1)
+        pick(B("KEEP", 0), B("ONE", 0), [[0, 8], [1, 16]], op=A.is_gt)
+        for q in range(3):
+            pick(B("SR", q), B("ONE", 0), [[0, 4], [1, 32]], op=A.is_gt)
         ts(cc(2), pH, 100.0, A.mult, pG, A.add)
         ts(cc(34), pH, 288.0, A.mult, -296.5, A.add)
-        ms(S("KEEP", 0, 128, 16), 0.0)
-        ts(S("LW", 16, 144, 16), S("U8", 0, 8), cc(2), A.is_equal)
-        ts(cc(35), pQ, -2.0, A.mult, 1.0, A.add)
-        ms(B("OH", 0), -7.5)
-        act(cc(40), pQ, F.Copy, 0.0, 7.5)
-        act(cc(41), pQ, F.Copy, -M16, 2 * M16)
+        act(cc(35), pH, F.Copy, -0.5, 0.0)
         act(cc(36, 4), I4, F.Identity, pP, 128.0)
-        act(B("W32", 2, 32), B("W32", 1, 32), F.Copy, 0.0, cc(25))
+        ts(S("LW", 32, 160, 32), I4, cc(2), A.is_equal)
         act(cc(36, 4), cc(36, 4), F.Copy, float(W))
-        for a in range(2):
-            act(B("W1", 4 + a, 256), B("W1", 2 + a, 256), F.Copy, 0.0, cc(25))
         act(B("ONf", 0), B("ONE", 0))
         pick(B("IDb", 0), B("ONE", 0), [[-1, 128]], 0, 1)
-        for H in range(2):
-            mm(B("YB", H), B("E0", 0), B("OH", 0), True, False)
-            for hi in range(16):
-                mm(B("YB", H), S("LW", 16 - hi, 144 - hi), B("WIN%d" % H, hi), False, hi == 15)
-        yield FILL["costs"]
-        act(S("T2", 0, 256), S("YB", 0, 256), F.Copy, M16, 1.0)
-        act(S("T3", 0, 256), S("YB", 0, 256), F.Identity, cc(40), pQ)
-        act(S("T2", 0, 256), S("T2", 0, 256), F.Identity, cc(41), cc(35))
-        yield FILL["parts"]
-        tt(S("ZB", 0, 256), S("T2", 0, 256), S("T3", 0, 256), A.add)
-        for hi in range(8):
-            pick(B("SGW", hi), B("ONE", 0), [[-8, 2], [-32, 4], [0, 16]], -hi, 1)
+        iota(S("CW1", 0, W), [[0, W]])
         pick(B("IDf", 0), B("ONf", 0), [[-1, 128]], 0, 1)
+        for H in range(2):
+            for hi in range(32):
+                mm(B("HH", H, 64), S("LW", 32 - hi, 160 - hi), B("WIN%d" % H, hi, 64), hi == 0, hi == 31)
+        yield FILL["costs"]
+        act(B("ZH", 0), B("HH", 0))
+
+    rest = []
 
     def lists(H, t):
         FILL = fills(H, t - 1)
@@ -373,37 +370,48 @@ def rank_program(g, core, T, topo):
         spread(B("VV", 4, 64), 2, "OWN", 2)
         spread(S("YB", 0, 16), 12, "OWN", 8)
         spread(S("YB", 16, 32), 20, "GG", 8)
-        if H + t == 0:
-            needs("v")
         yield FILL["mates"]
         act(S("UUS", 0, 64), S("UB", 0, 64), F.Copy, 17.0, 2.0)
         yield FILL["copied"]
-        act(S("UUS", 64, 80), S("YB", 0, 16), F.Copy, 17.0, 2.0)
-        for name, col, cols in LISTS:
+        def product(name, col, cols):
             if cols == 64:
                 tt(S("XI", col, col + 64), S("UUS", 0, 64), B("VV", int(name[1]), 64), A.mult)
+            else:
+                tt(S("XI", col, col + 16), S("UUS", 64, 80), S("YB", 16, 32), A.mult)
+
+        def places(a, b):
+            ts(S("XJ", a, b), S("XI", a, b), 5, A.logical_shift_right, 2047, A.bitwise_and)
+
+        def cast(a, b, by):
+            (act if by == "s" else cp)(S("LST", 336 * H + a, 336 * H + b), S("XJ", a, b))
+
+        for l in LISTS[:3]:
+            product(*l)
         needs("s")
-        tt(S("XI", F1, F1 + 16), S("UUS", 64, 80), S("YB", 16, 32), A.mult)
-        act(S("WIN%d" % H, W + 128 * t, W + 128 * t + 128), need, F.Copy, 0.0, 2.0)
+        act(S("UUS", 64, 80), S("YB", 0, 16), F.Copy, 17.0, 2.0)
         yield FILL["places"]
-        ts(S("XJ", 0, 336), S("XI", 0, 336), 5, A.logical_shift_right, 2047, A.bitwise_and)
-        if H + t:
-            needs("v")
+        places(0, F1)
+        needs("v")
         yield FILL["cast"]
-        cp(B("LST", H, 336), S("XJ", 0, 336))
+        cast(0, F1, CAST[0] if H + t else "v")
+        act(S("WIN%d" % H, W + 128 * t, W + 128 * t + 128), need, F.Copy, 0.0, 2.0)
+        rest.extend([lambda: product(*LISTS[4]), lambda: product(*LISTS[5]), lambda: product(*LISTS[3]), lambda: places(F1, 336), lambda: cast(F1, 336, CAST[1])])
 
     def tail(H, t):
         dst = T.cores[(rank + 1 + t % 3) % N]
         src = T.cores[(rank - 1 - t % 3) % N]
         last, FILL = t == ROUNDS - 1, fills(H, t)
         bank, win, r = "S%d" % H, "WIN%d" % H, slice(64 * H, 64 * H + 64)
+        for hi in range(4 * (2 * t + H), 4 * (2 * t + H) + 4):
+            if hi < 16:
+                pick(B("SGW", hi), B("ONE", 0), [[-16, 2], [-32, 4], [0, 16]], -hi, 1)
         yield FILL["start"]
         scan(S("MSC", 0, 256), S("DRM", 0, 256), S(bank, 0, 256), 0.0, A.max, A.min)
         yield FILL["min"]
         m, ck = S("MSC", 63, 256, 64), S("CK", 16 * H + t, 16 * H + 16, 4)
         taken = [S("CK", 16 * H + 4 * q + t, 16 * H + 4 * q + t + 1) for q in range(4)]
         cp(S("MI", 0, 4), m)
-        act(ck, m, F.Copy, -NONE)
+        act(ck, m, F.Copy, NONE, -1.0)
         yield FILL["index"]
         ts(S("MI", 4, 8), S("MI", 0, 4), 2 ** 19 + 15, A.bitwise_and)
         ts(S("MI", 8, 12), S("MI", 0, 4), 4, A.logical_shift_right, 2 ** 15 + 3, A.bitwise_and)
@@ -418,85 +426,102 @@ def rank_program(g, core, T, topo):
         yield FILL["product"]
         scan(B("SC", 0), B("KEEP", 0), B("PW", 0), 0.0, A.mult, A.add)
         yield FILL["sum"]
-        act(S("NT", 0, 4), ck, F.Relu, cc(36 + t))
+        act(S("NT", 0, 4), ck, F.Relu, cc(36 + t), -1.0)
         tt(S("KF", 0, 8), S("SC", 15, 128, 16), S("NM", 128, 136), A.add)
         yield FILL["names"]
-        for q in range(8):
-            act(B("EE", q, 16), S("MK", 0, 16), F.Copy, 0.0, S("KF", (q + 4) % 8, (q + 4) % 8 + 1))
-        mm(S("LQ", 0, 8), B("EE", 0), S("MS", 0, 8), True, True)
+        squares = (LAST_SQUARES if last else SQUARES)
+
+        def names():
+            for q in range(8):
+                act(B("EE", q, 16), S("MK", 0, 16), F.Copy, 0.0, S("KF", (q + 4) % 8, (q + 4) % 8 + 1))
+            mm(S("LQ", 0, 8), B("EE", 0), S("MS", 0, 8), True, True)
+
+        def send_names():
+            out, land = (B("MFo", H, 8), B("MFi", H, 8)) if last else (B("MSG", 3 * H + t, 8), B("MR", 3 * H + t, 8))
+            ts(out, S("LQ", 0, 8), cc(34), A.add)
+            send(land, out, dst, src, "rn%d%d" % (H, t))
+
+        def low(q):
+            for c in range(3):
+                col = S("LHF", 4 * c + q, 4 * c + q + 1)
+                if q in squares:
+                    act(B("SQ", 3 * q + c, 64), S("IOT", 0, 64), F.Square, col, -1.0)
+                else:
+                    ts(B("OL", 3 * q + c, 64), S("IOT", 0, 64), col, A.is_equal, taken[q], A.mult)
+
+        def hits(q):
+            if q in squares:
+                act(B("OL", q, 192), B("SQ", q, 192), F.Relu, taken[q], -2 * NONE)
+            costs = S("HH", 0, 64, 1, 32 * q, 32 * q + 32)
+            mm(costs, B("IDb", q, 32), B("ZH", H, 64), True, False)
+            for c in range(3):
+                mm(costs, B("OHH", 4 * c + q, 32), B("OL", 3 * q + c, 64), False, c == 2)
+
+        names()
         tt(S("XC", 8, 12), S("KF", 0, 4), S("KF", 4, 8), A.mult)
         tt(S("XC", 0, 8), S("KF", 0, 8), S("NM", 132, 140), A.mult)
         ts(S("LHI", 24, 28), S("XC", 8, 12), 5, A.logical_shift_right, 2047, A.bitwise_and)
-        ts(S("LHI", 12, 24), S("XC", 0, 12), 12, A.logical_shift_right, 15, A.bitwise_and)
+        ts(S("LHI", 0, 12), S("XC", 0, 12), 5, A.logical_shift_right, 63, A.bitwise_and)
         tt(S("OFF", 0, 4), S("LHI", 24, 28), S("NT", 0, 4), A.max)
-        ts(S("LHI", 0, 12), S("XC", 0, 12), 5, A.logical_shift_right, 127, A.bitwise_and)
+        ts(S("LHI", 12, 24), S("XC", 0, 12), 11, A.logical_shift_right, 31, A.bitwise_and)
+        cp(S("LHF", 0, 12), S("LHI", 0, 12))
         for q in range(4):
             act(B("EE2", q, 16), S("MK", 0, 16), F.Copy, 0.0, S("OFF", q, q + 1))
         for h in range(2):
             mm(part("UB", h, 64, 72), S("EE2", 0, 64), S("MS", 8, 16), True, True)
+        cp(S("SD", 0, 384, 32), S("LHI", 12, 24))
         yield FILL["spread"]
-        out, land = (B("MFo", H, 8), B("MFi", H, 8)) if last else (B("MSG", 3 * H + t, 8), B("MR", 3 * H + t, 8))
-        ts(out, S("LQ", 0, 8), cc(34), A.add)
-        send(land, out, dst, src, "rn%d%d" % (H, t))
-        cp(S("LHF", 0, 24), S("LHI", 0, 24))
+        send_names()
+        yield FILL["far"]
         cp(S("OFFL", 0, 8), S("UB", 64, 72))
         act(B("T1", 0), G(S(win, 0, W + 128 * t + 128), S("OFFL", 0, 8)), F.Copy, M2, 511.0 / 512)
-
-        def hot(q):
-            for c in range(3):
-                n = 4 * c + q
-                ts(B("OL", 3 * q + c), B("IOT", 0), S("LHF", n, n + 1), A.is_equal, taken[q], A.mult)
-                act(B("SQ", 3 * q + c, 32), S("I16", 0, 32), F.Square, S("LHF", 12 + n, 13 + n), -1.0)
-
-        def hits(half):
-            act(B("OHH", half, 192), B("SQ", half, 192), F.Relu, 1.0, -1.0)
-            for q in (2 * half, 2 * half + 1):
-                costs = S("HH", 0, 128, 1, 32 * q, 32 * q + 32)
-                mm(costs, B("IDb", q, 32), B("ZB", H), True, False)
-                for c in range(3):
-                    mm(costs, B("OHH", 3 * q + c, 32), B("OL", 3 * q + c), False, c == 2)
-
-        hot(0)
+        scan(S("SN", 0, 384), S("SR", 0, 384), S("SD", 0, 384), 0.0, A.mult, A.add)
+        for q in squares[:1]:
+            low(q)
         act(B("ZS", 4 * H + t), B("T1", 0), F.Copy, -M2 / 2, 0.5)
         send(B("ZI", 5 * H + t + 1), B("ZS", 4 * H + t), dst, src, "rz%d%d" % (H, t))
-        hot(1)
-        hot(2)
-        hits(0)
-        hot(3)
-        yield FILL["squares"]
-        hits(1)
+        low(3)
+        ts(S("OHH", 0, 384), S("SN", 0, 384), 0.0, A.is_equal, -1.0, A.mult)
+        for q in range(3):
+            if q not in squares[:1]:
+                low(q)
+        for q in sorted(range(4), key=lambda q: q in squares):
+            hits(q)
         yield FILL["sent"]
         if not last:
             later = lists(H, t + 1)
             if COSTS_LATE:
                 yield next(later)
-            act(B("ZB", H), B("HH", 0))
+            act(B("ZF", H, 64), B("HH", 0, 64), F.Relu)
+            act(B("ZH", H, 64), B("HH", 0, 64), F.Relu)
             cw = T["CW%d" % H]
-            dmas("y", "cw%d%d" % (H, t), [((cw[64 * h:64 * h + 64:8, :], [("CW%d" % H, 0, W, 1, False)]), B("ZB", H)) for h in range(2)])
+            dmas("y", "cw%d%d" % (H, t), [((cw[64 * h:64 * h + 64:16, :], [("CW%d" % H, 0, W, 1, False)]), B("ZF", H, 64)) for h in range(2)])
             yield from later
             return
-        act(B("SG", 0), B("HH", 0), F.Sign)
-        for hi in range(8):
-            mm(B(("VV", "UB")[hi // 4], hi % 4), B("SGW", hi), B("SG", 0), True, True)
-        ts(B("CI", 0, 16), B("CK", H, 16), NONE, A.add)
+        act(B("SG", 0, 64), B("HH", 0, 64), F.Sign, cc(35))
+        banks = ("VV", "UB", "S0", "YB") if H else ("VV", "UB")
+        n = 1024 // len(banks)
+        for hi in range(16):
+            mm(B(banks[64 * hi // n], hi % (n // 64), 64), B("SGW", hi), B("SG", 0, 64), True, True)
+        ts(B("CI", 0, 16), B("CK", H, 16), -1.0, A.mult, NONE, A.add)
         ts(B("CF", 0, 16), B("CK", H, 16), 0.0, A.is_equal, -8193.0, A.mult)
         ts(B("CI", 1, 16), B("CI", 0, 16), 6, A.logical_shift_right)
         yield FILL["mates"]
         tt(B("CF", 1, 16), B("CI", 1, 16), B("CF", 0, 16), A.add)
-        mm(S("YB", 0, 128, 1, 0, 16), B("CF", 1, 16), B("IDf", 0), True, True)
-        for u in range(2):
-            x0 = 1024 * H
-            tt(S("YF", x0 + 512 * u, x0 + 512 * u + 512), S("FIN", x0 + 512 * u, x0 + 512 * u + 512), S(("VV", "UB")[u], 0, 512), A.mult)
-            dmas("y", ("oa%d", "ob%d")[u] % H, [(X(T.yf[r, c:c + b - a]), part("YF", h, x0 + a, x0 + b)) for h, a, b, c in pieces(H, 512 * u, 512 * u + 512)])
-        act(S("YC", 128 * H, 128 * H + 128, 1, 0, 16), S("YB", 0, 128, 1, 0, 16))
+        mm(S("LQ", 0, 128, 1, 0, 16), B("CF", 1, 16), B("IDf", 0), True, True)
         q = "s" if H else "y"
-        dmas(q, "oc%d" % H, [(X(T.yc[4 * H:4 * H + 4, :]), S("YC", 128 * H, 128 * H + 128, 1, 0, 16))])
         dmas(q, "op%d" % H, [(X(T.yp[r, 8 - 8 * h:16 - 8 * h]), part("MFi", h, 8 * H, 8 * H + 8)) for h in range(2)])
+        act(S("YC", 128 * H, 128 * H + 128, 1, 0, 16), S("LQ", 0, 128, 1, 0, 16))
+        dmas(q, "oc%d" % H, [(X(T.yc[4 * H:4 * H + 4, :]), S("YC", 128 * H, 128 * H + 128, 1, 0, 16))])
         dmas(q, "oz%d" % H, [(X(T.yz[r, :]), part("ZI", 0, 640 * H + 512, 640 * H + 640))])
+        for u, name in enumerate(banks):
+            x0 = 1024 * H
+            tt(S("YF", x0 + n * u, x0 + n * u + n), S("FIN", x0 + n * u, x0 + n * u + n), S(name, 0, n), A.mult)
+            dmas("y", "y%d%d" % (u, H), [(X(T.yf[r, c:c + b - a]), part("YF", h, x0 + a, x0 + b)) for h, a, b, c in pieces(H, n * u, n * u + n)])
 
     def window(H, t, chain):
         bank, win = "S%d" % H, "WIN%d" % H
-        cost, kind, func = (win, 1, F.Copy) if t == 0 else ("CW%d" % H, 2, F.Relu)
+        cost, kind, func = (win if t == 0 else "CW%d" % H), 1, F.Copy
         mm(S(bank, 0, 256), B("E0", 0), S("BI", 0, 256), True, False)
         done, summed, left, waiting = {"FD": 0, "CD": 0}, {"FD": 0, "CD": 0}, [2 * len(LISTS)], []
 
@@ -523,7 +548,9 @@ def rank_program(g, core, T, topo):
             while done[data] < end:
                 e = done[data]
                 name, col, cols = [l for l in LISTS if 16 * l[1] <= e][-1]
-                e1 = min(end, 16 * (col + cols) if data == "FD" or col != F1 else 16 * (col + 80))
+                e1 = min(end, 16 * (col + cols) if data == "FD" else min(x for x in CUTS if x > e))
+                while e1 > 16 * F1 and mine:
+                    mine.pop(0)()
                 o = S("LST", 336 * H + e // 16, 336 * H + e1 // 16)
                 if data == "CD":
                     act(S("CD", e, e1), G(S(cost, 0, W), o), func)
@@ -539,9 +566,13 @@ def rank_program(g, core, T, topo):
             while waiting:
                 sums(*waiting.pop(0))
 
-        for nv, ns, free in chain:
+        mine = rest[:]
+        del rest[:]
+        for nv, ns, free, steps in chain:
             if free:
                 flush()
+            for _ in range(min(steps, len(mine))):
+                mine.pop(0)()
             gather("CD", ns)
             gather("FD", nv)
         while min(done.values()) < 5376:
@@ -550,9 +581,9 @@ def rank_program(g, core, T, topo):
                 gather(data, min(16 * (col + cols) - done[data] for name, col, cols in LISTS if 16 * (col + cols) > done[data] or col == LISTS[-1][1]))
         flush()
 
-    for pause, _ in enumerate(lists(0, 0)):
-        if pause == 0:
-            weights()
+    early = weights()
+    for _ in lists(0, 0):
+        next(early)
     chain = late_constants()
     for t in range(ROUNDS):
         for H in range(2):

@@ -2,23 +2,23 @@ from concourse.mybir import AluOpType as A, ActivationFunctionType as F
 
 N, W, ROUNDS = 8, 2048, 4
 SHIFT = 315
-BIG = float(2 ** 20)
-NONE = float(2 ** 19)
-M2, M16 = 1.5 * 2 ** 24, 1.5 * 2 ** 27
-OWN_ON_SCALAR = True
-MATES_ON_SCALAR = True
-COSTS_LATE = False
-CAST = "ss"
-SQUARES, LAST_SQUARES = (0, 1), (0, 1)
-NEEDS, FIRST_NEEDS = "gggggsss", "ssssvvvv"
-FILL = {"start": (640, 1792), "min": (0, 256), "index": (0, 512), "seed": (0, 0), "count": (0, 0), "hot": (128, 0), "product": (128, 0), "sum": (128, 0), "names": (128, 0),
-        "spread": (256, 512), "far": (128, 0), "sent": (2176, 1152), "mates": (256, 640), "copied": (256, 0), "places": (128, 1024), "cast": (128, 0),
-        "init": (768, 1024), "costs": (1024, 2304)}
-FIRST = {(0, 0): {"start": (768, 1408), "min": (0, 0), "index": (128, 256), "seed": (0, 0), "count": (0, 0), "product": (0, 0), "sum": (0, 0), "spread": (0, 512),
-                  "hot": (0, 0), "sent": (3072, 2688), "mates": (512, 0), "copied": (256, 384), "places": (0, 512)},
-         (1, -1): {"mates": (1024, 512)}, (0, 3): {"count": (256, 128), "spread": (384, 512), "sent": (1792, 1024)}}
-REST = {"min": 2, "index": 1, "seed": 1, "count": 1, "init": 5}
-FREE = ("min", "count", "sent", "mates", "places", "cast", "costs", "parts")
+BIG = float(2 ** 22)
+NONE = float(2 ** 21 + 32 * 4 + 16)
+M2 = 1.5 * 2 ** 24
+LAST_BANKS = ("VV", "UB", "S0", "YB")
+FUSE = False
+CAST = "sg"
+SQUARES, LAST_SQUARES = (0,), (0, 1)
+NEEDS, FIRST_NEEDS = "gggggsss", {(0, 0): "ssssvvvv", (0, 1): "ggssvvvv"}
+FILL = {"start": (640, 1408), "min": (0, 640), "count": (0, 0), "hot": (0, 0), "product": (128, 0), "sum": (128, 0), "names": (128, 0),
+        "spread": (320, 640), "far": (256, 0), "sent": (2752, 1088), "out": (0, 0), "mates": (0, 896), "copied": (0, 0), "places": (128, 1280), "cast": (0, 0),
+        "init": (768, 1024), "costs": (1280, 2304)}
+FIRST = {(0, 0): {"start": (768, 1408), "min": (0, 0), "product": (0, 0), "sum": (0, 0), "spread": (128, 512), "far": (128, 128), "sent": (2944, 768), "out": (128, 1920),
+                  "mates": (128, 0), "copied": (256, 896), "places": (256, 512)},
+         (1, -1): {"init": (768, 1280), "mates": (1024, 512), "copied": (256, 256), "places": (128, 896)},
+         (0, 3): {"sum": (256, 0), "spread": (640, 512), "sent": (2304, 896), "mates": (128, 1408), "cast": (0, 1024)}}
+REST = {"min": 2, "count": 1, "hot": 1, "product": 1, "init": 5}
+FREE = ("min", "count", "sent", "mates", "places", "cast", "costs")
 
 
 def fills(H, t):
@@ -26,14 +26,14 @@ def fills(H, t):
 
 
 SPEC = {
-    "bfloat16": "WIN0 2560 WIN1 2560 FIN 2048 YF 2048 ZR 2048 FD 5376 OL 768 SQ 768 SD 384 SR 384 SN 384 OHH 384 SG 64 "
-                "SEED 128 KEEP 128 CNT 128 OH 128 ZS 1024 ZI 1280 "
-                "IOT 128 N32 32 D16 128 ONE 128 IDb 128 E0 128 CA 128 CB 128 CC 128 CD1 128 CE 256 SEL 3584 NMW 128 OWW 140 W32 64 W1 1024 BI 256 LW 160 SGW 2048",
-    "float32": "CW0 2048 CW1 2048 ZF 128 MSC 256 PW 128 SC 128 CK 32 KF 8 NT 4 OFF 4 LHF 24 EE 128 EE2 64 UUS 80 T1 128 MK 16 MS 16 pF 8 cc 40 DRM 256 "
-               "IDf 128 ONf 128 YC 256 CF 64 MFo 16 MFi 16 OWNW 1024",
-    "int32": "NW0 1024 NW1 1024 PR 16 XI 336 XJ 336 MI 12 XC 12 LHI 28 CI 64 pI 8",
+    "bfloat16": "WIN0 2560 WIN1 2560 FIN 2048 YF 2048 ZR 2048 FD 5376 OL 768 SQ 768 SD 768 SR 384 SN 384 OHH 384 SG 64 TK 4 "
+                "SEED 136 KEEP 136 CNT 136 OH 136 ZS 1024 ZI 1280 "
+                "IOT 136 N32 32 C17 68 ONE 136 IDb 128 E0 128 CA 128 CB 128 CC 128 CD1 128 CE 256 SEL 3584 NMW 136 OWW 144 W32 64 W1 1024 BI 256 LW 160 SGW 2048",
+    "float32": "CW0 2048 CW1 2048 ZF 128 PW 136 SC 136 NT 4 OFF 4 EE 128 EE2 64 UUS 80 T1 128 MK 16 MS 16 pF 8 cc 40 DRM 256 "
+               "IDf 128 ONf 128 YC 256 CF 64 MFo 16 MFi 16 OWNW 1064",
+    "int32": "NW0 1064 NW1 1064 PR 16 XI 336 XJ 336 MSI 2048 SEEDI 136 XC 12 LHI 28 CI 64 pI 8",
     "float16": "GG 256 OWN 256 CD 5376 ZH 128",
-    "uint16": "NL 16 MSG 48 MR 48 OFFL 8 LST 672",
+    "uint16": "NL 16 MSG 128 MR 48 LST 672",
 }
 PSUM = ("S0", "S1", "NM", "VV", "UB", "LQ", "HH", "YB")
 SCRATCH = {n: ("psum", [128, 512], "float32") for n in PSUM}
@@ -41,7 +41,7 @@ for _ty, _l in SPEC.items():
     _l = _l.split()
     for _n, _c in zip(_l[::2], _l[1::2]):
         SCRATCH[_n] = ("sbuf", [128, int(_c)], _ty)
-SEMAPHORES = ["qv", "qs", "qt", "qg", "df", "ls"] + [p + str(h) for p in ("dl", "dn", "dm", "dw", "y0", "y1", "y2", "y3", "oc", "op", "oz") for h in range(2)] + \
+SEMAPHORES = ["qv", "qs", "qt", "qg", "df", "dc", "ls"] + [p + str(h) for p in ("dl", "dn", "dm", "dw", "y0", "y1", "y2", "y3", "oc", "op", "oz") for h in range(2)] + \
     [p + str(h) + str(t) for p in ("rn", "rz", "cw") for h in range(2) for t in range(ROUNDS)]
 F1 = 192
 CUTS = (2048, 3072, 4352, 5376)
@@ -185,7 +185,7 @@ def rank_program(g, core, T, topo):
         return S(name, a, b, 1, 64 * h, 64 * h + 64)
 
     def load_mates(q, H):
-        dmas(q, "dm%d" % H, [(part("NW%d" % H, 0, 0, 768), X(rows(T.cmate, H))), (part("NW%d" % H, 1, 0, 1024), X(rows(T.rmate, H)))])
+        dmas(q, "dm%d" % H, [(part("NW%d" % H, 0, 296, 1064), X(rows(T.cmate, H))), (part("NW%d" % H, 1, 8, 1032), X(rows(T.rmate, H)))])
 
     def load_figures(q, H):
         r = slice(64 * H, 64 * H + 64)
@@ -207,20 +207,21 @@ def rank_program(g, core, T, topo):
     dmas("y", "df", [(part("FIN", h, 1024 * H + a, 1024 * H + b), X(T.fig[64 * H:64 * H + 64, c:c + b - a])) for H in range(2) for h, a, b, c in pieces(H, 0, 1024)])
 
     iota(S("pI", 0, 1), [[0, 1]], 0, 1)
-    iota(B("IOT", 0), [[1, 128]])
+    iota(S("IOT", 0, 136), [[1, 136]])
     for h in range(2):
         iota(B("CA", h, 64), [[16, 4], [64, 2], [1, 8]], 8 * h)
         iota(B("CB", h, 64), [[1, 4], [4, 2], [0, 8]])
-    iota(S("OWNW", 0, 256), [[1, 256]])
+    iota(S("OWNW", 0, 266), [[1, 266]])
     for h in range(2):
         iota(B("CC", h, 64), [[1, 4], [4, 8], [0, 2]])
         iota(B("CD1", h, 64), [[1, 4], [4, 8], [32, 2]], 64 * h)
     iota(S("N32", 0, 32), [[1, 8], [0, 4]])
     for q in range(4):
-        iota(B("BI", q, 64), [[8, 2], [16, 4], [1, 8]])
+        iota(B("BI", q, 64), [[8, 2], [32, 4], [1, 8]])
     for q in range(4):
         iota(B("CE", q, 64), [[0, 2], [1, 4], [0, 8]], 4 * q)
-    iota(B("D16", 0), [[1, 8], [0, 16]])
+    iota(S("SEED", 0, 68), [[0, 68]], 17)
+    pick(S("C17", 0, 68), S("SEED", 0, 68), [[0, 4], [-1, 17]], 16, 0, A.is_gt)
     iota(S("CW0", 0, W), [[0, W]])
 
     def cc(i, n=1):
@@ -228,13 +229,17 @@ def rank_program(g, core, T, topo):
 
     pP, pH, pG, pS, pA, pM, pQ, pT = [S("pF", i, i + 1) for i in range(8)]
     I4 = S("IOT", 0, 4)
-    pad = [(part("NW%d" % H, 0, 768, 1024)[0], [("pad", H, H + 1, 1, True)]) for H in range(2)]
-    ms(pad[0], 0)
+    def pad(H):
+        for n, (h, a, b) in enumerate([(0, 0, 296), (1, 0, 8), (1, 1032, 1064)]):
+            ms((part("NW%d" % H, h, a, b)[0], [("pad", 3 * H + n, 3 * H + n + 1, 1, True)]), 0)
+
+    pad(0)
     for i, (sh, mask) in enumerate([(6, 1), (4, 3), (0, 15), (0, 3), (4, 7), (4, 1), (2, 3)]):
         ts(S("pI", i + 1, i + 2), S("pI", 0, 1), sh, A.logical_shift_right, mask, A.bitwise_and)
     cp(S("pF", 0, 8), S("pI", 0, 8))
     for q in range(1, 4):
-        act(B("OWNW", q, 256), B("OWNW", 0, 256), F.Copy, 256.0 * q)
+        act(B("OWNW", q, 266), B("OWNW", 0, 266), F.Copy, 266.0 * q)
+    ts(cc(34), pH, 288.0, A.mult, -296.5, A.add)
     ts(cc(0), pH, 1000.0, A.mult, pP, A.add)
     ts(cc(1), pH, -100.0, A.mult, 100.0, A.add)
     ts(cc(2), pS, 2.0, A.is_ge, 100.0, A.mult)
@@ -245,7 +250,7 @@ def rank_program(g, core, T, topo):
     ts(cc(17), pH, 593.0, A.mult)
     ts(cc(18), pS, 0.0, A.is_equal)
     ts(cc(19), pS, 1.0, A.is_equal)
-    ts(cc(20), pH, -584.5, A.mult, 593.0, A.add)
+    ts(cc(20), pH, -0.5, A.mult, 1.0, A.add)
     ts(cc(21), pH, -1.0, A.mult, 2.0, A.add)
     tt(cc(1), cc(1), pG, A.add)
     tt(cc(3), cc(3), cc(2), A.add)
@@ -269,62 +274,60 @@ def rank_program(g, core, T, topo):
         ts(B("SEL", 12 + c), B("CC", 0), 4.0 * c, A.subtract, cc(23), A.is_equal)
         ts(B("SEL", 20 + c), B("CD1", 0), 4.0 * c, A.subtract, cc(24), A.is_equal)
         if c == 3:
-            cp(B("NL", 0, 8), B("PR", 0, 8))
+            ts(B("NL", 0, 8), B("PR", 0, 8), cc(34), A.subtract, -0.5, A.add)
 
     def weights():
         ms(B("E0", 0), 1.0 / 128)
         ms(S("DRM", 0, 256), 0.0)
-        ms(B("ONE", 0), 1.0)
+        ms(S("ONE", 0, 136), 1.0)
         ts(cc(26), cc(22), 2.0, A.mult)
         ts(cc(27), cc(22), 2.0, A.mult, 1.0, A.add)
         ts(cc(29), pS, 2.0, A.is_lt)
         ts(cc(30), pS, -1.0, A.mult, pA, A.add)
-        ts(cc(31), pH, -4.0, A.mult, 4.0, A.add)
+        ts(cc(31), pH, 4.0, A.mult, pG, A.add)
+        ts(cc(32), pH, -56.0, A.mult, 72.0, A.add)
+        ts(cc(33), pG, 17.0, A.mult, pS, A.add)
         yield
         yield
-        ms(pad[1], 0)
+        pad(1)
         yield
         ts(B("W32", 0, 32), S("N32", 0, 32), cc(22), A.is_equal, BIG, A.mult)
-        ts(B("W32", 1, 32), S("N32", 0, 32), cc(22), A.is_equal, 64.0, A.mult)
+        ts(B("W32", 1, 32), S("N32", 0, 32), cc(22), A.is_equal, 256.0, A.mult)
         ms(S("DRM", 0, 256, 64), NONE)
         yield
 
     def late_constants():
         FILL = fills(1, -1)
-        yield FILL["init"]
-        cp(B("NL", 1, 8), B("PR", 1, 8))
         for a in range(2):
             ts(B("W1", a, 256), S("CE", 0, 256), cc(26 + a), A.is_equal, BIG, A.mult)
-            act(B("W1", 2 + a, 256), B("W1", a, 256), F.Copy, 0.0, 64.0 / BIG)
-        ts(cc(30), cc(30), pH, A.mult, pP, A.add)
-        tt(cc(31), cc(31), pG, A.add)
-        ts(cc(32), cc(18), pH, A.mult, -2.0, A.mult)
-        ts(cc(33), cc(16), cc(29), A.mult)
+            act(B("W1", 2 + a, 256), B("W1", a, 256), F.Copy, 0.0, 256.0 / BIG)
+        act(cc(35), pH, F.Copy, -0.5, 0.0)
+        act(cc(36, 4), I4, F.Identity, pP, 128.0)
+        act(B("ONf", 0), B("ONE", 0))
+        act(cc(36, 4), cc(36, 4), F.Copy, float(W))
+        ts(cc(30), cc(30), 68.0, A.add, pH, A.mult)
+        ts(cc(32), pG, 17.0, A.mult, cc(32), A.add)
         ts(cc(17), pH, 1.0, A.add, cc(29), A.mult)
+        tt(cc(30), cc(30), cc(33), A.add)
+        yield FILL["init"]
+        ts(B("NL", 1, 8), B("PR", 1, 8), cc(34), A.subtract, -0.5, A.add)
         ts(S("MK", 0, 16), S("IOT", 0, 16), pS, A.is_equal)
-        tt(cc(32), cc(32), cc(33), A.subtract)
-        ts(B("NMW", 0), B("IOT", 0), cc(30), A.is_equal, cc(21), A.mult)
-        ts(S("OWW", 128, 136), S("IOT", 0, 8), cc(31), A.is_equal, cc(17), A.mult)
-        ts(S("OWW", 136, 140), I4, cc(31), A.is_equal, cc(17), A.mult)
-        ts(B("OWW", 0), B("D16", 0), cc(31), A.is_equal, cc(32), A.mult)
+        ts(S("OWW", 136, 144), S("IOT", 0, 8), cc(31), A.is_equal, cc(17), A.mult)
+        ts(S("OWW", 0, 136), S("IOT", 0, 136), cc(32), A.is_equal, cc(17), A.mult)
+        ts(S("NMW", 0, 136), S("IOT", 0, 136), cc(30), A.is_equal, cc(21), A.mult)
         yield from lists(1, 0)
         ts(S("MS", 0, 8), S("IOT", 0, 8), pM, A.is_equal, 0.5, A.mult)
         ts(S("MS", 8, 16), S("IOT", 0, 8), pM, A.is_equal)
         ms(S("LW", 0, 160), 0.0)
-        iota(B("SEED", 0), [[0, 128]], -1)
-        iota(S("SD", 0, 384), [[0, 384]], -1)
-        pick(B("KEEP", 0), B("ONE", 0), [[0, 8], [1, 16]], op=A.is_gt)
+        iota(S("SEEDI", 0, 136), [[0, 136]], -1)
+        iota(S("SD", 384, 768), [[0, 384]], -1)
+        pick(S("KEEP", 0, 136), S("ONE", 0, 136), [[0, 8], [1, 17]], op=A.is_gt)
         for q in range(3):
             pick(B("SR", q), B("ONE", 0), [[0, 4], [1, 32]], op=A.is_gt)
         ts(cc(2), pH, 100.0, A.mult, pG, A.add)
-        ts(cc(34), pH, 288.0, A.mult, -296.5, A.add)
-        act(cc(35), pH, F.Copy, -0.5, 0.0)
-        act(cc(36, 4), I4, F.Identity, pP, 128.0)
         ts(S("LW", 32, 160, 32), I4, cc(2), A.is_equal)
-        act(cc(36, 4), cc(36, 4), F.Copy, float(W))
-        act(B("ONf", 0), B("ONE", 0))
         pick(B("IDb", 0), B("ONE", 0), [[-1, 128]], 0, 1)
-        iota(S("CW1", 0, W), [[0, W]])
+        dmas("y", "dc", [(S("CW1", 0, W), S("CW0", 0, W))])
         pick(B("IDf", 0), B("ONf", 0), [[-1, 128]], 0, 1)
         for H in range(2):
             for hi in range(32):
@@ -338,23 +341,17 @@ def rank_program(g, core, T, topo):
         FILL = fills(H, t - 1)
         nl = B("NL", H, 8) if t == 0 else B("MR", 3 * H + t - 1, 8)
         gg, own, need = B("GG", H), B("OWN", H), B("ZI", 5 * H + t)
-        mates = S("NW%d" % H, 0, 1024)
-        mates = (mates[0], mates[1] + pad[H][1])
-        if MATES_ON_SCALAR:
-            act(gg, G(mates, nl), F.Identity, cc(12 + (t + 1) % 4), cc(8 + t))
-        else:
-            ts(gg, G(mates, nl), cc(8 + t), A.mult, cc(12 + (t + 1) % 4), A.add)
-        if OWN_ON_SCALAR:
-            act(own, G(S("OWNW", 0, 1024), nl), F.Identity, cc(20), cc(28))
-        else:
-            ts(own, G(S("OWNW", 0, 1024), nl), cc(28), A.mult, cc(20), A.add)
+        mates = S("NW%d" % H, 0, 1064)
+        mates = (mates[0], mates[1] + [("pad", 3 * H, 3 * H + 3, 1, True)])
+        act(gg, G(mates, nl), F.Identity, cc(12 + (t + 1) % 4), cc(8 + t))
+        act(own, G(S("OWNW", 0, 1064), nl), F.Identity, cc(20), cc(28))
 
         def spread(out, sel, name, n):
             for c in range(n):
                 mm(out, B("SEL", sel + c), S(name, 128 * H + c, 128 * H + 128, n), c == 0, c == n - 1)
 
         def needs(who):
-            for b, by in enumerate(NEEDS if H + t else FIRST_NEEDS):
+            for b, by in enumerate(FIRST_NEEDS.get((H, t), NEEDS)):
                 o = S("ZR", 1024 * H + b, 1024 * H + 1024, 8)
                 if by == who == "s":
                     act(o, need)
@@ -380,106 +377,115 @@ def rank_program(g, core, T, topo):
                 tt(S("XI", col, col + 16), S("UUS", 64, 80), S("YB", 16, 32), A.mult)
 
         def places(a, b):
-            ts(S("XJ", a, b), S("XI", a, b), 5, A.logical_shift_right, 2047, A.bitwise_and)
+            ts(S("LST", 336 * H + a, 336 * H + b) if FUSE else S("XJ", a, b), S("XI", a, b), 5, A.logical_shift_right, 2047, A.bitwise_and)
 
         def cast(a, b, by):
-            (act if by == "s" else cp)(S("LST", 336 * H + a, 336 * H + b), S("XJ", a, b))
+            if FUSE:
+                return
+            if by == "g":
+                pick(S("LST", 336 * H + a, 336 * H + b), S("XJ", a, b), [[0, b - a]])
+            else:
+                (act if by == "s" else cp)(S("LST", 336 * H + a, 336 * H + b), S("XJ", a, b))
 
         for l in LISTS[:3]:
             product(*l)
         needs("s")
-        act(S("UUS", 64, 80), S("YB", 0, 16), F.Copy, 17.0, 2.0)
+        act(S("UUS", 64, 80), S("YB", 0, 16), F.Copy, 1.0, 2.0)
         yield FILL["places"]
         places(0, F1)
         needs("v")
         yield FILL["cast"]
         cast(0, F1, CAST[0] if H + t else "v")
         act(S("WIN%d" % H, W + 128 * t, W + 128 * t + 128), need, F.Copy, 0.0, 2.0)
-        rest.extend([lambda: product(*LISTS[4]), lambda: product(*LISTS[5]), lambda: product(*LISTS[3]), lambda: places(F1, 336), lambda: cast(F1, 336, CAST[1])])
+        rest.extend([lambda: product(*LISTS[4]), lambda: product(*LISTS[5]), lambda: product(*LISTS[3]), lambda: places(F1, 336), lambda: cast(F1, 336, CAST[1] if H + t else "s")])
 
     def tail(H, t):
         dst = T.cores[(rank + 1 + t % 3) % N]
         src = T.cores[(rank - 1 - t % 3) % N]
         last, FILL = t == ROUNDS - 1, fills(H, t)
         bank, win, r = "S%d" % H, "WIN%d" % H, slice(64 * H, 64 * H + 64)
-        for hi in range(4 * (2 * t + H), 4 * (2 * t + H) + 4):
-            if hi < 16:
-                pick(B("SGW", hi), B("ONE", 0), [[-16, 2], [-32, 4], [0, 16]], -hi, 1)
         yield FILL["start"]
-        scan(S("MSC", 0, 256), S("DRM", 0, 256), S(bank, 0, 256), 0.0, A.max, A.min)
+        scan(S("MSI", 1024 * H + t, 1024 * H + 1024, 4), S("DRM", 0, 256), S(bank, 0, 256), 0.0, A.max, A.min)
         yield FILL["min"]
-        m, ck = S("MSC", 63, 256, 64), S("CK", 16 * H + t, 16 * H + 16, 4)
-        taken = [S("CK", 16 * H + 4 * q + t, 16 * H + 4 * q + t + 1) for q in range(4)]
-        cp(S("MI", 0, 4), m)
-        act(ck, m, F.Copy, NONE, -1.0)
-        yield FILL["index"]
-        ts(S("MI", 4, 8), S("MI", 0, 4), 2 ** 19 + 15, A.bitwise_and)
-        ts(S("MI", 8, 12), S("MI", 0, 4), 4, A.logical_shift_right, 2 ** 15 + 3, A.bitwise_and)
-        yield FILL["seed"]
-        cp(S("SEED", 0, 128, 16), S("MI", 4, 12))
+        m = S("MSI", 1024 * H + 252 + t, 1024 * H + 1024, 256)
+        act(S("TK", 0, 4), m, F.Copy, NONE, -1.0)
+        ts(S("SEEDI", 0, 68, 17), m, 31, A.bitwise_and)
+        ts(S("SEEDI", 68, 136, 17), m, 5, A.logical_shift_right, 7, A.bitwise_and)
         yield FILL["count"]
-        scan(B("CNT", 0), B("KEEP", 0), B("SEED", 0), 0.0, A.mult, A.add)
+        scan(B("CNT", 0, 136), B("KEEP", 0, 136), B("SEEDI", 0, 136), 0.0, A.mult, A.add)
         yield FILL["hot"]
-        ts(B("OH", 0), B("CNT", 0), 0.0, A.is_equal)
+        ts(B("OH", 0, 136), B("CNT", 0, 136), 0.0, A.is_equal)
         yield FILL["product"]
-        tt(B("PW", 0), B("OH", 0), B("NM", 0), A.mult)
-        yield FILL["product"]
-        scan(B("SC", 0), B("KEEP", 0), B("PW", 0), 0.0, A.mult, A.add)
+        tt(B("PW", 0, 136), B("OH", 0, 136), B("NM", 0, 136), A.mult)
         yield FILL["sum"]
-        act(S("NT", 0, 4), ck, F.Relu, cc(36 + t), -1.0)
-        tt(S("KF", 0, 8), S("SC", 15, 128, 16), S("NM", 128, 136), A.add)
+        scan(B("SC", 0, 136), B("KEEP", 0, 136), B("PW", 0, 136), 0.0, A.mult, A.add)
         yield FILL["names"]
         squares = (LAST_SQUARES if last else SQUARES)
 
+        def new(a, b):
+            return S("SC", 17 * a + 16, 17 * b, 17)
+
         def names():
             for q in range(8):
-                act(B("EE", q, 16), S("MK", 0, 16), F.Copy, 0.0, S("KF", (q + 4) % 8, (q + 4) % 8 + 1))
+                act(B("EE", q, 16), S("MK", 0, 16), F.Copy, 0.0, S("SC", 17 * ((q + 4) % 8) + 16, 17 * ((q + 4) % 8) + 17))
+                if q == 0:
+                    act(S("NT", 0, 4), S("TK", 0, 4), F.Relu, cc(36 + t), -1.0)
             mm(S("LQ", 0, 8), B("EE", 0), S("MS", 0, 8), True, True)
-
-        def send_names():
-            out, land = (B("MFo", H, 8), B("MFi", H, 8)) if last else (B("MSG", 3 * H + t, 8), B("MR", 3 * H + t, 8))
-            ts(out, S("LQ", 0, 8), cc(34), A.add)
-            send(land, out, dst, src, "rn%d%d" % (H, t))
 
         def low(q):
             for c in range(3):
-                col = S("LHF", 4 * c + q, 4 * c + q + 1)
+                col = S("SD", 32 * (4 * c + q), 32 * (4 * c + q) + 1)
                 if q in squares:
                     act(B("SQ", 3 * q + c, 64), S("IOT", 0, 64), F.Square, col, -1.0)
                 else:
-                    ts(B("OL", 3 * q + c, 64), S("IOT", 0, 64), col, A.is_equal, taken[q], A.mult)
+                    ts(B("OL", 3 * q + c, 64), S("IOT", 0, 64), col, A.is_equal, S("TK", q, q + 1), A.mult)
 
         def hits(q):
             if q in squares:
-                act(B("OL", q, 192), B("SQ", q, 192), F.Relu, taken[q], -2 * NONE)
+                act(B("OL", q, 192), B("SQ", q, 192), F.Relu, S("TK", q, q + 1), -2 * NONE)
             costs = S("HH", 0, 64, 1, 32 * q, 32 * q + 32)
             mm(costs, B("IDb", q, 32), B("ZH", H, 64), True, False)
             for c in range(3):
                 mm(costs, B("OHH", 4 * c + q, 32), B("OL", 3 * q + c, 64), False, c == 2)
 
         names()
-        tt(S("XC", 8, 12), S("KF", 0, 4), S("KF", 4, 8), A.mult)
-        tt(S("XC", 0, 8), S("KF", 0, 8), S("NM", 132, 140), A.mult)
+        tt(S("XC", 8, 12), new(0, 4), new(4, 8), A.mult)
+        tt(S("XC", 0, 8), new(0, 8), S("NM", 136, 144), A.mult)
         ts(S("LHI", 24, 28), S("XC", 8, 12), 5, A.logical_shift_right, 2047, A.bitwise_and)
-        ts(S("LHI", 0, 12), S("XC", 0, 12), 5, A.logical_shift_right, 63, A.bitwise_and)
-        tt(S("OFF", 0, 4), S("LHI", 24, 28), S("NT", 0, 4), A.max)
-        ts(S("LHI", 12, 24), S("XC", 0, 12), 11, A.logical_shift_right, 31, A.bitwise_and)
-        cp(S("LHF", 0, 12), S("LHI", 0, 12))
+        ts(S("SD", 0, 384, 32) if FUSE else S("LHI", 0, 12), S("XC", 0, 12), 5, A.logical_shift_right, 63, A.bitwise_and)
+        if FUSE:
+            tt(S("OFF", 0, 4), S("LHI", 24, 28), S("NT", 0, 4), A.max)
+        ts(S("SD", 384, 768, 32) if FUSE else S("LHI", 12, 24), S("XC", 0, 12), 11, A.logical_shift_right, 31, A.bitwise_and)
+        if not FUSE:
+            tt(S("OFF", 0, 4), S("LHI", 24, 28), S("NT", 0, 4), A.max)
+            cp(S("SD", 0, 768, 32), S("LHI", 0, 24))
         for q in range(4):
-            act(B("EE2", q, 16), S("MK", 0, 16), F.Copy, 0.0, S("OFF", q, q + 1))
+            act(B("EE2", q, 16), S("MK", 0, 16), F.Copy, 1.0 / 32, S("OFF", q, q + 1))
+        k = 4 if last else 8
         for h in range(2):
-            mm(part("UB", h, 64, 72), S("EE2", 0, 64), S("MS", 8, 16), True, True)
-        cp(S("SD", 0, 384, 32), S("LHI", 12, 24))
+            m0 = 8 + h * (8 - k)
+            mm(part("UB", h, 64, 64 + k), S("EE2", 0, 64), S("MS", m0, m0 + k), True, True)
         yield FILL["spread"]
-        send_names()
+        msg = 16 * (4 * H + t)
+        if last:
+            ts(B("MFo", H, 8), S("LQ", 0, 8), cc(34), A.add)
+            send(B("MFi", H, 8), B("MFo", H, 8), dst, src, "rn%d%d" % (H, t))
+        else:
+            ts(S("MSG", msg, msg + 8), S("LQ", 0, 8), -0.5, A.add)
+            send(B("MR", 3 * H + t, 8), S("MSG", msg, msg + 8), dst, src, "rn%d%d" % (H, t))
         yield FILL["far"]
-        cp(S("OFFL", 0, 8), S("UB", 64, 72))
-        act(B("T1", 0), G(S(win, 0, W + 128 * t + 128), S("OFFL", 0, 8)), F.Copy, M2, 511.0 / 512)
-        scan(S("SN", 0, 384), S("SR", 0, 384), S("SD", 0, 384), 0.0, A.mult, A.add)
-        for q in squares[:1]:
-            low(q)
-        act(B("ZS", 4 * H + t), B("T1", 0), F.Copy, -M2 / 2, 0.5)
-        send(B("ZI", 5 * H + t + 1), B("ZS", 4 * H + t), dst, src, "rz%d%d" % (H, t))
+        ts(S("MSG", msg + 8, msg + 8 + k), S("UB", 64, 64 + k), -0.5, A.add)
+        act(S("T1", 0, 16 * k), G(S(win, 0, W + 128 * t + 128), S("MSG", msg + 8, msg + 8 + k)), F.Copy, M2, 511.0 / 512)
+        scan(S("SN", 0, 384), S("SR", 0, 384), S("SD", 384, 768), 0.0, A.mult, A.add)
+        if squares and not last:
+            low(squares[0])
+        zs, zi = 128 * (4 * H + t), 128 * (5 * H + t + 1)
+        act(S("ZS", zs, zs + 16 * k), S("T1", 0, 16 * k), F.Copy, -M2 / 2, 0.5)
+        send(S("ZI", zi, zi + 16 * k), S("ZS", zs, zs + 16 * k), dst, src, "rz%d%d" % (H, t))
+        if last:
+            low(squares[0])
+        for hi in range(3 * (2 * t + H), min(16, 3 * (2 * t + H) + 3)):
+            pick(B("SGW", hi), B("ONE", 0), [[-16, 2], [-32, 4], [0, 16]], -hi, 1)
         low(3)
         ts(S("OHH", 0, 384), S("SN", 0, 384), 0.0, A.is_equal, -1.0, A.mult)
         for q in range(3):
@@ -489,31 +495,31 @@ def rank_program(g, core, T, topo):
             hits(q)
         yield FILL["sent"]
         if not last:
-            later = lists(H, t + 1)
-            if COSTS_LATE:
-                yield next(later)
             act(B("ZF", H, 64), B("HH", 0, 64), F.Relu)
-            act(B("ZH", H, 64), B("HH", 0, 64), F.Relu)
             cw = T["CW%d" % H]
             dmas("y", "cw%d%d" % (H, t), [((cw[64 * h:64 * h + 64:16, :], [("CW%d" % H, 0, W, 1, False)]), B("ZF", H, 64)) for h in range(2)])
-            yield from later
+            pick(B("ZH", H, 64), B("ZF", H, 64), [[0, 64]])
+            yield FILL["out"]
+            yield from lists(H, t + 1)
             return
         act(B("SG", 0, 64), B("HH", 0, 64), F.Sign, cc(35))
-        banks = ("VV", "UB", "S0", "YB") if H else ("VV", "UB")
+        banks = LAST_BANKS if H else ("VV", "UB")
         n = 1024 // len(banks)
         for hi in range(16):
             mm(B(banks[64 * hi // n], hi % (n // 64), 64), B("SGW", hi), B("SG", 0, 64), True, True)
-        ts(B("CI", 0, 16), B("CK", H, 16), -1.0, A.mult, NONE, A.add)
-        ts(B("CF", 0, 16), B("CK", H, 16), 0.0, A.is_equal, -8193.0, A.mult)
-        ts(B("CI", 1, 16), B("CI", 0, 16), 6, A.logical_shift_right)
+        for q in range(4):
+            ts(B("CI", q, 4), S("MSI", 1024 * H + 256 * q + 252, 1024 * H + 256 * q + 256), 8, A.logical_shift_right)
+        yield FILL["product"]
+        ts(B("CF", 0, 16), B("CI", 0, 16), 8192.0, A.is_equal, -8193.0, A.mult)
         yield FILL["mates"]
-        tt(B("CF", 1, 16), B("CI", 1, 16), B("CF", 0, 16), A.add)
+        tt(B("CF", 1, 16), B("CI", 0, 16), B("CF", 0, 16), A.add)
         mm(S("LQ", 0, 128, 1, 0, 16), B("CF", 1, 16), B("IDf", 0), True, True)
         q = "s" if H else "y"
-        dmas(q, "op%d" % H, [(X(T.yp[r, 8 - 8 * h:16 - 8 * h]), part("MFi", h, 8 * H, 8 * H + 8)) for h in range(2)])
+        yield FILL["cast"]
         act(S("YC", 128 * H, 128 * H + 128, 1, 0, 16), S("LQ", 0, 128, 1, 0, 16))
         dmas(q, "oc%d" % H, [(X(T.yc[4 * H:4 * H + 4, :]), S("YC", 128 * H, 128 * H + 128, 1, 0, 16))])
-        dmas(q, "oz%d" % H, [(X(T.yz[r, :]), part("ZI", 0, 640 * H + 512, 640 * H + 640))])
+        dmas(q, "op%d" % H, [(X(T.yp[r, 8 - 8 * h:16 - 8 * h]), part("MFi", h, 8 * H, 8 * H + 8)) for h in range(2)])
+        dmas(q, "oz%d" % H, [(X(T.yz[r, 64 * h:64 * h + 64]), part("ZI", h, 640 * H + 512, 640 * H + 576)) for h in range(2)])
         for u, name in enumerate(banks):
             x0 = 1024 * H
             tt(S("YF", x0 + n * u, x0 + n * u + n), S("FIN", x0 + n * u, x0 + n * u + n), S(name, 0, n), A.mult)
@@ -540,8 +546,9 @@ def rank_program(g, core, T, topo):
                     out, w = S(bank, 8 * int(name[1]) + b, 256, 32), S("W32", 32 * k, 32 * k + 32, 4)
                 mm(out, S(data, pos + b, pos + n, 8), w, False, left[0] == 0 and b == 7)
             if name == "c4" and k == 0:
-                mm(S("NM", 0, 140), B("OWN", H), S("OWW", 0, 140), True, False)
-                mm(B("NM", 0), B("GG", H), B("NMW", 0), False, True)
+                mm(S("NM", 0, 144), B("OWN", H), S("OWW", 0, 144), True, False)
+                mm(S("NM", 0, 68), B("E0", 0), S("C17", 0, 68), False, False)
+                mm(S("NM", 0, 136), B("GG", H), S("NMW", 0, 136), False, True)
 
         def gather(data, n):
             end = min(done[data] + n, 5376)

from concourse.mybir import AluOpType as A, ActivationFunctionType as F

N, W, ROUNDS = 8, 2048, 4
SHIFT = 315
BIG = float(2 ** 22)
NONE = float(2 ** 21 + 32 * 4 + 16)
M2 = 1.5 * 2 ** 24
LAST_BANKS = ("VV", "UB", "S0", "YB")
FUSE = False
CAST = "sg"
SQUARES, LAST_SQUARES = (0,), (0, 1)
NEEDS, FIRST_NEEDS = "gggggsss", {(0, 0): "ssssvvvv", (0, 1): "ggssvvvv"}
FILL = {"start": (640, 1408), "min": (0, 640), "count": (0, 0), "hot": (0, 0), "product": (128, 0), "sum": (128, 0), "names": (128, 0),
        "spread": (320, 640), "far": (256, 0), "sent": (2752, 1088), "out": (0, 0), "mates": (0, 896), "copied": (0, 0), "places": (128, 1280), "cast": (0, 0),
        "init": (768, 1024), "costs": (1280, 2304)}
FIRST = {(0, 0): {"start": (768, 1408), "min": (0, 0), "product": (0, 0), "sum": (0, 0), "spread": (128, 512), "far": (128, 128), "sent": (2944, 768), "out": (128, 1920),
                  "mates": (128, 0), "copied": (256, 896), "places": (256, 512)},
         (1, -1): {"init": (768, 1280), "mates": (1024, 512), "copied": (256, 256), "places": (128, 896)},
         (0, 3): {"sum": (256, 0), "spread": (640, 512), "sent": (2304, 896), "mates": (128, 1408), "cast": (0, 1024)}}
REST = {"min": 2, "count": 1, "hot": 1, "product": 1, "init": 5}
FREE = ("min", "count", "sent", "mates", "places", "cast", "costs")


def fills(H, t):
    return {k: v + (k in FREE, REST.get(k, 0)) for k, v in dict(FILL, **FIRST.get((H, t), {})).items()}


SPEC = {
    "bfloat16": "WIN0 2560 WIN1 2560 FIN 2048 YF 2048 ZR 2048 FD 5376 OL 768 SQ 768 SD 768 SR 384 SN 384 OHH 384 SG 64 TK 4 "
                "SEED 136 KEEP 136 CNT 136 OH 136 ZS 1024 ZI 1280 "
                "IOT 136 N32 32 C17 68 ONE 136 IDb 128 E0 128 CA 128 CB 128 CC 128 CD1 128 CE 256 SEL 3584 NMW 136 OWW 144 W32 64 W1 1024 BI 256 LW 160 SGW 2048",
    "float32": "CW0 2048 CW1 2048 ZF 128 PW 136 SC 136 NT 4 OFF 4 EE 128 EE2 64 UUS 80 T1 128 MK 16 MS 16 pF 8 cc 40 DRM 256 "
               "IDf 128 ONf 128 YC 256 CF 64 MFo 16 MFi 16 OWNW 1064",
    "int32": "NW0 1064 NW1 1064 PR 16 XI 336 XJ 336 MSI 2048 SEEDI 136 XC 12 LHI 28 CI 64 pI 8",
    "float16": "GG 256 OWN 256 CD 5376 ZH 128",
    "uint16": "NL 16 MSG 128 MR 48 LST 672",
}
PSUM = ("S0", "S1", "NM", "VV", "UB", "LQ", "HH", "YB")
SCRATCH = {n: ("psum", [128, 512], "float32") for n in PSUM}
for _ty, _l in SPEC.items():
    _l = _l.split()
    for _n, _c in zip(_l[::2], _l[1::2]):
        SCRATCH[_n] = ("sbuf", [128, int(_c)], _ty)
SEMAPHORES = ["qv", "qs", "qt", "qg", "df", "dc", "ls"] + [p + str(h) for p in ("dl", "dn", "dm", "dw", "y0", "y1", "y2", "y3", "oc", "op", "oz") for h in range(2)] + \
    [p + str(h) + str(t) for p in ("rn", "rz", "cw") for h in range(2) for t in range(ROUNDS)]
F1 = 192
CUTS = (2048, 3072, 4352, 5376)
LISTS = [("a0", 0, 64), ("a1", 64, 64), ("a2", 128, 64), ("f1", F1, 16), ("c4", 208, 64), ("a3", 272, 64)]


def rank_program(g, core, T, topo):
    rank = T.rank_of(core)
    if rank is None:
        return
    queues = {"v": g.vector, "s": g.scalar, "t": g.tensor, "g": g, "y": g.sync}
    acc, cnt, final = {}, {}, {}
    known = {q: {} for q in "vstgyx"}

    def overlap(a, b):
        if max(a[1], b[1]) >= min(a[2], b[2]):
            return False
        if a[3] == b[3]:
            return a[3] == 1 or (a[1] - b[1]) % a[3] == 0
        if a[3] < b[3]:
            a, b = b, a
        return any(x in range(b[1], b[2], b[3]) for x in range(a[1], a[2], a[3]))

    def before(q, reads, writes):
        deps = {}
        for kind, regs in (("r", reads), ("w", writes)):
            for r in regs:
                for k2, r2, q2, ev, clk in acc.get(r[0], ()):
                    both = kind == "r" and k2 == "r"
                    if r[0] in PSUM:
                        if q == q2 and (q == "t" or both or not overlap(r, r2)):
                            continue
                    elif both or not overlap(r, r2):
                        continue
                    if known[q].get(ev[0], 0) < ev[1] and (ev[0] not in deps or deps[ev[0]][0] < ev[1]):
                        deps[ev[0]] = (ev[1], clk)
        for s in sorted(deps):
            if not any(s2 != s and deps[s2][1].get(s, 0) >= deps[s][0] for s2 in deps):
                queues[q].wait_ge(T.sem[s], deps[s][0])
        for s in deps:
            for s2, v in list(deps[s][1].items()) + [(s, deps[s][0])]:
                known[q][s2] = max(known[q].get(s2, 0), v)

    def after(q, reads, writes, ev):
        clk = dict(known[q])
        clk[ev[0]] = max(clk.get(ev[0], 0), ev[1])
        for kind, regs in (("r", reads), ("w", writes)):
            for r in regs:
                keep = []
                for e in acc.get(r[0], ()):
                    inside = r[4] and r[1] <= e[1][1] and e[1][2] <= r[2] and (r[3] == 1 or (r[3] == e[1][3] and (r[1] - e[1][1]) % r[3] == 0))
                    if not (inside and (kind == "w" or (e[0] == "r" and e[2] == q))):
                        keep.append(e)
                acc[r[0]] = keep + [(kind, r, q, ev, clk)]

    def emit(q, call, reads, writes):
        before(q, reads, writes)
        s = "q" + q
        cnt[s] = cnt.get(s, 0) + 1
        call().then_inc(T.sem[s], 1)
        final[s] = cnt[s]
        after(q, reads, writes, (s, cnt[s]))

    def dmas(q, sem, moves):
        total = 16 * len(moves)
        for out, in_ in moves:
            before(q, in_[1], out[1])
        for out, in_ in moves:
            queues[q].dma_start(out[0], in_[0]).then_inc(T.sem[sem], 16)
        for out, in_ in moves:
            after(q, in_[1], out[1], (sem, total))
        final[sem] = total

    def S(name, a, b, step=1, p0=0, p1=128):
        t = T[name]
        return (t[p0:p1, a:b] if step == 1 else t[p0:p1, a:b:step], [(name, a, b, step, p1 - p0 == 128)])

    def B(name, i, n=128):
        return S(name, n * i, n * i + n)

    def X(ap):
        return (ap, [])

    def G(win, off):
        return (win[0].indirect(off[0]), win[1] + off[1])

    def sc(x):
        return x[0] if isinstance(x, tuple) else x

    def rg(*xs):
        r = []
        for x in xs:
            r = r + (x[1] if isinstance(x, tuple) else [])
        return r

    def cp(out, in_):
        emit("v", lambda: g.vector.tensor_copy(out[0], in_[0]), in_[1], out[1])

    def tt(out, a, b, op):
        emit("v", lambda: g.vector.tensor_tensor(out[0], a[0], b[0], op), a[1] + b[1], out[1])

    def ts(out, a, s1, op0, s2=None, op1=None):
        if op1 is None:
            emit("v", lambda: g.vector.tensor_scalar(out[0], a[0], sc(s1), None, op0), rg(a, s1), out[1])
        else:
            emit("v", lambda: g.vector.tensor_scalar(out[0], a[0], sc(s1), sc(s2), op0, op1), rg(a, s1, s2), out[1])

    def ms(out, c):
        emit("v", lambda: g.vector.memset(out[0], c), [], out[1])

    def scan(out, a, b, init, op0, op1):
        emit("v", lambda: g.vector.tensor_tensor_scan(out[0], a[0], b[0], init, op0, op1), rg(a, b), out[1])

    def act(out, in_, func=F.Copy, bias=0.0, scale=1.0):
        emit("s", lambda: g.scalar.activation(out[0], in_[0], func, bias=sc(bias), scale=sc(scale)), rg(in_, bias, scale), out[1])

    def mm(out, lhsT, rhs, start, stop):
        emit("t", lambda: g.tensor.matmul(out[0], lhsT[0], rhs[0], start, stop), lhsT[1] + rhs[1], out[1])

    def iota(out, pattern, base=0, cm=0):
        if SCRATCH[out[1][0][0]][2] == "int32":
            emit("g", lambda: g.iota(out[0], pattern, base, cm), [], out[1])
        else:
            emit("g", lambda: g.iota(out[0], pattern, base, cm, allow_small_or_imprecise_dtypes=True), [], out[1])

    def pick(out, in_, pattern, base=0, cm=0, op=A.is_equal):
        emit("g", lambda: g.affine_select(out[0], in_[0], pattern, op, 0.0, base, cm), in_[1], out[1])

    def send(out, src, dst, frm, rsem):
        before("g", src[1], [])
        rid, pid = topo.addr(dst, core)
        g.remote_dma(out[0], src[0], T.sem[rsem], T.sem["ls"], pid, rid, topo.mask(core, dst))
        final["ls"] = final.get("ls", 0) + len(topo.engines(core, dst))
        final[rsem] = len(topo.engines(frm, core))
        after("x", [], out[1], (rsem, final[rsem]))

    def rows(t, H):
        return t[64 * H:64 * H + 64, :]

    def part(name, h, a, b):
        return S(name, a, b, 1, 64 * h, 64 * h + 64)

    def load_mates(q, H):
        dmas(q, "dm%d" % H, [(part("NW%d" % H, 0, 296, 1064), X(rows(T.cmate, H))), (part("NW%d" % H, 1, 8, 1032), X(rows(T.rmate, H)))])

    def load_figures(q, H):
        r = slice(64 * H, 64 * H + 64)
        dmas(q, "dw%d" % H, [m for h in range(2) for m in ((part("WIN%d" % H, h, SHIFT, W), X(T.fig[r, 0:W - SHIFT])), (part("WIN%d" % H, h, 0, SHIFT), X(T.fig[r, W - SHIFT:W])))])

    def pieces(H, x0, x1):
        cuts = [(0, x0, min(x1, SHIFT)), (0, max(x0, SHIFT), x1), (1, x0, x1)]
        return [(h, a, b, (1024 * h + a - SHIFT) % W) for h, a, b in cuts if a < b]

    for H in range(2):
        dmas("s", "dl%d" % H, [(part("PR", h, 8 * H, 8 * H + 8), X(rows((T.pcol, T.prow)[h], H))) for h in range(2)])
        dmas("s", "dn%d" % H, [(part("ZI", h, 640 * H, 640 * H + 128), X(rows(T.need, H))) for h in range(2)])
    load_mates("y", 0)
    load_figures("y", 0)
    before("y", S("NW0", 0, 1024)[1], [])
    load_mates("y", 1)
    load_figures("y", 1)
    before("y", S("NW1", 0, 1024)[1], [])
    dmas("y", "df", [(part("FIN", h, 1024 * H + a, 1024 * H + b), X(T.fig[64 * H:64 * H + 64, c:c + b - a])) for H in range(2) for h, a, b, c in pieces(H, 0, 1024)])

    iota(S("pI", 0, 1), [[0, 1]], 0, 1)
    iota(S("IOT", 0, 136), [[1, 136]])
    for h in range(2):
        iota(B("CA", h, 64), [[16, 4], [64, 2], [1, 8]], 8 * h)
        iota(B("CB", h, 64), [[1, 4], [4, 2], [0, 8]])
    iota(S("OWNW", 0, 266), [[1, 266]])
    for h in range(2):
        iota(B("CC", h, 64), [[1, 4], [4, 8], [0, 2]])
        iota(B("CD1", h, 64), [[1, 4], [4, 8], [32, 2]], 64 * h)
    iota(S("N32", 0, 32), [[1, 8], [0, 4]])
    for q in range(4):
        iota(B("BI", q, 64), [[8, 2], [32, 4], [1, 8]])
    for q in range(4):
        iota(B("CE", q, 64), [[0, 2], [1, 4], [0, 8]], 4 * q)
    iota(S("SEED", 0, 68), [[0, 68]], 17)
    pick(S("C17", 0, 68), S("SEED", 0, 68), [[0, 4], [-1, 17]], 16, 0, A.is_gt)
    iota(S("CW0", 0, W), [[0, W]])

    def cc(i, n=1):
        return S("cc", i, i + n)

    pP, pH, pG, pS, pA, pM, pQ, pT = [S("pF", i, i + 1) for i in range(8)]
    I4 = S("IOT", 0, 4)
    def pad(H):
        for n, (h, a, b) in enumerate([(0, 0, 296), (1, 0, 8), (1, 1032, 1064)]):
            ms((part("NW%d" % H, h, a, b)[0], [("pad", 3 * H + n, 3 * H + n + 1, 1, True)]), 0)

    pad(0)
    for i, (sh, mask) in enumerate([(6, 1), (4, 3), (0, 15), (0, 3), (4, 7), (4, 1), (2, 3)]):
        ts(S("pI", i + 1, i + 2), S("pI", 0, 1), sh, A.logical_shift_right, mask, A.bitwise_and)
    cp(S("pF", 0, 8), S("pI", 0, 8))
    for q in range(1, 4):
        act(B("OWNW", q, 266), B("OWNW", 0, 266), F.Copy, 266.0 * q)
    ts(cc(34), pH, 288.0, A.mult, -296.5, A.add)
    ts(cc(0), pH, 1000.0, A.mult, pP, A.add)
    ts(cc(1), pH, -100.0, A.mult, 100.0, A.add)
    ts(cc(2), pS, 2.0, A.is_ge, 100.0, A.mult)
    ts(cc(3), pH, 100.0, A.mult, pG, A.add)
    ts(cc(4, 4), I4, pA, A.not_equal, 100.0, A.mult)
    ts(cc(8, 4), I4, pT, A.is_equal, 2.0, A.mult)
    ts(cc(16), pH, -1.0, A.mult, 1.0, A.add)
    ts(cc(17), pH, 593.0, A.mult)
    ts(cc(18), pS, 0.0, A.is_equal)
    ts(cc(19), pS, 1.0, A.is_equal)
    ts(cc(20), pH, -0.5, A.mult, 1.0, A.add)
    ts(cc(21), pH, -1.0, A.mult, 2.0, A.add)
    tt(cc(1), cc(1), pG, A.add)
    tt(cc(3), cc(3), cc(2), A.add)
    ts(cc(8, 4), cc(8, 4), pH, A.mult, cc(16), A.add)
    ts(cc(12, 4), I4, pT, A.is_equal, cc(17), A.mult)
    tt(cc(20), cc(20), cc(19), A.mult)
    tt(cc(28), cc(21), cc(18), A.mult)
    ts(cc(4, 4), cc(4, 4), cc(1), A.add)
    ts(cc(23), pS, 0.0, A.not_equal, 100.0, A.mult)
    ts(cc(24), pA, 32.0, A.mult, cc(1), A.add)
    ts(cc(22), pG, 2.0, A.mult, pH, A.add)
    tt(cc(23), cc(23), cc(1), A.add)
    ts(cc(24), cc(16), 100.0, A.mult, cc(24), A.add)
    for kp in range(2):
        ts(B("SEL", kp), B("CA", 0), 64.0 * kp, A.subtract, cc(0), A.is_equal)
        ts(B("SEL", 2 + kp), B("CB", 0), 4.0 * kp, A.subtract, cc(3), A.is_equal)
    for a in range(4):
        for kp in range(2):
            ts(B("SEL", 4 + 2 * a + kp), B("CB", 0), 4.0 * kp, A.subtract, cc(4 + a), A.is_equal)
    for c in range(8):
        ts(B("SEL", 12 + c), B("CC", 0), 4.0 * c, A.subtract, cc(23), A.is_equal)
        ts(B("SEL", 20 + c), B("CD1", 0), 4.0 * c, A.subtract, cc(24), A.is_equal)
        if c == 3:
            ts(B("NL", 0, 8), B("PR", 0, 8), cc(34), A.subtract, -0.5, A.add)

    def weights():
        ms(B("E0", 0), 1.0 / 128)
        ms(S("DRM", 0, 256), 0.0)
        ms(S("ONE", 0, 136), 1.0)
        ts(cc(26), cc(22), 2.0, A.mult)
        ts(cc(27), cc(22), 2.0, A.mult, 1.0, A.add)
        ts(cc(29), pS, 2.0, A.is_lt)
        ts(cc(30), pS, -1.0, A.mult, pA, A.add)
        ts(cc(31), pH, 4.0, A.mult, pG, A.add)
        ts(cc(32), pH, -56.0, A.mult, 72.0, A.add)
        ts(cc(33), pG, 17.0, A.mult, pS, A.add)
        yield
        yield
        pad(1)
        yield
        ts(B("W32", 0, 32), S("N32", 0, 32), cc(22), A.is_equal, BIG, A.mult)
        ts(B("W32", 1, 32), S("N32", 0, 32), cc(22), A.is_equal, 256.0, A.mult)
        ms(S("DRM", 0, 256, 64), NONE)
        yield

    def late_constants():
        FILL = fills(1, -1)
        for a in range(2):
            ts(B("W1", a, 256), S("CE", 0, 256), cc(26 + a), A.is_equal, BIG, A.mult)
            act(B("W1", 2 + a, 256), B("W1", a, 256), F.Copy, 0.0, 256.0 / BIG)
        act(cc(35), pH, F.Copy, -0.5, 0.0)
        act(cc(36, 4), I4, F.Identity, pP, 128.0)
        act(B("ONf", 0), B("ONE", 0))
        act(cc(36, 4), cc(36, 4), F.Copy, float(W))
        ts(cc(30), cc(30), 68.0, A.add, pH, A.mult)
        ts(cc(32), pG, 17.0, A.mult, cc(32), A.add)
        ts(cc(17), pH, 1.0, A.add, cc(29), A.mult)
        tt(cc(30), cc(30), cc(33), A.add)
        yield FILL["init"]
        ts(B("NL", 1, 8), B("PR", 1, 8), cc(34), A.subtract, -0.5, A.add)
        ts(S("MK", 0, 16), S("IOT", 0, 16), pS, A.is_equal)
        ts(S("OWW", 136, 144), S("IOT", 0, 8), cc(31), A.is_equal, cc(17), A.mult)
        ts(S("OWW", 0, 136), S("IOT", 0, 136), cc(32), A.is_equal, cc(17), A.mult)
        ts(S("NMW", 0, 136), S("IOT", 0, 136), cc(30), A.is_equal, cc(21), A.mult)
        yield from lists(1, 0)
        ts(S("MS", 0, 8), S("IOT", 0, 8), pM, A.is_equal, 0.5, A.mult)
        ts(S("MS", 8, 16), S("IOT", 0, 8), pM, A.is_equal)
        ms(S("LW", 0, 160), 0.0)
        iota(S("SEEDI", 0, 136), [[0, 136]], -1)
        iota(S("SD", 384, 768), [[0, 384]], -1)
        pick(S("KEEP", 0, 136), S("ONE", 0, 136), [[0, 8], [1, 17]], op=A.is_gt)
        for q in range(3):
            pick(B("SR", q), B("ONE", 0), [[0, 4], [1, 32]], op=A.is_gt)
        ts(cc(2), pH, 100.0, A.mult, pG, A.add)
        ts(S("LW", 32, 160, 32), I4, cc(2), A.is_equal)
        pick(B("IDb", 0), B("ONE", 0), [[-1, 128]], 0, 1)
        dmas("y", "dc", [(S("CW1", 0, W), S("CW0", 0, W))])
        pick(B("IDf", 0), B("ONf", 0), [[-1, 128]], 0, 1)
        for H in range(2):
            for hi in range(32):
                mm(B("HH", H, 64), S("LW", 32 - hi, 160 - hi), B("WIN%d" % H, hi, 64), hi == 0, hi == 31)
        yield FILL["costs"]
        act(B("ZH", 0), B("HH", 0))

    rest = []

    def lists(H, t):
        FILL = fills(H, t - 1)
        nl = B("NL", H, 8) if t == 0 else B("MR", 3 * H + t - 1, 8)
        gg, own, need = B("GG", H), B("OWN", H), B("ZI", 5 * H + t)
        mates = S("NW%d" % H, 0, 1064)
        mates = (mates[0], mates[1] + [("pad", 3 * H, 3 * H + 3, 1, True)])
        act(gg, G(mates, nl), F.Identity, cc(12 + (t + 1) % 4), cc(8 + t))
        act(own, G(S("OWNW", 0, 1064), nl), F.Identity, cc(20), cc(28))

        def spread(out, sel, name, n):
            for c in range(n):
                mm(out, B("SEL", sel + c), S(name, 128 * H + c, 128 * H + 128, n), c == 0, c == n - 1)

        def needs(who):
            for b, by in enumerate(FIRST_NEEDS.get((H, t), NEEDS)):
                o = S("ZR", 1024 * H + b, 1024 * H + 1024, 8)
                if by == who == "s":
                    act(o, need)
                elif by == who == "v":
                    cp(o, need)
                elif by == who:
                    pick(o, need, [[0, 128]])

        needs("g")
        spread(S("UB", 0, 64), 0, "GG", 2)
        for a in range(4):
            spread(B("VV", a, 64), 4 + 2 * a, "GG", 2)
        spread(B("VV", 4, 64), 2, "OWN", 2)
        spread(S("YB", 0, 16), 12, "OWN", 8)
        spread(S("YB", 16, 32), 20, "GG", 8)
        yield FILL["mates"]
        act(S("UUS", 0, 64), S("UB", 0, 64), F.Copy, 17.0, 2.0)
        yield FILL["copied"]
        def product(name, col, cols):
            if cols == 64:
                tt(S("XI", col, col + 64), S("UUS", 0, 64), B("VV", int(name[1]), 64), A.mult)
            else:
                tt(S("XI", col, col + 16), S("UUS", 64, 80), S("YB", 16, 32), A.mult)

        def places(a, b):
            ts(S("LST", 336 * H + a, 336 * H + b) if FUSE else S("XJ", a, b), S("XI", a, b), 5, A.logical_shift_right, 2047, A.bitwise_and)

        def cast(a, b, by):
            if FUSE:
                return
            if by == "g":
                pick(S("LST", 336 * H + a, 336 * H + b), S("XJ", a, b), [[0, b - a]])
            else:
                (act if by == "s" else cp)(S("LST", 336 * H + a, 336 * H + b), S("XJ", a, b))

        for l in LISTS[:3]:
            product(*l)
        needs("s")
        act(S("UUS", 64, 80), S("YB", 0, 16), F.Copy, 1.0, 2.0)
        yield FILL["places"]
        places(0, F1)
        needs("v")
        yield FILL["cast"]
        cast(0, F1, CAST[0] if H + t else "v")
        act(S("WIN%d" % H, W + 128 * t, W + 128 * t + 128), need, F.Copy, 0.0, 2.0)
        rest.extend([lambda: product(*LISTS[4]), lambda: product(*LISTS[5]), lambda: product(*LISTS[3]), lambda: places(F1, 336), lambda: cast(F1, 336, CAST[1] if H + t else "s")])

    def tail(H, t):
        dst = T.cores[(rank + 1 + t % 3) % N]
        src = T.cores[(rank - 1 - t % 3) % N]
        last, FILL = t == ROUNDS - 1, fills(H, t)
        bank, win, r = "S%d" % H, "WIN%d" % H, slice(64 * H, 64 * H + 64)
        yield FILL["start"]
        scan(S("MSI", 1024 * H + t, 1024 * H + 1024, 4), S("DRM", 0, 256), S(bank, 0, 256), 0.0, A.max, A.min)
        yield FILL["min"]
        m = S("MSI", 1024 * H + 252 + t, 1024 * H + 1024, 256)
        act(S("TK", 0, 4), m, F.Copy, NONE, -1.0)
        ts(S("SEEDI", 0, 68, 17), m, 31, A.bitwise_and)
        ts(S("SEEDI", 68, 136, 17), m, 5, A.logical_shift_right, 7, A.bitwise_and)
        yield FILL["count"]
        scan(B("CNT", 0, 136), B("KEEP", 0, 136), B("SEEDI", 0, 136), 0.0, A.mult, A.add)
        yield FILL["hot"]
        ts(B("OH", 0, 136), B("CNT", 0, 136), 0.0, A.is_equal)
        yield FILL["product"]
        tt(B("PW", 0, 136), B("OH", 0, 136), B("NM", 0, 136), A.mult)
        yield FILL["sum"]
        scan(B("SC", 0, 136), B("KEEP", 0, 136), B("PW", 0, 136), 0.0, A.mult, A.add)
        yield FILL["names"]
        squares = (LAST_SQUARES if last else SQUARES)

        def new(a, b):
            return S("SC", 17 * a + 16, 17 * b, 17)

        def names():
            for q in range(8):
                act(B("EE", q, 16), S("MK", 0, 16), F.Copy, 0.0, S("SC", 17 * ((q + 4) % 8) + 16, 17 * ((q + 4) % 8) + 17))
                if q == 0:
                    act(S("NT", 0, 4), S("TK", 0, 4), F.Relu, cc(36 + t), -1.0)
            mm(S("LQ", 0, 8), B("EE", 0), S("MS", 0, 8), True, True)

        def low(q):
            for c in range(3):
                col = S("SD", 32 * (4 * c + q), 32 * (4 * c + q) + 1)
                if q in squares:
                    act(B("SQ", 3 * q + c, 64), S("IOT", 0, 64), F.Square, col, -1.0)
                else:
                    ts(B("OL", 3 * q + c, 64), S("IOT", 0, 64), col, A.is_equal, S("TK", q, q + 1), A.mult)

        def hits(q):
            if q in squares:
                act(B("OL", q, 192), B("SQ", q, 192), F.Relu, S("TK", q, q + 1), -2 * NONE)
            costs = S("HH", 0, 64, 1, 32 * q, 32 * q + 32)
            mm(costs, B("IDb", q, 32), B("ZH", H, 64), True, False)
            for c in range(3):
                mm(costs, B("OHH", 4 * c + q, 32), B("OL", 3 * q + c, 64), False, c == 2)

        names()
        tt(S("XC", 8, 12), new(0, 4), new(4, 8), A.mult)
        tt(S("XC", 0, 8), new(0, 8), S("NM", 136, 144), A.mult)
        ts(S("LHI", 24, 28), S("XC", 8, 12), 5, A.logical_shift_right, 2047, A.bitwise_and)
        ts(S("SD", 0, 384, 32) if FUSE else S("LHI", 0, 12), S("XC", 0, 12), 5, A.logical_shift_right, 63, A.bitwise_and)
        if FUSE:
            tt(S("OFF", 0, 4), S("LHI", 24, 28), S("NT", 0, 4), A.max)
        ts(S("SD", 384, 768, 32) if FUSE else S("LHI", 12, 24), S("XC", 0, 12), 11, A.logical_shift_right, 31, A.bitwise_and)
        if not FUSE:
            tt(S("OFF", 0, 4), S("LHI", 24, 28), S("NT", 0, 4), A.max)
            cp(S("SD", 0, 768, 32), S("LHI", 0, 24))
        for q in range(4):
            act(B("EE2", q, 16), S("MK", 0, 16), F.Copy, 1.0 / 32, S("OFF", q, q + 1))
        k = 4 if last else 8
        for h in range(2):
            m0 = 8 + h * (8 - k)
            mm(part("UB", h, 64, 64 + k), S("EE2", 0, 64), S("MS", m0, m0 + k), True, True)
        yield FILL["spread"]
        msg = 16 * (4 * H + t)
        if last:
            ts(B("MFo", H, 8), S("LQ", 0, 8), cc(34), A.add)
            send(B("MFi", H, 8), B("MFo", H, 8), dst, src, "rn%d%d" % (H, t))
        else:
            ts(S("MSG", msg, msg + 8), S("LQ", 0, 8), -0.5, A.add)
            send(B("MR", 3 * H + t, 8), S("MSG", msg, msg + 8), dst, src, "rn%d%d" % (H, t))
        yield FILL["far"]
        ts(S("MSG", msg + 8, msg + 8 + k), S("UB", 64, 64 + k), -0.5, A.add)
        act(S("T1", 0, 16 * k), G(S(win, 0, W + 128 * t + 128), S("MSG", msg + 8, msg + 8 + k)), F.Copy, M2, 511.0 / 512)
        scan(S("SN", 0, 384), S("SR", 0, 384), S("SD", 384, 768), 0.0, A.mult, A.add)
        if squares and not last:
            low(squares[0])
        zs, zi = 128 * (4 * H + t), 128 * (5 * H + t + 1)
        act(S("ZS", zs, zs + 16 * k), S("T1", 0, 16 * k), F.Copy, -M2 / 2, 0.5)
        send(S("ZI", zi, zi + 16 * k), S("ZS", zs, zs + 16 * k), dst, src, "rz%d%d" % (H, t))
        if last:
            low(squares[0])
        for hi in range(3 * (2 * t + H), min(16, 3 * (2 * t + H) + 3)):
            pick(B("SGW", hi), B("ONE", 0), [[-16, 2], [-32, 4], [0, 16]], -hi, 1)
        low(3)
        ts(S("OHH", 0, 384), S("SN", 0, 384), 0.0, A.is_equal, -1.0, A.mult)
        for q in range(3):
            if q not in squares[:1]:
                low(q)
        for q in sorted(range(4), key=lambda q: q in squares):
            hits(q)
        yield FILL["sent"]
        if not last:
            act(B("ZF", H, 64), B("HH", 0, 64), F.Relu)
            cw = T["CW%d" % H]
            dmas("y", "cw%d%d" % (H, t), [((cw[64 * h:64 * h + 64:16, :], [("CW%d" % H, 0, W, 1, False)]), B("ZF", H, 64)) for h in range(2)])
            pick(B("ZH", H, 64), B("ZF", H, 64), [[0, 64]])
            yield FILL["out"]
            yield from lists(H, t + 1)
            return
        act(B("SG", 0, 64), B("HH", 0, 64), F.Sign, cc(35))
        banks = LAST_BANKS if H else ("VV", "UB")
        n = 1024 // len(banks)
        for hi in range(16):
            mm(B(banks[64 * hi // n], hi % (n // 64), 64), B("SGW", hi), B("SG", 0, 64), True, True)
        for q in range(4):
            ts(B("CI", q, 4), S("MSI", 1024 * H + 256 * q + 252, 1024 * H + 256 * q + 256), 8, A.logical_shift_right)
        yield FILL["product"]
        ts(B("CF", 0, 16), B("CI", 0, 16), 8192.0, A.is_equal, -8193.0, A.mult)
        yield FILL["mates"]
        tt(B("CF", 1, 16), B("CI", 0, 16), B("CF", 0, 16), A.add)
        mm(S("LQ", 0, 128, 1, 0, 16), B("CF", 1, 16), B("IDf", 0), True, True)
        q = "s" if H else "y"
        yield FILL["cast"]
        act(S("YC", 128 * H, 128 * H + 128, 1, 0, 16), S("LQ", 0, 128, 1, 0, 16))
        dmas(q, "oc%d" % H, [(X(T.yc[4 * H:4 * H + 4, :]), S("YC", 128 * H, 128 * H + 128, 1, 0, 16))])
        dmas(q, "op%d" % H, [(X(T.yp[r, 8 - 8 * h:16 - 8 * h]), part("MFi", h, 8 * H, 8 * H + 8)) for h in range(2)])
        dmas(q, "oz%d" % H, [(X(T.yz[r, 64 * h:64 * h + 64]), part("ZI", h, 640 * H + 512, 640 * H + 576)) for h in range(2)])
        for u, name in enumerate(banks):
            x0 = 1024 * H
            tt(S("YF", x0 + n * u, x0 + n * u + n), S("FIN", x0 + n * u, x0 + n * u + n), S(name, 0, n), A.mult)
            dmas("y", "y%d%d" % (u, H), [(X(T.yf[r, c:c + b - a]), part("YF", h, x0 + a, x0 + b)) for h, a, b, c in pieces(H, n * u, n * u + n)])

    def window(H, t, chain):
        bank, win = "S%d" % H, "WIN%d" % H
        cost, kind, func = (win if t == 0 else "CW%d" % H), 1, F.Copy
        mm(S(bank, 0, 256), B("E0", 0), S("BI", 0, 256), True, False)
        done, summed, left, waiting = {"FD": 0, "CD": 0}, {"FD": 0, "CD": 0}, [2 * len(LISTS)], []

        def sums(data, k, i):
            name, col, cols = LISTS[i]
            pos, n = 16 * col, 16 * cols
            left[0] -= 1
            if name == "f1":
                for a in range(2):
                    mm(S(bank, 0, 256), S(data, pos + a, pos + n, 2), B("W1", 2 * k + a, 256), False, False)
                return
            for b in range(8):
                if name == "c4":
                    out, w = S(bank, b, 256, 8), B("W32", k, 32)
                else:
                    out, w = S(bank, 8 * int(name[1]) + b, 256, 32), S("W32", 32 * k, 32 * k + 32, 4)
                mm(out, S(data, pos + b, pos + n, 8), w, False, left[0] == 0 and b == 7)
            if name == "c4" and k == 0:
                mm(S("NM", 0, 144), B("OWN", H), S("OWW", 0, 144), True, False)
                mm(S("NM", 0, 68), B("E0", 0), S("C17", 0, 68), False, False)
                mm(S("NM", 0, 136), B("GG", H), S("NMW", 0, 136), False, True)

        def gather(data, n):
            end = min(done[data] + n, 5376)
            while done[data] < end:
                e = done[data]
                name, col, cols = [l for l in LISTS if 16 * l[1] <= e][-1]
                e1 = min(end, 16 * (col + cols) if data == "FD" else min(x for x in CUTS if x > e))
                while e1 > 16 * F1 and mine:
                    mine.pop(0)()
                o = S("LST", 336 * H + e // 16, 336 * H + e1 // 16)
                if data == "CD":
                    act(S("CD", e, e1), G(S(cost, 0, W), o), func)
                else:
                    step, z = 64 // cols, 1024 * H
                    tt(S("FD", e, e1), G(S(win, 0, W), o), S("ZR", z + step * (e - 16 * col), z + step * (e1 - 16 * col), step), A.is_lt)
                done[data] = e1
                while summed[data] < len(LISTS) and 16 * (LISTS[summed[data]][1] + LISTS[summed[data]][2]) <= e1:
                    waiting.append((data, 0 if data == "FD" else kind, summed[data]))
                    summed[data] += 1

        def flush():
            while waiting:
                sums(*waiting.pop(0))

        mine = rest[:]
        del rest[:]
        for nv, ns, free, steps in chain:
            if free:
                flush()
            for _ in range(min(steps, len(mine))):
                mine.pop(0)()
            gather("CD", ns)
            gather("FD", nv)
        while min(done.values()) < 5376:
            flush()
            for data in sorted(done, key=done.get):
                gather(data, min(16 * (col + cols) - done[data] for name, col, cols in LISTS if 16 * (col + cols) > done[data] or col == LISTS[-1][1]))
        flush()

    early = weights()
    for _ in lists(0, 0):
        next(early)
    chain = late_constants()
    for t in range(ROUNDS):
        for H in range(2):
            window(H, t, chain)
            chain = tail(H, t)
    for _ in chain:
        pass

    for s in sorted(final):
        g.wait_ge(T.sem[s], final[s])
